import numpy as np, ml_dtypes
CORES = [66,74,82,90,194,202,210,218]
N = 8
import mx_ref
BF = ml_dtypes.bfloat16
def gcols(t, e):
    v = np.concatenate([t.reshape(8, 16, -1, 4), np.zeros((8, 16, 1, 4), BF)], axis=2)
    return np.ascontiguousarray(np.stack([v[g][:, e[g]] for g in range(8)])).reshape(128, -1)
def tile(rs):
    return np.stack(rs, axis=2).reshape(128, -1).astype(BF)
def pick(q, e):
    c = np.concatenate([q[0].reshape(128, -1, 4), np.zeros((128, 1, 4), np.uint8)], axis=1); s = np.concatenate([q[1], np.ones((16, 1), np.uint8)], axis=1)
    return (np.ascontiguousarray(c[:, e].reshape(128, -1)), np.ascontiguousarray(s[:, e]))
def join(*qs):
    return (np.concatenate([q[0] for q in qs], axis=1), np.concatenate([q[1] for q in qs], axis=1))
def put(q, e, v):
    c, s = q[0].reshape(128, -1, 4).copy(), q[1].copy(); c[:, e] = v[0].reshape(128, -1, 4); s[:, e] = v[1]
    return (c.reshape(128, -1), s)
def pk(c, s):
    return (np.ascontiguousarray(c), mx_ref.live(s))
def emit(q):
    return q[0], q[1]
def packed(v, rng):
    q = [mx_ref.quantize(np.ascontiguousarray(v[r])) for r in range(N)]
    return np.stack([a for a, b in q]), np.stack([mx_ref.plane(b, rng) for a, b in q])
def values_of_codes():
    e, c = np.zeros((128, 128, 4), np.float32), np.zeros((128, 2, 4), np.uint8)
    e[np.arange(128), np.arange(128), 0] = 1
    c[:127, :, 0] = np.arange(256).reshape(2, 128).T[:127]
    return mx_ref.matmul(mx_ref.quantize(e.reshape(128, 512).astype(BF)), (c.reshape(128, 8), np.full((16, 2), 127, np.uint8))).T.reshape(-1).astype(np.float64)
CODE_VALUE, SCALE_VALUE = values_of_codes(), 2.0 ** (np.arange(256) - 127.0)
def decode(q):
    return (CODE_VALUE[q[0]].reshape(16, 8, -1, 4) * SCALE_VALUE[q[1]][:, None, :, None] + 0.0).reshape(128, -1).astype(np.float32)
def f(rng, *shape):
    return mx_ref.flush((rng.standard_normal(shape, dtype=np.float32) * np.exp2(rng.integers(-2, 3, shape[:-1] + (1,)))).astype(BF))
def wide(rng, *shape, cols=0):
    v = rng.standard_normal(shape, dtype=np.float32) * np.exp2(rng.integers(-12, 13, shape)).astype(np.float32)
    if cols: v *= np.repeat(np.exp2(rng.integers(-cols, cols + 1, shape[:-2] + (1, shape[-1] // 4))) * (rng.random(shape[:-2] + (1, shape[-1] // 4)) > 0.0625), 4, axis=-1).astype(np.float32)
    return mx_ref.flush(v.astype(BF))
C, K, E, R = 288, 48, 336, 3
def numbers_of(rng):
    return {"x": np.array(f(rng, N, 128, 4 * E)), "u": np.array(f(rng, N, 128, 512)), "v": np.array(f(rng, N, 128, 512))}
def layers(rng, still=[]):
    w = np.array(f(rng, N, 128, 2048)).reshape(N, 8, 16, 4, 8, 16, 4)
    for i in still:
        w[:, :, i] = 0
        w[:, :, :, :, :, i] = 0
    return w
def weights(rng, w):
    c, s = packed(np.ascontiguousarray(w).reshape(N, 128, 2048), rng)
    return {"wc": c, "ws": s}
def setup_inputs(rng):
    return {**numbers_of(rng), **weights(rng, layers(rng))}
def setup_inputs_ties(rng):
    d = numbers_of(rng)
    x = d["x"].reshape(N, 8, 16, E, 4)
    k = rng.integers(0, 4, (N, 8, E))
    k[:, :, C:] = rng.integers(-1, 5, (N, 8, K))
    x[:, :, 0] = 0
    x[:, :, 0, :, 0] = k.astype(np.float32).astype(BF)
    u = d["u"].reshape(N, 128, 128, 4)
    u[:, :, ::16] = 0
    o = rng.permutation(N)
    for r in range(N):
        for h in range(0, 128, 16): u[r, h, h, 0] = 0.0 if r == o[0] else -1.0 if r == o[1] else 1.0
    return {"x": x.reshape(N, 128, 4 * E), "u": u.reshape(N, 128, 512), "v": d["v"], **weights(rng, layers(rng, [0]))}
def close():
    t = np.zeros((128, 40, 4), np.float32)
    t[8, :, 0] = 1.96875
    t[9, :, 0] = (np.arange(8, 16) * np.exp2(-np.arange(14.0, 19.0))[:, None]).reshape(-1)
    once = decode(mx_ref.quantize(t.reshape(128, 160).astype(BF)))
    twice = decode(mx_ref.quantize(once.astype(BF)))[9, ::4]
    return max([np.unique(once[9, ::4][twice == k]) for k in twice], key=len)
def setup_inputs_edges(rng):
    d = numbers_of(rng)
    x = d["x"].astype(np.float32).reshape(N, 8, 16, E, 4)
    k = rng.integers(64, 192, (N, 8, E))
    k[:, :, :K // 2] = 200
    k[:, :, :C] = rng.permuted(k[:, :, :C], axis=2)
    for r in range(N):
        h = rng.permutation(8)
        for i in range(5): k[r, h[i], C:] = [255, 0, 199, 200, 128][i]
        k[r, h[5], C:] = rng.permutation(K) % 2 * 255
    b = np.arange(4)
    x[:, :, 0] = ((k[:, :, :, None] >> b) & 1) * np.exp2(b)
    x[:, :, 1] = ((k[:, :, :, None] >> (b + 4)) & 1) * np.exp2(b + 4)
    a = np.exp2(rng.integers(-14, -7, (N, 4, 8, E, 4))) * (1.0 + (2 * rng.integers(0, 64, (N, 4, 8, E, 4)) + 1) * 2.0 ** -7) * rng.choice([-1.0, 1.0], (N, 4, 8, E, 4))
    a[:, :, 0, :, 0] = 1.96875
    a[:, :, 1] = 0
    a[:, :, 1, :, 0] = rng.choice(close(), (N, 4, E))
    x[:, 4:, 8:] = a
    x[:, 0, 9] = 0
    u = d["u"].reshape(N, 128, 128, 4)
    u[:, :, ::16] = 0
    for h in range(0, 128, 16):
        u[:, h, h] = 1.0
        u[:, h + 1, h] = 1.0
    u[:, 9, 0, 0] = 2.0 ** 8
    w = layers(rng, [0, 1, 9])
    w[:, :, :, :, 4:, 8:] = 0
    return {"x": x.reshape(N, 128, 4 * E).astype(BF), "u": u.reshape(N, 128, 512), "v": d["v"], **weights(rng, w)}
def setup_inputs_near(rng):
    d = numbers_of(rng)
    x = d["x"].astype(np.float32).reshape(N, 8, 16, E, 4)
    x[:, :, 0] = 0
    x[:, :, 8:] = 0
    s = rng.integers(0, 256, (N, 8, E))
    b = np.arange(4)
    u = d["u"].reshape(N, 128, 128, 4)
    u[:, :, ::16] = 0
    o = rng.permutation(N) % 4
    for r in range(N):
        sign = rng.choice([-1.0, 1.0], (8, E))
        if o[r] < 2:
            x[r, :, 0, :, 0] = sign
            x[r, :, 11, :, 0] = 2.0 ** -10
            sign = np.ones((8, E))
        else:
            for g in rng.permutation(8)[:4]: x[r, g, 0, rng.integers(E), 0] = rng.choice([-1.0, 1.0]) * 2.0 ** 29
        least = -30.0 if o[r] == 2 else -23.0
        x[r, :, 8] = ((s[r, :, :, None] >> b) & 1) * np.exp2(b + least) * sign[:, :, None]
        x[r, :, 9] = ((s[r, :, :, None] >> (b + 4)) & 1) * np.exp2(b + 4 + least) * sign[:, :, None]
        k = 1.0 if o[r] == 0 else 2.0 ** -30
        for h in range(0, 128, 16):
            u[r, h, h, 0] = k
            u[r, h + 8, h] = k
            u[r, h + 9, h] = k
            u[r, h + 11, h, 0] = k
    return {"x": x.reshape(N, 128, 4 * E).astype(BF), "u": u.reshape(N, 128, 512), "v": d["v"], **weights(rng, layers(rng, [0, 8, 9, 10, 11, 12, 13, 14, 15]))}
def setup_inputs_huge(rng):
    d = numbers_of(rng)
    o = rng.permutation(N)
    c = rng.choice([-1.0, 1.0], (N, 8, 1, E, 1))
    u = d["u"].reshape(N, 128, 128, 4)
    u[:, :, ::16] = 0
    for r in range(N):
        a = (2.0 ** 30 * (1.0 - 0.1 * rng.random((128, 8, 4)))).astype(np.float32).astype(BF)
        if o[r] < N // 2:
            c[r] = c[r, :1].copy()
            u[r, :, ::16] = a
        else:
            c[r, rng.permutation(8)[:4]] = -1.0
            for g in range(8): u[r, 16 * g:16 * g + 16, 16 * g] = a[16 * g:16 * g + 16, g]
    x = c * (0.8 + 0.2 * rng.random((N, 8, 16, E, 4))) * 2.0 ** 30
    w = np.zeros((N, 128, 4, 128, 4), np.float32)
    i = np.arange(128)
    for b in range(4): w[:, i, b, i, b] = -2
    return {"x": x.astype(np.float32).reshape(N, 128, 4 * E).astype(BF), "u": u.reshape(N, 128, 512), "v": d["v"], **weights(rng, w.astype(BF))}
def setup_inputs_spread(rng):
    d = setup_inputs(rng)
    d["x"] = wide(rng, N, 128, 4 * E, cols=6)
    return d
def check_inputs(d):
    b = []
    for k in ("x", "u", "v"):
        a = np.abs(d[k].astype(np.float32))
        if not (np.isfinite(a).all() and ((a == 0) | (a >= 2.0 ** -30) & (a <= 2.0 ** 30)).all()): b.append("a value of " + k)
    none, least, most = [emit(mx_ref.quantize(np.full((128, 16), k, np.float32).astype(BF)))[1][0, 0] for k in (0.0, 2.0 ** -30, 2.0 ** 30)]
    for r in range(N):
        if ((d["wc"][r] == 0x7F) | (d["wc"][r] == 0xFF)).any(): b.append("wc: a code that is no number")
        s = mx_ref.live(d["ws"][r])
        if ((s != none) & ((s < least) | (s > most))).any(): b.append("ws: a scale out of range")
    return b
def reference(x, u, v, wc, ws):
    qu = [mx_ref.quantize(u[r]) for r in range(N)]
    lay = [pk(wc[r], ws[r]) for r in range(N)]
    now = [x[r] for r in range(N)]
    le = np.zeros((N, 8, E), np.float32)
    for t in range(R):
        made, sent = [], []
        for r in range(N):
            s = mx_ref.matmul(qu[r], mx_ref.quantize(now[r]))[::16] + np.float32(0.0)
            o = np.argsort(s[:, :C], axis=1, kind="stable")
            b = C + np.argsort(s[:, C:], axis=1, kind="stable")
            e = np.concatenate([o, b], axis=1)
            for g in range(8):
                k = np.searchsorted(s[g, o[g]], s[g, b[g]], side="right")
                p = np.maximum.accumulate(k - np.arange(K)) + np.arange(K)
                j = np.flatnonzero(p < C)
                e[g, p[j]] = b[g, j]
                e[g, C + j] = o[g, p[j]]
            le[r] = e
            z = gcols(now[r], e)
            q = mx_ref.quantize(z)
            m = tile([mx_ref.matmul(pick(lay[r], np.arange(128 * a, 128 * a + 128)), q) * np.float32(0.015625) + z[:, a::4].astype(np.float32) for a in range(4)]).reshape(8, 16, E, 4)
            made.append(m)
            sent.append(mx_ref.quantize(np.ascontiguousarray(m[7, :, C:].reshape(16, K // 8, 8, 4).transpose(2, 0, 1, 3)).reshape(128, -1)))
        now = []
        for r in range(N):
            came = decode(sent[(r - t - 1) % N]).astype(BF).reshape(8, 16, K // 8, 4).transpose(1, 2, 0, 3).reshape(1, 16, K, 4)
            wait = np.concatenate([came, made[r][:7, :, C:]])
            now.append(np.ascontiguousarray(np.concatenate([made[r][:, :, :C], wait], axis=2)).reshape(128, -1))
    y = np.zeros((N, 128, E), np.float32)
    oc, osc = np.zeros((N, 128, 4 * E), np.uint8), np.zeros((N, 16, E), np.uint8)
    for r in range(N):
        q = mx_ref.quantize(now[r])
        y[r] = mx_ref.matmul(mx_ref.quantize(v[r]), q)
        oc[r], osc[r] = emit(q)
    return {"y": y, "le": le, "oc": oc, "osc": osc}

@@ -1,0 +1,534 @@
+from concourse.mybir import dt, AluOpType, ActivationFunctionType
+
+ALU, ACT = AluOpType, ActivationFunctionType
+C, K, E, R = 288, 48, 336, 3
+H = C // 2
+BIG = 2.0e29
+CODE = "float8_e4m3fn_x4"
+NV = 12
+RW = 8 * NV
+WG = "ssssssssvvss"
+ZG = "vvssvvssvsss"
+DN = "ssssssvv"
+GE = "ssv"
+ORDER = [
+    7,0,25,27,30,6,14,13,10,37,11,12,9,38,16,150,33,45,32,8,57,56,52,55,49,50,68,69,54,15,19,18,17,59,28,34,39,43,40,22,41,
+    36,53,44,31,1,2,3,4,175,176,42,35,58,26,87,29,89,92,93,88,90,133,108,98,94,100,104,95,91,127,125,128,129,123,131,151,
+    152,99,102,115,112,134,153,96,120,121,97,117,154,109,114,110,161,135,116,155,118,51,106,122,119,156,136,124,145,126,
+    137,139,140,141,101,162,103,107,157,105,130,132,138,113,111,166,146,172,142,143,144,61,147,163,167,158,168,159,164,169,
+    21,165,160,173,174,148,179,71,149,20,178,170,70,72,180,171,181,62,182,63,183,64,23,184,47,24,177,60,185,187,186,188,48,
+    189,311,65,190,66,216,192,193,194,191,195,199,203,197,217,219,196,200,198,201,202,204,218,235,238,239,46,236,207,205,
+    206,208,209,5,74,75,76,77,78,73,220,221,211,212,245,213,222,237,241,242,214,215,225,243,244,223,240,232,233,226,227,
+    247,228,229,246,248,224,230,249,251,86,67,231,234,255,256,250,253,295,254,278,281,282,269,259,271,283,265,257,260,294,
+    279,267,273,276,272,252,288,284,286,287,292,290,275,266,312,313,263,274,296,261,314,315,316,317,318,319,320,321,322,
+    285,291,298,262,297,300,301,293,323,325,324,210,352,289,351,326,354,270,302,327,328,280,258,277,329,303,306,330,334,
+    343,299,268,337,264,342,338,307,331,304,305,333,308,332,309,348,349,310,350,335,344,339,345,340,336,341,346,355,356,
+    347,357,358,359,360,361,363,362,353,364,367,368,370,369,365,366,392,394,371,379,373,393,372,374,380,377,375,376,378,
+    395,411,415,412,416,414,79,80,81,82,384,382,381,383,83,386,385,487,396,397,419,420,387,423,388,424,389,401,399,413,417,
+    418,390,391,404,405,398,400,402,408,409,403,421,406,407,422,425,427,410,426,431,432,429,428,464,460,462,468,461,463,
+    469,471,455,458,430,457,433,443,447,451,449,470,441,454,448,437,452,435,450,456,472,488,489,490,491,492,493,494,465,
+    466,467,474,434,439,445,438,473,495,496,497,498,501,500,499,502,527,530,529,528,459,503,504,475,505,476,482,506,519,
+    510,440,436,442,513,453,446,444,515,520,516,511,477,478,479,480,481,483,509,508,518,484,514,507,485,524,486,525,526,
+    517,521,512,522,531,532,523,533,534,535,536,537,539,540,544,543,538,546,545,603,548,602,604,84,547,541,553,554,555,556,
+    549,550,551,552,542,569,571,570,559,560,558,562,85,557,561,563,564,565,566,568,572,587,575,591,573,574,576,582,578,592,
+    590,589,577,580,584,588,597,579,583,585,581,595,599,598,600,593,596,586,605,606,594,601,615,610,616,609,607,608,613,
+    567,617,619,618,620,611,614,612,621,622,623,624,625,626,627,629,631,628,630,632,633,639,638,635,636,634,637,640]
+
+
+def _sb(n, d):
+    return ("sbuf", [128, n], d)
+
+
+SCRATCH = {
+    "X": _sb(4 * E, "bfloat16"), "P64": _sb(4 * E, "bfloat16"), "Z": _sb(4 * C, "bfloat16"), "Z64": _sb(4 * C, "bfloat16"),
+    "ZW": _sb(512, "bfloat16"), "ZW64": _sb(4 * K, "bfloat16"), "qzw": _sb(128, CODE), "szw": _sb(128, "uint8"),
+    "U": _sb(512, "bfloat16"), "V": _sb(512, "bfloat16"),
+    "qu": _sb(128, CODE), "su": _sb(128, "uint8"), "qk": _sb(128, CODE), "sk": _sb(128, "uint8"),
+    "qv": _sb(128, CODE), "sv": _sb(128, "uint8"), "qw": _sb(512, CODE), "sw": _sb(512, "uint8"),
+    "qx": _sb(C, CODE), "sx": _sb(C, "uint8"), "qa": _sb(128, CODE), "sa": _sb(128, "uint8"),
+    "qz": _sb(C, CODE), "sz": _sb(C, "uint8"),
+    "ONE": _sb(512, "bfloat16"), "ZT": _sb(512, "bfloat16"), "OD1": _sb(512, "bfloat16"), "OD": _sb(512, "bfloat16"),
+    "qo": _sb(128, CODE), "so": _sb(128, "uint8"), "q0": _sb(128, CODE), "s0": _sb(128, "uint8"),
+    "EM": _sb(4 * 528, "bfloat16"), "qe": _sb(528, CODE), "se": _sb(528, "uint8"),
+    "PI": _sb(2, "int32"), "PB": _sb(5, "int32"), "PF": _sb(5, "float32"), "PC": _sb(10, "float32"),
+    "RI": _sb(C, "float32"), "AM": _sb(C, "float32"), "RR": _sb(C, "float32"), "AC": _sb(C, "float32"),
+    "KEEP": _sb(C, "bfloat16"), "IV": _sb(E, "bfloat16"), "CI": _sb(18, "float32"), "CM": _sb(18, "float32"),
+    "UI": _sb(8, "int32"), "ou": _sb(8, "uint16"),
+    "LI": _sb(6, "float32"), "LA": _sb(18, "int32"), "LB": _sb(18, "float32"), "ol": _sb(6, "uint16"),
+    "BI": _sb(4, "float32"), "ob": _sb(4, "uint16"), "KI": _sb(4, "float32"), "ok": _sb(4, "uint16"),
+    "KX": _sb(C, "float32"), "SH": _sb(C, "float32"), "KXW": _sb(K, "float32"), "SHW": _sb(K, "float32"),
+    "TT": _sb(4 * 832, "bfloat16"), "qt": _sb(1024, CODE), "st": _sb(1024, "uint8"),
+    "TW": _sb(512, "bfloat16"), "qtw": _sb(128, CODE), "stw": _sb(128, "uint8"),
+    "SG": _sb(2448, "bfloat16"), "SGW": _sb(3 * C, "bfloat16"), "SGX": _sb(3 * C, "bfloat16"),
+    "CN": _sb(4, "float32"), "BC": _sb(96, "float32"), "BD": _sb(96, "float32"),
+    "RS": _sb(18 * RW, "float32"), "DS": _sb(C, "bfloat16"), "U0": _sb(18, "float32"), "U1": _sb(18, "float32"),
+    "CV": _sb(C, "float32"), "RK": _sb(18, "float32"), "ork": _sb(18, "uint16"),
+    "CW": _sb(K, "float32"), "orb": _sb(4, "uint16"), "KU": _sb(K, "float32"), "KS": _sb(K, "float32"),
+    "PP": _sb(K, "float32"), "CP": _sb(K, "float32"), "op": _sb(4, "uint16"),
+    "B0": _sb(K, "bfloat16"), "W": _sb(C + K, "bfloat16"), "WB": _sb(K, "bfloat16"),
+    "CE": _sb(C, "float32"), "oe": _sb(18, "uint16"), "CB": _sb(K, "float32"), "ow": _sb(4, "uint16"),
+    "MW64": _sb(4 * K, "bfloat16"), "MW": _sb(512, "bfloat16"),
+    "G": _sb(64, "bfloat16"), "TB": _sb(64, "bfloat16"), "BT": _sb(512, "bfloat16"),
+    "LE": _sb(E, "float32"), "Y": _sb(E, "float32"),
+}
+for _t in range(R):
+    SCRATCH["qb%d" % _t] = _sb(128, CODE)
+    SCRATCH["sb%d" % _t] = _sb(128, "uint8")
+    SCRATCH["ql%d" % _t] = _sb(32, CODE)
+    SCRATCH["sl%d" % _t] = _sb(32, "uint8")
+    SCRATCH["qm%d" % _t] = _sb(192, CODE)
+    SCRATCH["sm%d" % _t] = _sb(192, "uint8")
+for _b in range(8):
+    SCRATCH["ps%d" % _b] = ("psum", [128, 512], "float32")
+
+DMA_SEMS = ["ldu", "ldx", "ldz", "ldw", "lds", "ldv", "sh0", "sh1", "sh2", "oa", "oz"] + ["z%d" % _i for _i in range(4 * R)]
+SEMAPHORES = ["cv", "cs", "ct", "cg", "sent", "arr0", "arr1", "arr2"] + DMA_SEMS
+COUNTER = {"v": "cv", "s": "cs", "t": "ct", "g": "cg"}
+
+
+def _clash(a, b):
+    if a[0].startswith("ps"):
+        if a[6] is not None and a[6] == b[6]:
+            return False
+        return a[5] != b[5] or a[4] or b[4]
+    if not (a[4] or b[4]) or a[2] <= b[1] or b[2] <= a[1]:
+        return False
+    return not a[3].isdisjoint(b[3])
+
+
+def _needs(ops):
+    seen, needs = {}, []
+    for i, o in enumerate(ops):
+        needs.append(set(j for a in o["acc"] for (j, b) in seen.get(a[0], []) if _clash(a, b)))
+        for a in o["acc"]:
+            seen.setdefault(a[0], []).append((i, a))
+    return needs
+
+
+def _links(ops):
+    needs, soft, prev = _needs(ops), [None] * len(ops), {}
+    for i, o in enumerate(ops):
+        if o["chain"] is not None:
+            soft[i] = prev.get(o["chain"])
+            prev[o["chain"]] = i
+    return needs, soft
+
+
+def _keeps(order, links):
+    needs, soft = links
+    place = {i: n for n, i in enumerate(order)}
+    return sorted(order) == list(range(len(needs))) and all(
+        place[j] < place[i] for i in order for j in list(needs[i]) + ([] if soft[i] is None else [soft[i]]))
+
+
+def _emit(g, T, ops):
+    eng = {"v": g.vector, "s": g.scalar, "t": g.tensor, "g": g, "y": g.sync}
+    known, clock, waits, batch = {q: {} for q in list(eng) + ["x"]}, [], [], {}
+    for i, o in enumerate(ops):
+        if o["sem"]:
+            batch.setdefault(o["sem"], []).append(i)
+    for i, (o, nd) in enumerate(zip(ops, _needs(ops))):
+        need = {}
+        for j in nd:
+            key = ops[j]["sem"] or ops[j]["q"]
+            assert not ops[j]["sem"] or len(batch[key]) == 1
+            need[key] = max(need.get(key, -1), j)
+        kn, w = known[o["q"]], []
+        for key, j in sorted(need.items(), key=lambda kv: -kv[1]):
+            if kn.get(key, -1) >= j:
+                continue
+            w.append(j)
+            kn[key] = j
+            for k2, j2 in clock[j].items():
+                kn[k2] = max(kn.get(k2, -1), j2)
+        waits.append(w)
+        clock.append(dict(kn))
+    marked = set(j for w in waits for j in w)
+    count, value = {}, {}
+    for i, o in enumerate(ops):
+        if o["sem"]:
+            value[i] = o["full"] or 16 * len(batch[o["sem"]])
+        elif i in marked:
+            count[o["q"]] = count.get(o["q"], 0) + 1
+            value[i] = count[o["q"]]
+    for i, o in enumerate(ops):
+        for j in waits[i]:
+            eng[o["q"]].wait_ge(T.sem[ops[j]["sem"] or COUNTER[ops[j]["q"]]], value[j])
+        if o["fn"] is None:
+            continue
+        ins = o["fn"]()
+        if o["sem"]:
+            ins.then_inc(T.sem[o["sem"]], 16)
+        elif i in marked:
+            ins.then_inc(T.sem[COUNTER[o["q"]]], 1)
+    for key, members in batch.items():
+        if members[-1] not in marked:
+            eng[ops[members[-1]]["q"]].wait_ge(T.sem[key], value[members[-1]])
+
+
+def rank_program(g, core, T, topo):
+    rank = T.rank_of(core)
+    if rank is None:
+        return
+    ops = _calls(g, core, T, topo, rank)
+    assert _keeps(ORDER, _links(ops))
+    _emit(g, T, [ops[i] for i in ORDER])
+    g.wait_ge(T.sem.sent, 16 * R)
+
+
+def _calls(g, core, T, topo, rank):
+    N = len(T.cores)
+    ops = []
+
+    def A(name, c0=0, c1=None, step=1, p0=0, p1=128):
+        if c1 is None:
+            c1 = SCRATCH[name][1][1]
+        ap = T[name][p0:p1, c0:c1] if step == 1 else T[name][p0:p1, c0:c1:step]
+        return (ap, name, p0, p1, frozenset(range(c0, c1, step)))
+
+    def rec(q, fn, outs, ins, size, sem=None, full=0, grp=None, chain=None):
+        acc = [(a[1], a[2], a[3], a[4], True, q, grp) for a in outs]
+        acc += [(a[1], a[2], a[3], a[4], False, q, None) for a in ins if isinstance(a, tuple)]
+        ops.append({"q": q, "fn": fn, "acc": acc, "sem": sem, "full": full, "size": size, "chain": chain or grp})
+
+    def val(a):
+        return a[0] if isinstance(a, tuple) else a
+
+    def span(out, a, rate=None, off=None, q="v"):
+        if off is not None:
+            return ("gat", 16 * len(off[4]))
+        if rate is None:
+            rate = 0.5 if all(SCRATCH[z[1]][2] == "bfloat16" for z in (out, a)) else 1.0
+        return (q, len(a[4]) * rate)
+
+    def ts(out, a, s1, op0, s2=None, op1=None, off=None):
+        src = a[0] if off is None else a[0].indirect(off[0])
+        if op1 is None:
+            rec("v", lambda: g.vector.tensor_scalar(out[0], src, val(s1), None, op0), [out], [a, s1, off], span(out, a, None, off))
+        else:
+            rec("v", lambda: g.vector.tensor_scalar(out[0], src, val(s1), val(s2), op0, op1), [out], [a, s1, s2, off], span(out, a, None, off))
+
+    def tt(out, a, b, op, off=None):
+        src = a[0] if off is None else a[0].indirect(off[0])
+        rec("v", lambda: g.vector.tensor_tensor(out[0], src, b[0], op), [out], [a, b, off],
+            span(out, a, 1.0 if a[1].startswith("ps") else 2.0, off))
+
+    def cp(out, a):
+        rec("v", lambda: g.vector.tensor_copy(out[0], a[0]), [out], [a], span(out, a))
+
+    def scatter(win, off, a):
+        rec("v", lambda: g.vector.tensor_copy(win[0].indirect(off[0]), a[0]), [win], [a, off], ("sca", len(a[4])))
+
+    def scan(out, d0, d1, init, op0, op1):
+        rec("v", lambda: g.vector.tensor_tensor_scan(out[0], d0[0], d1[0], init, op0, op1), [out], [d0, d1], span(out, d1))
+
+    def turn(out, a):
+        rec("v", lambda: g.vector.transpose(out[0], a[0]), [out], [a], span(out, a))
+
+    def fill(out, c):
+        rec("v", lambda: g.vector.memset(out[0], c), [out], [], span(out, out))
+
+    def quant(qn, sn, c0, a):
+        n = len(a[4]) // 4
+        q, s = A(qn, c0, c0 + n), A(sn, c0, c0 + n)
+        rec("v", lambda: g.vector.quantize_mx(q[0], s[0], a[0]), [q, s], [a], ("q", n))
+
+    def pick(qo, so, n, qi, si, nw, off):
+        a, b, c, d = A(qo, 0, n), A(so, 0, n), A(qi, 0, nw), A(si, 0, nw)
+        rec("v", lambda: g.vector.tensor_copy(a[0].bitcast(dt.uint32), c[0].bitcast(dt.uint32).indirect(off[0])), [a], [c, off],
+            span(a, c, None, off))
+        rec("s", lambda: g.scalar.activation(b[0], d[0].indirect(off[0]), ACT.Copy), [b], [d, off], span(b, d, None, off))
+
+    def act(out, a, func, bias=None, scale=None, acc=None, off=None):
+        src = a[0] if off is None else a[0].indirect(off[0])
+        kw = {}
+        if bias is not None:
+            kw["bias"] = val(bias)
+        if scale is not None:
+            kw["scale"] = val(scale)
+        if acc is not None:
+            kw["accum_out"] = acc[0]
+        rec("s", lambda: g.scalar.activation(out[0], src, func, **kw), [out] + ([acc] if acc else []), [a, bias, scale, off],
+            span(out, a, 1.0, off, "s"))
+
+    def times(on, out, a, c, off=None):
+        if on == "s":
+            act(out, a, ACT.Copy, None, c, off=off)
+        else:
+            ts(out, a, c, ALU.mult, off=off)
+
+    def zero(out):
+        act(out, A("ZT", 0, len(out[4])), ACT.Copy)
+
+    def mm(bank, n, ql, sl, l0, qr, sr, r0, start=True, stop=True, grp=None):
+        o = A("ps%d" % bank, 0, n)
+        a, b, c, d = A(ql, l0, l0 + 128), A(sl, l0, l0 + 128), A(qr, r0, r0 + n), A(sr, r0, r0 + n)
+        rec("t", lambda: g.tensor.matmul_mx(o[0], a[0], b[0], c[0], d[0], start, stop), [o], [a, b, c, d], ("pe", n), grp=grp)
+
+    def dma(q, sem, out, a, raw=False, chain=None):
+        e = {"y": g.sync, "s": g.scalar}[q]
+        o, i = val(out), val(a)
+        if raw:
+            o = o.bitcast(dt.uint8) if isinstance(out, tuple) else o
+            i = i.bitcast(dt.uint8) if isinstance(a, tuple) else i
+        rec(q, lambda: e.dma_start(o, i), [out] if isinstance(out, tuple) else [], [a], ("dma", 0), sem=sem, chain=chain)
+
+    def iota(out, pat, base, cm, small=True):
+        if small:
+            rec("g", lambda: g.iota(out[0], pat, base, cm, allow_small_or_imprecise_dtypes=True), [out], [], ("g", len(out[4])))
+        else:
+            rec("g", lambda: g.iota(out[0], pat, base, cm), [out], [], ("g", len(out[4])))
+
+    def sel(out, a, pat, op, base, cm):
+        rec("g", lambda: g.affine_select(out[0], a[0], pat, op, 0.0, base, cm), [out], [a], ("g", len(out[4])))
+
+    def col(name, j):
+        return A(name, j, j + 1)
+
+    def ends(name, n):
+        return A(name, 15, n, 16)
+
+    def ps(bank, c0, c1, p0=0, p1=128):
+        return A("ps%d" % bank, c0, c1, 1, p0, p1)
+
+    dma("y", "ldu", A("U"), T.u[:], chain="loads")
+    dma("y", "ldx", A("X", 0, 4 * H), T.x[:, 0:4 * H], chain="loads")
+    dma("y", "ldz", A("X", 4 * H, 4 * E), T.x[:, 4 * H:4 * E], chain="loads")
+    dma("y", "ldw", A("qw"), T.wc[:], raw=True, chain="loads")
+    dma("y", "lds", A("sw"), T.ws[:], chain="loads")
+    dma("y", "ldv", A("V"), T.v[:], chain="loads")
+    iota(A("PI", 0, 1), [[0, 1]], 0, 1, False)
+    iota(A("UI"), [[16, 8]], 0, 0, False)
+    iota(A("RI"), [[0, 18], [16384, 16]], 0, 0)
+    fill(A("ONE"), 1.0)
+    for j, (c, op) in enumerate(((15, ALU.bitwise_and), (12, ALU.bitwise_and), (3, ALU.bitwise_and),
+                                 (5, ALU.arith_shift_right), (31, ALU.bitwise_and))):
+        ts(col("PB", j), A("PI", 0, 1), c, op)
+    cp(A("ou"), A("UI"))
+    cp(A("PF"), A("PB"))
+    q = col("PF", 0)
+    act(col("PC", 0), q, ACT.Identity, 0.0, 16384.0)
+    act(col("PC", 1), q, ACT.Identity, 15000.0, 16384.0)
+    act(col("PC", 2), q, ACT.Identity, -7681.0, 512.0)
+    act(col("PC", 3), q, ACT.Identity, -7680.0, 512.0)
+    act(col("PC", 4), q, ACT.Identity, -7680.0 + 168.0, 512.0)
+    act(col("PC", 5), q, ACT.Identity, 0.0, 511.0)
+    act(col("PC", 6), col("PF", 1), ACT.Identity, col("PF", 2), 8.0)
+    act(col("PC", 7), col("PF", 3), ACT.Identity, col("PC", 6), 8.0)
+    fill(A("RR"), -BIG)
+    fill(A("RR", 0, C, 16), BIG)
+    fill(A("ZT"), 0.0)
+    ts(A("AM"), A("RI"), col("PC", 0), ALU.not_equal, BIG, ALU.mult)
+    ts(A("AC"), A("RI"), col("PC", 1), ALU.subtract, 512.0, ALU.min)
+    for c0, c1 in ((240, 288), (464, 512), (624, 672), (720, 832)):
+        zero(A("TT", 4 * c0, 4 * c1))
+    quant("qu", "su", 0, A("U"))
+    pick("qk", "sk", 128, "qu", "su", 128, A("ou"))
+    quant("qt", "st", 512, A("ZT"))
+    quant("qt", "st", 896, A("ZT"))
+    quant("q0", "s0", 0, A("ZT"))
+    act(A("KEEP"), A("ONE", 0, C), ACT.Copy)
+    zero(A("KEEP", 0, C, 16))
+    zero(col("RS", RW - 1))
+    zero(A("TW", 4 * K, 512))
+    zero(A("ZW", 4 * K, 512))
+    zero(A("MW", 192, 256))
+    zero(A("MW", 448, 512))
+    zero(A("EM", 2048, 2112))
+    zero(A("BT", 32, 512))
+    sel(A("OD1"), A("ONE"), [[-16, 8], [0, 64]], ALU.is_ge, 0, 1)
+    sel(A("OD"), A("OD1"), [[16, 8], [0, 64]], ALU.is_ge, 15, -1)
+    quant("qo", "so", 0, A("OD"))
+    iota(A("CI"), [[16, 18]], 15 - 7680, 0)
+    act(A("CM"), A("CI"), ACT.Identity, col("PC", 5))
+    iota(A("IV"), [[1, E]], -168, 0)
+    iota(A("LI"), [[-1, 2], [16, 3]], 2, 0)
+    iota(A("BI"), [[4, 2], [128, 2]], 0, 0)
+    iota(A("KI", 0, 3), [[32, 3]], 0, 0)
+    ts(A("LA", 0, 6), A("LI"), q, ALU.add)
+    ts(col("PC", 8), col("PF", 3), 3.0, ALU.is_lt, 256.0, ALU.mult)
+    ts(A("ob"), A("BI"), col("PC", 7), ALU.add, col("PC", 8), ALU.add)
+    ts(A("ok", 0, 3), A("KI", 0, 3), col("PF", 4), ALU.add)
+    ts(A("LA", 6, 12), A("LA", 0, 6), 7, ALU.bitwise_and)
+    ts(A("LA", 12, 18), A("LA", 0, 6), 3, ALU.arith_shift_right)
+    ts(A("LB", 0, 6), A("LA", 6, 12), 0.0, ALU.is_equal)
+    ts(A("LB", 6, 12), A("LA", 12, 18), -17.0, ALU.add)
+    tt(A("LB", 12, 18), A("LB", 0, 6), A("LB", 6, 12), ALU.mult)
+    ts(A("ol"), A("LB", 12, 18), 16.0, ALU.add)
+    for a in range(4):
+        sel(A("EM", 512 * a, 512 * a + 512), A("ONE"), [[-128, 4], [-1, 32], [128, 4]], ALU.is_equal, -32 * a, 1)
+    quant("qe", "se", 0, A("EM", 0, 1056))
+    quant("qe", "se", 264, A("EM", 1056, 2112))
+    for t in range(R):
+        for j, (n_, c0, c1) in enumerate((("l", 16, 18), ("m", 96, 192))):
+            dma("y", "z%d" % (4 * t + 2 * j), A("q%s%d" % (n_, t), c0, c1), A("q0", 0, c1 - c0), raw=True, chain="loads")
+            dma("y", "z%d" % (4 * t + 2 * j + 1), A("s%s%d" % (n_, t), c0, c1), A("s0", 0, c1 - c0), chain="loads")
+    quant("qv", "sv", 0, A("V"))
+
+    base = {}
+    for m in range(1, 18):
+        c0, t_ = ((0, 18 - m) if m >= 15 else (288, 14 - m) if m >= 11 else (512, 10 - m) if m >= 7
+                  else (672, 6 - m) if m >= 3 else (800, 2 - m))
+        base[m] = 4 * c0 + t_
+
+    def slot(m, c0=0, c1=None):
+        c1 = 16 * m if c1 is None else c1
+        return A("TT", base[m] + 4 * c0, base[m] + 4 * c1 - 3, 4)
+
+    def key(m):
+        return col("SH", 16 * m + 15)
+
+    def wslot(t_, c0=0, c1=K):
+        return A("TW", 4 * c0 + t_, 4 * c1 + t_ - 3, 4)
+
+    def unpack(t):
+        rec("x", None, [A("ql%d" % t, 0, 6), A("sl%d" % t, 0, 6)], [], ("none", 0), sem="arr%d" % t, full=16, chain="far%d" % t)
+        pick("qm%d" % t, "sm%d" % t, 96, "ql%d" % t, "sl%d" % t, 32, A("ol"))
+        for h in range(8):
+            mm(7, 128, "qe", "se", 128 * (h // 2) + 16 * (h % 2), "qm%d" % t, "sm%d" % t,
+               (55 if h % 2 else 6) - h, h == 0, h == 7, grp="u%d" % t)
+        for b in range(4):
+            cp(A("X", 4 * C + b, 4 * E, 4, 0, 16), ps(7, 0, K, 32 * b, 32 * b + 16))
+
+    def keys(c0, c1):
+        out = []
+        if c0 < H:
+            out.append((c0, min(c1, H), ps(4, c0, min(c1, H))))
+        if c1 > H:
+            out.append((max(c0, H), c1, ps(2, max(c0, H) - H, c1 - H)))
+        return out
+
+    quant("qx", "sx", 0, A("X", 0, 4 * H))
+    quant("qx", "sx", H, A("X", 4 * H, 4 * C))
+    for t in range(R):
+        first = t == 0
+        mm(4, H, "qk", "sk", 0, "qx", "sx", 0)
+        mm(2, H, "qk", "sk", 0, "qx", "sx", H)
+        mm(5, C, "qk", "sk", 0, "qx", "sx", 0)
+        for c0, c1, k_ in keys(0, C):
+            tt(A("KX", c0, c1), k_, A("AM", c0, c1), ALU.add)
+            scan(A("SH", c0, c1), A("RR", c0, c1), A("KX", c0, c1), BIG, ALU.max, ALU.min)
+        for m in range(1, 18):
+            if m <= NV:
+                for c0, c1, k_ in keys(0, 16 * m):
+                    ts(slot(m, c0, c1), k_, key(m), ALU.is_gt)
+                scan(A("RS", RW * m + RW - 8 * m, RW * m + RW), slot(m, 0, 8 * m), slot(m, 8 * m, 16 * m), 0.0, ALU.add, ALU.add)
+            else:
+                sg = A("SG", 8 * m * (m - 1), 8 * m * (m + 1))
+                act(sg, ps(5, 0, 16 * m), ACT.Sign, key(m), -1.0)
+                act(slot(m), sg, ACT.Relu, None, -1.0, col("RS", RW * m + RW - 1))
+        for c0, c1, k_ in keys(0, C):
+            tt(A("TT", 4 * c0, 4 * c1, 4), k_, A("SH", c0, c1), ALU.is_ge)
+        scan(A("DS"), A("KEEP"), A("TT", 0, 4 * C, 4), 0.0, ALU.mult, ALU.add)
+        quant("qt", "st", 576, A("TT", 4 * 512, 4 * 832))
+        quant("qt", "st", 288, A("TT", 4 * 288, 4 * 512))
+        quant("qt", "st", 0, A("TT", 0, 4 * 288))
+        for i, (c0, n) in enumerate(((288, 288), (576, 160), (736, 128), (864, 128), (0, 288))):
+            mm(6, n, "qo", "so", 0, "qt", "st", c0, i == 0, i == 4, grp="c%d" % t)
+        scan(A("CV"), A("AC"), ps(6, 0, C), 0.0, ALU.add, ALU.max)
+        tt(A("U0"), ends("DS", C), A("CM"), ALU.subtract)
+        tt(A("U1"), A("U0"), A("RS", RW - 1, 18 * RW, RW), ALU.add)
+        tt(A("RK"), ends("CV", C), A("U1"), ALU.subtract)
+        cp(A("ork"), A("RK"))
+        scatter(A("W", 0, C), A("ork"), A("IV", 0, C))
+        fill(A("W", C, C + K), 1024.0)
+        if not first:
+            unpack(t - 1)
+        quant("qa", "sa", 0, A("X", 4 * (E - 128), 4 * E))
+        mm(0, 128, "qk", "sk", 0, "qa", "sa", 0)
+        tt(A("KXW"), ps(0, 80, 128), A("AM", 0, K), ALU.add)
+        scan(A("SHW"), A("RR", 0, K), A("KXW"), BIG, ALU.max, ALU.min)
+        tt(wslot(3), ps(0, 80, 128), A("SHW"), ALU.is_equal)
+        for m in range(3):
+            e_ = 16 * m + 16
+            kw_ = col("SHW", e_ - 1)
+            ts(wslot(m, 0, e_), ps(0, 80, 80 + e_), kw_, ALU.is_gt)
+            if e_ < K:
+                ts(wslot(m, e_, K), ps(0, 80 + e_, 128), kw_, ALU.is_ge)
+            act(A("SGW", C * m, C * m + C), ps(5, 0, C), ACT.Sign, kw_, -1.0)
+            act(A("SGX", C * m, C * m + C), A("SGW", C * m, C * m + C), ACT.Relu, None, -1.0, col("CN", m))
+            act(A("BC", 32 * m, 32 * m + 32), A("ZT", 0, 32), ACT.Identity, col("CN", m))
+        turn(A("BD"), A("BC"))
+        act(A("KU"), A("BD"), ACT.Identity, float(C), -1.0, off=A("ok", 0, 3))
+        quant("qtw", "stw", 0, A("TW"))
+        mm(3, 128, "qo", "so", 0, "qtw", "stw", 0)
+        scan(A("CW"), A("AC", 0, K), ps(3, 0, K), 0.0, ALU.add, ALU.max)
+        for b in range(4):
+            c0 = 0 if first else C
+            act(A("P64", E * b + c0, E * b + E), A("X", 4 * c0 + b, 4 * E, 4), ACT.Copy, None, 64.0)
+        ts(A("orb", 0, 3), ends("CW", K), col("PC", 2), ALU.add)
+        scatter(A("B0"), A("orb", 0, 3), A("IV", C, E))
+        scatter(A("KS"), A("orb", 0, 3), A("KU"))
+        scan(A("PP"), A("ONE", 0, K), A("KS"), -1.0, ALU.add, ALU.max)
+        scan(A("CP"), A("AC", 0, K), A("PP"), 0.0, ALU.add, ALU.max)
+        ts(A("op", 0, 3), ends("CP", K), col("PC", 3), ALU.add)
+        tt(A("WB"), A("W"), A("B0"), ALU.min, off=A("op", 0, 3))
+        scatter(A("W"), A("op", 0, 3), A("B0"))
+        scan(A("CB"), A("AC", 0, K), A("WB"), 0.0, ALU.add, ALU.max)
+        ts(A("ow", 0, 3), ends("CB", K), col("PC", 4), ALU.add)
+        scan(A("CE"), A("AC"), A("W", 0, C), 0.0, ALU.add, ALU.max)
+        ts(A("oe"), ends("CE", C), col("PC", 4), ALU.add)
+        for b in range(4):
+            times(WG[4 * t + b], A("ZW", b, 4 * K, 4), A("P64", E * b, E * b + E), 0.015625, A("ow", 0, 3))
+        quant("qzw", "szw", 0, A("ZW"))
+        times("s", A("ZW64"), A("ZW", 0, 4 * K), 64.0)
+        for b in range(4):
+            mm(b, 128, "qw", "sw", 128 * b, "qzw", "szw", 0)
+            tt(A("MW64", b, 4 * K, 4), ps(b, 0, K), A("ZW64", b, 4 * K, 4), ALU.add)
+        for a in range(3):
+            times("v", A("MW", 256, 256 + 4 * K, 1, 32 * a, 32 * a + 32), A("MW64", 0, 4 * K, 1, 96, 128), 0.015625)
+        times("v", A("MW", 0, 4 * K), A("MW64"), 0.015625)
+        times(GE[t], A("G"), A("MW"), 1.0, A("ob"))
+        dma("y", "sh%d" % t, A("X", 4 * C, 4 * E, 1, 16, 128), A("MW", 0, 4 * K, 1, 0, 112))
+        turn(A("TB"), A("G"))
+        cp(A("TB", 32, 48), A("TB", 16, 32))
+        turn(A("BT", 0, 32), A("TB", 32, 64))
+        quant("qb%d" % t, "sb%d" % t, 0, A("BT"))
+        if t == R - 1:
+            ops[-1]["chain"] = "b last"
+        dst = T.cores[(rank + t + 1) % N]
+        rid, pid = topo.addr(dst, core)
+        mask = topo.mask(core, dst)
+        assert len(topo.engines(core, dst)) == 8
+
+        def ship(t=t, rid=rid, pid=pid, mask=mask):
+            g.remote_dma(T["ql%d" % t][:, 0:6].bitcast(dt.uint8), T["qb%d" % t][:, 0:6].bitcast(dt.uint8),
+                         T.sem["arr%d" % t], T.sem.sent, pid, rid, mask)
+            return g.remote_dma(T["sl%d" % t][:, 0:6], T["sb%d" % t][:, 0:6], T.sem["arr%d" % t], T.sem.sent, pid, rid, mask)
+
+        rec("g", ship, [], [A("qb%d" % t, 0, 6), A("sb%d" % t, 0, 6)], ("far", 0), chain="far%d" % t)
+        for b in range(4):
+            times(ZG[4 * t + b], A("Z", b, 4 * C, 4), A("P64", E * b, E * b + E), 0.015625, A("oe"))
+            if t == R - 1 and ZG[4 * t + b] == "v":
+                ops[-1]["chain"] = "b last"
+        for h in range(2):
+            zh = A("Z", 4 * H * h, 4 * H * (h + 1))
+            quant("qz", "sz", H * h, zh)
+            times("s", A("Z64", 4 * H * h, 4 * H * (h + 1)), zh, 64.0)
+            for b in range(4):
+                mm(4 * (1 - h) + b, H, "qw", "sw", 128 * b, "qz", "sz", H * h)
+            for b in range(4):
+                p_ = A("P64", E * b + H * h, E * b + H * h + H)
+                tt(p_, ps(4 * (1 - h) + b, 0, H), A("Z64", 4 * H * h + b, 4 * H * (h + 1), 4), ALU.add)
+                times(DN[4 * h + b], A("X", 4 * H * h + b, 4 * H * (h + 1), 4), p_, 0.015625)
+            quant("qx", "sx", H * h, A("X", 4 * H * h, 4 * H * (h + 1)))
+
+    act(A("LE", 0, C), A("W", 0, C), ACT.Identity, 168.0)
+    act(A("LE", C, E), A("WB"), ACT.Identity, 168.0)
+    dma("y", "oa", T.le[:], (T.LE[0:128:16, :],) + A("LE")[1:])
+    for h in range(2):
+        mm(4 - 2 * h, H, "qv", "sv", 0, "qx", "sx", H * h)
+        dma("y", "oa", T.oc[:, 4 * H * h:4 * H * (h + 1)], A("qx", H * h, H * (h + 1)), raw=True)
+        act(A("Y", H * h, H * (h + 1)), ps(4 - 2 * h, 0, H), ACT.Copy)
+        dma("y", "oa", T.y[:, H * h:H * (h + 1)], A("Y", H * h, H * (h + 1)))
+    for k in range(4):
+        dma("y", "oa", T.osc[4 * k:4 * k + 4, 0:C], A("sx", 0, C, 1, 32 * k, 32 * k + 4))
+    unpack(R - 1)
+    quant("qa", "sa", 0, A("X", 4 * (E - 128), 4 * E))
+    mm(5, 128, "qv", "sv", 0, "qa", "sa", 0)
+    dma("y", "oa", T.oc[:, 4 * C:4 * E], A("qa", 80, 128), raw=True)
+    for k in range(4):
+        dma("y" if k < 1 else "s", "oa" if k < 1 else "oz", T.osc[4 * k:4 * k + 4, C:E], A("sa", 80, 128, 1, 32 * k, 32 * k + 4))
+    cp(A("Y", C, E), ps(5, 80, 128))
+    dma("y", "oa", T.y[:, C:E], A("Y", C, E))
+    return ops

@@ -121,6 +121,48 @@ def _keeps(order, links):
         place[j] < place[i] for i in order for j in list(needs[i]) + ([] if soft[i] is None else [soft[i]]))
 
 
+def _time(o):
+    kind, n = o["size"]
+    if kind in ("v", "s"):
+        return max(64, n + 20) * 0.83
+    fixed, each = {"gat": (55, 1.3), "sca": (50, 3.1), "q": (12, 0.88), "pe": (10, 0.6), "g": (150, 1.66),
+                   "dma": (60, 0), "far": (300, 0), "none": (0, 0)}[kind]
+    return fixed + each * n
+
+
+def _order(ops, hop=200, look=50):
+    needs, soft = _links(ops)
+    n = len(ops)
+    hold = [_time(o) for o in ops]
+    fly = [{"dma": 900, "far": 1500}.get(o["size"][0], 0) for o in ops]
+    after = [[] for _ in ops]
+    for k in range(n):
+        for j in needs[k]:
+            after[j].append((k, hold[j] + (fly[j] if ops[j]["size"][0] == "dma" else 0) + (hop if ops[k]["fn"] else 0)))
+        if soft[k] is not None:
+            j = soft[k]
+            after[j].append((k, hold[j] + (0 if ops[k]["fn"] else fly[j])))
+    tail = [0] * n
+    for i in range(n - 1, -1, -1):
+        tail[i] = max([hold[i] + fly[i]] + [d + tail[k] for k, d in after[i]])
+    left = [len(needs[i]) + (soft[i] is not None) for i in range(n)]
+    can, free, order = [0] * n, {}, []
+    ready = [i for i in range(n) if left[i] == 0]
+    while ready:
+        at = {i: max(free.get(ops[i]["q"], 0), can[i]) for i in ready}
+        first = min(ready, key=lambda i: (at[i], -tail[i], i))
+        i = max((i for i in ready if ops[i]["q"] == ops[first]["q"] and at[i] <= at[first] + look), key=lambda i: (tail[i], -i))
+        ready.remove(i)
+        order.append(i)
+        free[ops[i]["q"]] = at[i] + hold[i]
+        for k, d in after[i]:
+            can[k] = max(can[k], at[i] + d)
+            left[k] -= 1
+            if left[k] == 0:
+                ready.append(k)
+    return order
+
+
 def _emit(g, T, ops):
     eng = {"v": g.vector, "s": g.scalar, "t": g.tensor, "g": g, "y": g.sync}
     known, clock, waits, batch = {q: {} for q in list(eng) + ["x"]}, [], [], {}
@@ -171,8 +213,9 @@ def rank_program(g, core, T, topo):
     if rank is None:
         return
     ops = _calls(g, core, T, topo, rank)
-    assert _keeps(ORDER, _links(ops))
-    _emit(g, T, [ops[i] for i in ORDER])
+    order = _order(ops)
+    assert _keeps(order, _links(ops))
+    _emit(g, T, [ops[i] for i in order])
     g.wait_ge(T.sem.sent, 16 * R)
 
 

@@ -2,37 +2,30 @@ from concourse.mybir import dt, AluOpType, ActivationFunctionType
 
 ALU, ACT = AluOpType, ActivationFunctionType
 C, K, E, R = 288, 48, 336, 3
-H = C // 2
 BIG = 2.0e29
 CODE = "float8_e4m3fn_x4"
-NV = 12
-RW = 8 * NV
-WG = "ssssssssvvss"
-ZG = "vvssvvssvsss"
-DN = "ssssssvv"
-GE = "ssv"
-ORDER = [
-    7,0,25,27,30,6,14,13,10,37,11,12,9,38,16,150,33,45,32,8,57,56,52,55,49,50,68,69,54,15,19,18,17,59,28,34,39,43,40,22,41,
-    36,53,44,31,1,2,3,4,175,176,42,35,58,26,87,29,89,92,93,88,90,133,108,98,94,100,104,95,91,127,125,128,129,123,131,151,
-    152,99,102,115,112,134,153,96,120,121,97,117,154,109,114,110,161,135,116,155,118,51,106,122,119,156,136,124,145,126,
-    137,139,140,141,101,162,103,107,157,105,130,132,138,113,111,166,146,172,142,143,144,61,147,163,167,158,168,159,164,169,
-    21,165,160,173,174,148,179,71,149,20,178,170,70,72,180,171,181,62,182,63,183,64,23,184,47,24,177,60,185,187,186,188,48,
-    189,311,65,190,66,216,192,193,194,191,195,199,203,197,217,219,196,200,198,201,202,204,218,235,238,239,46,236,207,205,
-    206,208,209,5,74,75,76,77,78,73,220,221,211,212,245,213,222,237,241,242,214,215,225,243,244,223,240,232,233,226,227,
-    247,228,229,246,248,224,230,249,251,86,67,231,234,255,256,250,253,295,254,278,281,282,269,259,271,283,265,257,260,294,
-    279,267,273,276,272,252,288,284,286,287,292,290,275,266,312,313,263,274,296,261,314,315,316,317,318,319,320,321,322,
-    285,291,298,262,297,300,301,293,323,325,324,210,352,289,351,326,354,270,302,327,328,280,258,277,329,303,306,330,334,
-    343,299,268,337,264,342,338,307,331,304,305,333,308,332,309,348,349,310,350,335,344,339,345,340,336,341,346,355,356,
-    347,357,358,359,360,361,363,362,353,364,367,368,370,369,365,366,392,394,371,379,373,393,372,374,380,377,375,376,378,
-    395,411,415,412,416,414,79,80,81,82,384,382,381,383,83,386,385,487,396,397,419,420,387,423,388,424,389,401,399,413,417,
-    418,390,391,404,405,398,400,402,408,409,403,421,406,407,422,425,427,410,426,431,432,429,428,464,460,462,468,461,463,
-    469,471,455,458,430,457,433,443,447,451,449,470,441,454,448,437,452,435,450,456,472,488,489,490,491,492,493,494,465,
-    466,467,474,434,439,445,438,473,495,496,497,498,501,500,499,502,527,530,529,528,459,503,504,475,505,476,482,506,519,
-    510,440,436,442,513,453,446,444,515,520,516,511,477,478,479,480,481,483,509,508,518,484,514,507,485,524,486,525,526,
-    517,521,512,522,531,532,523,533,534,535,536,537,539,540,544,543,538,546,545,603,548,602,604,84,547,541,553,554,555,556,
-    549,550,551,552,542,569,571,570,559,560,558,562,85,557,561,563,564,565,566,568,572,587,575,591,573,574,576,582,578,592,
-    590,589,577,580,584,588,597,579,583,585,581,595,599,598,600,593,596,586,605,606,594,601,615,610,616,609,607,608,613,
-    567,617,619,618,620,611,614,612,621,622,623,624,625,626,627,629,631,628,630,632,633,639,638,635,636,634,637,640]
+LAND, GAP = 42, 128
+CFG = {
+    "NV": 17,
+    "SS": 10, "ZE": "s",
+    "H": 128,
+    "UC": "s",
+    "XG": "s",
+    "PW": "ssss",
+    "SC": (8,),
+    "WG": "vsvv",
+    "QC": "vsv",
+    "GE": "s",
+    "ZG": "vvssvsss",
+    "Z6": "ss",
+    "DN": "sssvssvv",
+    "KC": "sss",
+    "K96": False, "T8": True, "GP": True, "CVP": False,
+    "SPLIT": True,
+    "HOP": 190, "ADD": 45, "TURNS": 2500,
+}
+FLIGHT = {"dma": 900, "far": 1500}
+RWMAX = 8 * 17
 
 
 def _sb(n, d):
@@ -50,40 +43,35 @@ SCRATCH = {
     "ONE": _sb(512, "bfloat16"), "ZT": _sb(512, "bfloat16"), "OD1": _sb(512, "bfloat16"), "OD": _sb(512, "bfloat16"),
     "qo": _sb(128, CODE), "so": _sb(128, "uint8"), "q0": _sb(128, CODE), "s0": _sb(128, "uint8"),
     "EM": _sb(4 * 528, "bfloat16"), "qe": _sb(528, CODE), "se": _sb(528, "uint8"),
-    "PI": _sb(2, "int32"), "PB": _sb(5, "int32"), "PF": _sb(5, "float32"), "PC": _sb(10, "float32"),
-    "RI": _sb(C, "float32"), "AM": _sb(C, "float32"), "RR": _sb(C, "float32"), "AC": _sb(C, "float32"),
-    "KEEP": _sb(C, "bfloat16"), "IV": _sb(E, "bfloat16"), "CI": _sb(18, "float32"), "CM": _sb(18, "float32"),
-    "UI": _sb(8, "int32"), "ou": _sb(8, "uint16"),
-    "LI": _sb(6, "float32"), "LA": _sb(18, "int32"), "LB": _sb(18, "float32"), "ol": _sb(6, "uint16"),
-    "BI": _sb(4, "float32"), "ob": _sb(4, "uint16"), "KI": _sb(4, "float32"), "ok": _sb(4, "uint16"),
+    "PI": _sb(2, "int32"), "PB": _sb(4, "int32"), "PF": _sb(4, "float32"), "PC": _sb(16, "float32"),
+    "RI": _sb(C, "bfloat16"), "AM": _sb(C, "bfloat16"), "RR": _sb(C, "bfloat16"), "AG": _sb(C, "float32"),
+    "AT": _sb(C, "float32"), "AE": _sb(C, "bfloat16"), "AV": _sb(C, "float32"), "DA": _sb(C, "bfloat16"),
+    "IV": _sb(E, "bfloat16"), "LI": _sb(40, "float32"),
+    "ou": _sb(8, "uint16"), "ob": _sb(4, "uint16"), "ok": _sb(4, "uint16"), "ox": _sb(12, "uint16"),
     "KX": _sb(C, "float32"), "SH": _sb(C, "float32"), "KXW": _sb(K, "float32"), "SHW": _sb(K, "float32"),
-    "TT": _sb(4 * 832, "bfloat16"), "qt": _sb(1024, CODE), "st": _sb(1024, "uint8"),
-    "TW": _sb(512, "bfloat16"), "qtw": _sb(128, CODE), "stw": _sb(128, "uint8"),
-    "SG": _sb(2448, "bfloat16"), "SGW": _sb(3 * C, "bfloat16"), "SGX": _sb(3 * C, "bfloat16"),
-    "CN": _sb(4, "float32"), "BC": _sb(96, "float32"), "BD": _sb(96, "float32"),
-    "RS": _sb(18 * RW, "float32"), "DS": _sb(C, "bfloat16"), "U0": _sb(18, "float32"), "U1": _sb(18, "float32"),
-    "CV": _sb(C, "float32"), "RK": _sb(18, "float32"), "ork": _sb(18, "uint16"),
-    "CW": _sb(K, "float32"), "orb": _sb(4, "uint16"), "KU": _sb(K, "float32"), "KS": _sb(K, "float32"),
+    "TT": _sb(4 * 800, "bfloat16"), "qt": _sb(1088, CODE), "st": _sb(1088, "uint8"),
+    "TW": _sb(3 * K, "bfloat16"), "TE": _sb(3 * K, "bfloat16"), "RW": _sb(3 * K, "bfloat16"),
+    "SG": _sb(2448, "bfloat16"), "SGW": _sb(3 * C, "bfloat16"), "SGX": _sb(3 * (C + 64), "bfloat16"),
+    "CN": _sb(4, "float32"), "BC": _sb(144 + 96, "bfloat16"), "BD": _sb(96, "bfloat16"),
+    "RS": _sb(18 * RWMAX, "bfloat16"), "CA": _sb(18, "float32"), "DS": _sb(C, "bfloat16"),
+    "CV": _sb(C, "float32"), "ork": _sb(18, "uint16"),
+    "orb": _sb(4, "uint16"), "KU": _sb(K, "float32"), "KS": _sb(2 * K, "float32"), "o96": _sb(6, "uint16"),
     "PP": _sb(K, "float32"), "CP": _sb(K, "float32"), "op": _sb(4, "uint16"),
-    "B0": _sb(K, "bfloat16"), "W": _sb(C + K, "bfloat16"), "WB": _sb(K, "bfloat16"),
-    "CE": _sb(C, "float32"), "oe": _sb(18, "uint16"), "CB": _sb(K, "float32"), "ow": _sb(4, "uint16"),
-    "MW64": _sb(4 * K, "bfloat16"), "MW": _sb(512, "bfloat16"),
+    "B0": _sb(K, "bfloat16"), "W": _sb(R * E, "bfloat16"), "WB": _sb(K, "bfloat16"),
+    "CE": _sb(C, "float16"), "oe": _sb(18, "uint16"), "CB": _sb(K, "float32"), "ow": _sb(4, "uint16"),
+    "MW64": _sb(512, "bfloat16"), "ST": _sb(256, "bfloat16"), "BU": _sb(32, "bfloat16"), "NEG": _sb(32, "bfloat16"),
     "G": _sb(64, "bfloat16"), "TB": _sb(64, "bfloat16"), "BT": _sb(512, "bfloat16"),
+    "qb": _sb(128 * R, CODE), "sb": _sb(128 * R, "uint8"),
+    "ql": _sb(LAND + GAP * R, CODE), "sl": _sb(LAND + GAP * R, "uint8"),
     "LE": _sb(E, "float32"), "Y": _sb(E, "float32"),
 }
-for _t in range(R):
-    SCRATCH["qb%d" % _t] = _sb(128, CODE)
-    SCRATCH["sb%d" % _t] = _sb(128, "uint8")
-    SCRATCH["ql%d" % _t] = _sb(32, CODE)
-    SCRATCH["sl%d" % _t] = _sb(32, "uint8")
-    SCRATCH["qm%d" % _t] = _sb(192, CODE)
-    SCRATCH["sm%d" % _t] = _sb(192, "uint8")
 for _b in range(8):
     SCRATCH["ps%d" % _b] = ("psum", [128, 512], "float32")
 
-DMA_SEMS = ["ldu", "ldx", "ldz", "ldw", "lds", "ldv", "sh0", "sh1", "sh2", "oa", "oz"] + ["z%d" % _i for _i in range(4 * R)]
+DMA_SEMS = ["ldu", "ldx", "ldz", "ldw", "lds", "ldv", "sh0", "sh1", "sh2", "oa", "oz"] + ["z%d" % _i for _i in range(14)]
 SEMAPHORES = ["cv", "cs", "ct", "cg", "sent", "arr0", "arr1", "arr2"] + DMA_SEMS
 COUNTER = {"v": "cv", "s": "cs", "t": "ct", "g": "cg"}
+WIDTH = {"float32": 4, "int32": 4, "bfloat16": 2, "float16": 2, "uint16": 2, "uint8": 1, CODE: 4}
 
 
 def _clash(a, b):
@@ -96,71 +84,92 @@ def _clash(a, b):
     return not a[3].isdisjoint(b[3])
 
 
-def _needs(ops):
-    seen, needs = {}, []
+def _links(ops):
+    seen, needs, soft, prev = {}, [], [], {}
     for i, o in enumerate(ops):
-        needs.append(set(j for a in o["acc"] for (j, b) in seen.get(a[0], []) if _clash(a, b)))
+        hard, order = set(), set()
+        for a in o["acc"]:
+            hard.update(j for j, b in seen.get(a[0], []) if _clash(a, b))
         for a in o["acc"]:
             seen.setdefault(a[0], []).append((i, a))
-    return needs
-
-
-def _links(ops):
-    needs, soft, prev = _needs(ops), [None] * len(ops), {}
-    for i, o in enumerate(ops):
         if o["chain"] is not None:
-            soft[i] = prev.get(o["chain"])
+            if o["chain"] in prev:
+                order.add(prev[o["chain"]])
             prev[o["chain"]] = i
+        needs.append(hard)
+        soft.append(order - hard)
     return needs, soft
-
-
-def _keeps(order, links):
-    needs, soft = links
-    place = {i: n for n, i in enumerate(order)}
-    return sorted(order) == list(range(len(needs))) and all(
-        place[j] < place[i] for i in order for j in list(needs[i]) + ([] if soft[i] is None else [soft[i]]))
 
 
 def _time(o):
     kind, n = o["size"]
     if kind in ("v", "s"):
-        return max(64, n + 20) * 0.83
+        return max(64, n + CFG["ADD"]) * 0.83
     fixed, each = {"gat": (55, 1.3), "sca": (50, 3.1), "q": (12, 0.88), "pe": (10, 0.6), "g": (150, 1.66),
                    "dma": (60, 0), "far": (300, 0), "none": (0, 0)}[kind]
     return fixed + each * n
 
 
-def _order(ops, hop=200, look=50):
-    needs, soft = _links(ops)
+def _place(seq, behind, hold, queue, first):
+    start, busy = [0] * len(hold), {}
+    for i in seq:
+        at = max([first[i]] + [start[j] + d for j, d in behind[i]])
+        line = busy.setdefault(queue[i], [])
+        n = len(line)
+        while n and line[n - 1][1] > at:
+            n -= 1
+        while n < len(line) and line[n][0] < at + hold[i]:
+            at = max(at, line[n][1])
+            n += 1
+        line.insert(n, (at, at + hold[i]))
+        start[i] = at
+    return start
+
+
+_ORDERS = {}
+
+
+def _order(ops):
     n = len(ops)
-    hold = [_time(o) for o in ops]
-    fly = [{"dma": 900, "far": 1500}.get(o["size"][0], 0) for o in ops]
-    after = [[] for _ in ops]
+    if n in _ORDERS:
+        return _ORDERS[n]
+    needs, soft = _links(ops)
+    hold, queue = [_time(o) for o in ops], [o["q"] for o in ops]
+    fly = [FLIGHT.get(o["size"][0], 0) for o in ops]
+    land = [f if o["size"][0] == "dma" else 0 for o, f in zip(ops, fly)]
+    before, after = [[] for _ in ops], [[] for _ in ops]
     for k in range(n):
-        for j in needs[k]:
-            after[j].append((k, hold[j] + (fly[j] if ops[j]["size"][0] == "dma" else 0) + (hop if ops[k]["fn"] else 0)))
-        if soft[k] is not None:
-            j = soft[k]
-            after[j].append((k, hold[j] + (0 if ops[k]["fn"] else fly[j])))
+        for j in sorted(needs[k] | soft[k]):
+            if j in soft[k]:
+                gap = 0 if ops[k]["fn"] else fly[j]
+            else:
+                gap = land[j] + CFG["HOP"] if ops[k]["fn"] else 0
+            before[k].append((j, hold[j] + gap))
+            after[j].append((k, hold[k] + gap))
+
+    def plan(key):
+        key = list(key)
+        for i in range(n):
+            key[i] = max([key[i]] + [key[j] + 0.001 for j, d in before[i]])
+        plans = [_place(sorted(range(n), key=lambda i: key[i]), before, hold, queue, [0] * n)]
+        late = _place(sorted(range(n), key=lambda i: (-plans[0][i] - hold[i], -i)), after, hold, queue, land)
+        plans.append(_place(sorted(range(n), key=lambda i: (-late[i] - hold[i], i)), before, hold, queue, [0] * n))
+        return min((max(s[i] + hold[i] + land[i] for i in range(n)), s) for s in plans)
+
     tail = [0] * n
     for i in range(n - 1, -1, -1):
-        tail[i] = max([hold[i] + fly[i]] + [d + tail[k] for k, d in after[i]])
-    left = [len(needs[i]) + (soft[i] is not None) for i in range(n)]
-    can, free, order = [0] * n, {}, []
-    ready = [i for i in range(n) if left[i] == 0]
-    while ready:
-        at = {i: max(free.get(ops[i]["q"], 0), can[i]) for i in ready}
-        first = min(ready, key=lambda i: (at[i], -tail[i], i))
-        i = max((i for i in ready if ops[i]["q"] == ops[first]["q"] and at[i] <= at[first] + look), key=lambda i: (tail[i], -i))
-        ready.remove(i)
-        order.append(i)
-        free[ops[i]["q"]] = at[i] + hold[i]
-        for k, d in after[i]:
-            can[k] = max(can[k], at[i] + d)
-            left[k] -= 1
-            if left[k] == 0:
-                ready.append(k)
-    return order
+        tail[i] = max([fly[i]] + [d + tail[k] for k, d in after[i]])
+    best, seed = plan([-tail[i] - hold[i] for i in range(n)]), [1]
+
+    def draw():
+        seed[0] = seed[0] * 16807 % 2147483647
+        return seed[0] / 2147483647
+
+    for turn in range(CFG["TURNS"]):
+        mid, wide, far = draw() * best[0], (500, 1500, 4000)[turn % 3], (100, 300, 800)[turn // 3 % 3]
+        best = min(best, plan([s + (far * (2 * draw() - 1) if abs(s - mid) < wide else 0) for s in best[1]]), key=lambda b: b[0])
+    _ORDERS[n] = sorted(range(n), key=lambda i: (best[1][i], i))
+    return _ORDERS[n]
 
 
 def _emit(g, T, ops):
@@ -169,7 +178,7 @@ def _emit(g, T, ops):
     for i, o in enumerate(ops):
         if o["sem"]:
             batch.setdefault(o["sem"], []).append(i)
-    for i, (o, nd) in enumerate(zip(ops, _needs(ops))):
+    for i, (o, nd) in enumerate(zip(ops, _links(ops)[0])):
         need = {}
         for j in nd:
             key = ops[j]["sem"] or ops[j]["q"]
@@ -213,14 +222,15 @@ def rank_program(g, core, T, topo):
     if rank is None:
         return
     ops = _calls(g, core, T, topo, rank)
-    order = _order(ops)
-    assert _keeps(order, _links(ops))
-    _emit(g, T, [ops[i] for i in order])
+    _emit(g, T, [ops[i] for i in _order(ops)])
     g.wait_ge(T.sem.sent, 16 * R)
 
 
 def _calls(g, core, T, topo, rank):
     N = len(T.cores)
+    NV, SS, H = CFG["NV"], CFG["SS"], CFG["H"]
+    RW = 8 * NV
+    pieces = ((0, H), (H, C))
     ops = []
 
     def A(name, c0=0, c1=None, step=1, p0=0, p1=128):
@@ -237,39 +247,40 @@ def _calls(g, core, T, topo, rank):
     def val(a):
         return a[0] if isinstance(a, tuple) else a
 
-    def span(out, a, rate=None, off=None, q="v"):
+    def span(out, ins, rate=None, off=None, q="v"):
         if off is not None:
             return ("gat", 16 * len(off[4]))
         if rate is None:
-            rate = 0.5 if all(SCRATCH[z[1]][2] == "bfloat16" for z in (out, a)) else 1.0
-        return (q, len(a[4]) * rate)
+            rate = 0.5 if all(WIDTH[SCRATCH[z[1]][2]] == 2 for z in [out] + ins) else 1.0
+        return (q, len(ins[0][4]) * rate)
 
     def ts(out, a, s1, op0, s2=None, op1=None, off=None):
         src = a[0] if off is None else a[0].indirect(off[0])
         if op1 is None:
-            rec("v", lambda: g.vector.tensor_scalar(out[0], src, val(s1), None, op0), [out], [a, s1, off], span(out, a, None, off))
+            rec("v", lambda: g.vector.tensor_scalar(out[0], src, val(s1), None, op0), [out], [a, s1, off], span(out, [a], None, off))
         else:
-            rec("v", lambda: g.vector.tensor_scalar(out[0], src, val(s1), val(s2), op0, op1), [out], [a, s1, s2, off], span(out, a, None, off))
+            rec("v", lambda: g.vector.tensor_scalar(out[0], src, val(s1), val(s2), op0, op1), [out], [a, s1, s2, off], span(out, [a], None, off))
 
     def tt(out, a, b, op, off=None):
         src = a[0] if off is None else a[0].indirect(off[0])
         rec("v", lambda: g.vector.tensor_tensor(out[0], src, b[0], op), [out], [a, b, off],
-            span(out, a, 1.0 if a[1].startswith("ps") else 2.0, off))
+            span(out, [a], 1.0 if a[1].startswith("ps") else 2.0, off))
 
     def cp(out, a):
-        rec("v", lambda: g.vector.tensor_copy(out[0], a[0]), [out], [a], span(out, a))
+        rec("v", lambda: g.vector.tensor_copy(out[0], a[0]), [out], [a], span(out, [a]))
 
     def scatter(win, off, a):
         rec("v", lambda: g.vector.tensor_copy(win[0].indirect(off[0]), a[0]), [win], [a, off], ("sca", len(a[4])))
 
     def scan(out, d0, d1, init, op0, op1):
-        rec("v", lambda: g.vector.tensor_tensor_scan(out[0], d0[0], d1[0], init, op0, op1), [out], [d0, d1], span(out, d1))
+        rec("v", lambda: g.vector.tensor_tensor_scan(out[0], d0[0], d1[0], val(init), op0, op1), [out], [d0, d1, init],
+            span(out, [d0, d1]))
 
     def turn(out, a):
-        rec("v", lambda: g.vector.transpose(out[0], a[0]), [out], [a], span(out, a))
+        rec("v", lambda: g.vector.transpose(out[0], a[0]), [out], [a], span(out, [a]))
 
     def fill(out, c):
-        rec("v", lambda: g.vector.memset(out[0], c), [out], [], span(out, out))
+        rec("v", lambda: g.vector.memset(out[0], c), [out], [], span(out, [out]))
 
     def quant(qn, sn, c0, a):
         n = len(a[4]) // 4
@@ -279,8 +290,8 @@ def _calls(g, core, T, topo, rank):
     def pick(qo, so, n, qi, si, nw, off):
         a, b, c, d = A(qo, 0, n), A(so, 0, n), A(qi, 0, nw), A(si, 0, nw)
         rec("v", lambda: g.vector.tensor_copy(a[0].bitcast(dt.uint32), c[0].bitcast(dt.uint32).indirect(off[0])), [a], [c, off],
-            span(a, c, None, off))
-        rec("s", lambda: g.scalar.activation(b[0], d[0].indirect(off[0]), ACT.Copy), [b], [d, off], span(b, d, None, off))
+            span(a, [c], None, off))
+        rec("s", lambda: g.scalar.activation(b[0], d[0].indirect(off[0]), ACT.Copy), [b], [d, off], span(b, [d], None, off))
 
     def act(out, a, func, bias=None, scale=None, acc=None, off=None):
         src = a[0] if off is None else a[0].indirect(off[0])
@@ -292,7 +303,7 @@ def _calls(g, core, T, topo, rank):
         if acc is not None:
             kw["accum_out"] = acc[0]
         rec("s", lambda: g.scalar.activation(out[0], src, func, **kw), [out] + ([acc] if acc else []), [a, bias, scale, off],
-            span(out, a, 1.0, off, "s"))
+            span(out, [a], 1.0, off, "s"))
 
     def times(on, out, a, c, off=None):
         if on == "s":
@@ -334,84 +345,106 @@ def _calls(g, core, T, topo, rank):
     def ps(bank, c0, c1, p0=0, p1=128):
         return A("ps%d" % bank, c0, c1, 1, p0, p1)
 
+    T8 = CFG["T8"]
     dma("y", "ldu", A("U"), T.u[:], chain="loads")
     dma("y", "ldx", A("X", 0, 4 * H), T.x[:, 0:4 * H], chain="loads")
     dma("y", "ldz", A("X", 4 * H, 4 * E), T.x[:, 4 * H:4 * E], chain="loads")
     dma("y", "ldw", A("qw"), T.wc[:], raw=True, chain="loads")
     dma("y", "lds", A("sw"), T.ws[:], chain="loads")
     dma("y", "ldv", A("V"), T.v[:], chain="loads")
-    iota(A("PI", 0, 1), [[0, 1]], 0, 1, False)
-    iota(A("UI"), [[16, 8]], 0, 0, False)
-    iota(A("RI"), [[0, 18], [16384, 16]], 0, 0)
+    iota(col("PI", 0), [[0, 1]], 0, 1, False)
+    iota(A("LI", 0, 8), [[16, 8]], 0, 0)
+    iota(A("RI"), [[0, 18], [1, 16]], 0, 0)
+    iota(col("PF", 3), [[0, 1]], 0, 1)
     fill(A("ONE"), 1.0)
-    for j, (c, op) in enumerate(((15, ALU.bitwise_and), (12, ALU.bitwise_and), (3, ALU.bitwise_and),
-                                 (5, ALU.arith_shift_right), (31, ALU.bitwise_and))):
-        ts(col("PB", j), A("PI", 0, 1), c, op)
-    cp(A("ou"), A("UI"))
-    cp(A("PF"), A("PB"))
-    q = col("PF", 0)
-    act(col("PC", 0), q, ACT.Identity, 0.0, 16384.0)
-    act(col("PC", 1), q, ACT.Identity, 15000.0, 16384.0)
-    act(col("PC", 2), q, ACT.Identity, -7681.0, 512.0)
-    act(col("PC", 3), q, ACT.Identity, -7680.0, 512.0)
-    act(col("PC", 4), q, ACT.Identity, -7680.0 + 168.0, 512.0)
-    act(col("PC", 5), q, ACT.Identity, 0.0, 511.0)
-    act(col("PC", 6), col("PF", 1), ACT.Identity, col("PF", 2), 8.0)
-    act(col("PC", 7), col("PF", 3), ACT.Identity, col("PC", 6), 8.0)
+    for j, c in enumerate((15, 3, 31)):
+        ts(col("PB", j), col("PI", 0), c, ALU.bitwise_and)
+    cp(A("ou"), A("LI", 0, 8))
+    cp(A("PF", 0, 3), A("PB", 0, 3))
+    q, q3, q31, p = (col("PF", j) for j in range(4))
     fill(A("RR"), -BIG)
     fill(A("RR", 0, C, 16), BIG)
     fill(A("ZT"), 0.0)
-    ts(A("AM"), A("RI"), col("PC", 0), ALU.not_equal, BIG, ALU.mult)
-    ts(A("AC"), A("RI"), col("PC", 1), ALU.subtract, 512.0, ALU.min)
-    for c0, c1 in ((240, 288), (464, 512), (624, 672), (720, 832)):
+    act(A("NEG"), A("ONE", 0, 32), ACT.Copy, None, -1.0)
+    zero(A("ST"))
+    ts(A("AM"), A("RI"), q, ALU.not_equal, BIG, ALU.mult)
+    act(col("PC", 0), q, ACT.Identity, 2.0)
+    act(A("AG"), A("RI"), ACT.Relu, col("PC", 0), -1.0)
+    act(A("AT"), A("AG"), ACT.Square, -24.0, 32.0)
+    act(A("AE"), A("AT"), ACT.Identity, 576.0, -1.0)
+    act(A("AV", 0, C - 1), A("AT", 1, C), ACT.Identity, 576.0, -1.0)
+    ts(col("PC", 1), q, 15.0, ALU.is_lt, -512.0, ALU.mult)
+    act(col("PC", 2), col("PC", 1), ACT.Identity, 168.0)
+    act(col("PC", 3), col("PC", 1), ACT.Identity, 1024.0 + 159.0)
+    act(col("PC", 4), q, ACT.Identity, col("PC", 3), -1.0)
+    if T8:
+        act(col("PC", 14), q3, ACT.Identity, 0.0, 63.75)
+        act(col("PC", 15), q, ACT.Identity, col("PC", 14), 0.25)
+        act(col("PC", 5), q3, ACT.Identity, 0.0, 7.75)
+        act(col("PC", 8), q, ACT.Identity, col("PC", 5), 0.25)
+        for b in range(4):
+            zero(A("MW64", 64 * b + K, 64 * b + 64))
+    else:
+        act(col("PC", 5), q3, ACT.Identity, 0.0, -7.0)
+        act(col("PC", 6), q, ACT.Identity, col("PC", 5), 8.0)
+        act(col("PC", 7), p, ACT.Identity, col("PC", 6), 0.25)
+        act(col("PC", 8), q31, ACT.Identity, col("PC", 7), -0.25)
+        zero(A("MW64", 192, 256))
+        zero(A("MW64", 448, 512))
+    act(col("PC", 9), q3, ACT.Identity, 0.0, 62.5)
+    act(col("PC", 10), q, ACT.Identity, col("PC", 9), 1.5)
+    if CFG["K96"]:
+        act(col("PC", 11), q31, ACT.Identity, q, -1.0)
+        act(col("PC", 12), col("PC", 11), ACT.Identity, float(K), -3.0)
+        act(col("PC", 13), col("PC", 11), ACT.Identity, float(2 * K), 3.0)
+    for m in range(3):
+        if CFG["KC"][m] == "v":
+            zero(A("SGX", (C + 64) * m + C, (C + 64) * (m + 1)))
+    for c0, c1 in ((240, 320), (496, 544), (656, 704), (752, 800)):
         zero(A("TT", 4 * c0, 4 * c1))
     quant("qu", "su", 0, A("U"))
     pick("qk", "sk", 128, "qu", "su", 128, A("ou"))
-    quant("qt", "st", 512, A("ZT"))
-    quant("qt", "st", 896, A("ZT"))
     quant("q0", "s0", 0, A("ZT"))
-    act(A("KEEP"), A("ONE", 0, C), ACT.Copy)
-    zero(A("KEEP", 0, C, 16))
-    zero(col("RS", RW - 1))
-    zero(A("TW", 4 * K, 512))
+    gaps = [("t", 896, 1024), ("t", 1024, 1088), ("t", 320, 416), ("l", 0, LAND)]
+    gaps += [("l", LAND + GAP * t + 6, LAND + GAP * (t + 1)) for t in range(R)]
+    for j, (n_, c0, c1) in enumerate(gaps):
+        dma("y", "z%d" % (2 * j), A("q" + n_, c0, c1), A("q0", 0, c1 - c0), raw=True, chain="loads")
+        dma("y", "z%d" % (2 * j + 1), A("s" + n_, c0, c1), A("s0", 0, c1 - c0), chain="loads")
+    zero(A("TE"))
+    zero(col("CA", 0))
     zero(A("ZW", 4 * K, 512))
-    zero(A("MW", 192, 256))
-    zero(A("MW", 448, 512))
     zero(A("EM", 2048, 2112))
     zero(A("BT", 32, 512))
+    iota(A("DA"), [[-16, 18], [512, 16]], 144, 0)
     sel(A("OD1"), A("ONE"), [[-16, 8], [0, 64]], ALU.is_ge, 0, 1)
     sel(A("OD"), A("OD1"), [[16, 8], [0, 64]], ALU.is_ge, 15, -1)
     quant("qo", "so", 0, A("OD"))
-    iota(A("CI"), [[16, 18]], 15 - 7680, 0)
-    act(A("CM"), A("CI"), ACT.Identity, col("PC", 5))
     iota(A("IV"), [[1, E]], -168, 0)
-    iota(A("LI"), [[-1, 2], [16, 3]], 2, 0)
-    iota(A("BI"), [[4, 2], [128, 2]], 0, 0)
-    iota(A("KI", 0, 3), [[32, 3]], 0, 0)
-    ts(A("LA", 0, 6), A("LI"), q, ALU.add)
-    ts(col("PC", 8), col("PF", 3), 3.0, ALU.is_lt, 256.0, ALU.mult)
-    ts(A("ob"), A("BI"), col("PC", 7), ALU.add, col("PC", 8), ALU.add)
-    ts(A("ok", 0, 3), A("KI", 0, 3), col("PF", 4), ALU.add)
-    ts(A("LA", 6, 12), A("LA", 0, 6), 7, ALU.bitwise_and)
-    ts(A("LA", 12, 18), A("LA", 0, 6), 3, ALU.arith_shift_right)
-    ts(A("LB", 0, 6), A("LA", 6, 12), 0.0, ALU.is_equal)
-    ts(A("LB", 6, 12), A("LA", 12, 18), -17.0, ALU.add)
-    tt(A("LB", 12, 18), A("LB", 0, 6), A("LB", 6, 12), ALU.mult)
-    ts(A("ol"), A("LB", 12, 18), 16.0, ALU.add)
+    iota(A("LI", 8, 11), [[32, 3]], 0, 0)
+    iota(A("LI", 12, 16), [[0, 2], [4, 2]] if T8 else [[4, 2], [128, 2]], 0, 0)
+    iota(A("LI", 16, 28), [[4 if T8 else 16, 12]], 0, 0)
+    iota(A("LI", 28, 40), [[1, 6], [24, 2]], 0, 0)
+    for t in range(R):
+        iota(A("W", E * t + C, E * t + E), [[0, K]], 1024, 0)
+    if not CFG["K96"]:
+        ts(A("ok", 0, 3), A("LI", 8, 11), q31, ALU.add)
+    if T8:
+        ts(A("ob", 0, 2), A("LI", 12, 14), col("PC", 8), ALU.add)
+    else:
+        ts(A("ob"), A("LI", 12, 16), col("PC", 8), ALU.add, 256.0, ALU.add)
+        ts(A("ob", 0, 4, 1, 96, 128), A("LI", 12, 16, 1, 96, 128), A("PC", 8, 9, 1, 96, 128), ALU.add)
+    ts(A("ox"), A("LI", 16, 28), col("PC", 15) if T8 else q, ALU.add)
+    ts(A("ox", 0, 12, 1, 0, 16), A("LI", 28, 40, 1, 0, 16), A("PC", 10, 11, 1, 0, 16), ALU.add)
     for a in range(4):
         sel(A("EM", 512 * a, 512 * a + 512), A("ONE"), [[-128, 4], [-1, 32], [128, 4]], ALU.is_equal, -32 * a, 1)
     quant("qe", "se", 0, A("EM", 0, 1056))
     quant("qe", "se", 264, A("EM", 1056, 2112))
-    for t in range(R):
-        for j, (n_, c0, c1) in enumerate((("l", 16, 18), ("m", 96, 192))):
-            dma("y", "z%d" % (4 * t + 2 * j), A("q%s%d" % (n_, t), c0, c1), A("q0", 0, c1 - c0), raw=True, chain="loads")
-            dma("y", "z%d" % (4 * t + 2 * j + 1), A("s%s%d" % (n_, t), c0, c1), A("s0", 0, c1 - c0), chain="loads")
     quant("qv", "sv", 0, A("V"))
 
     base = {}
     for m in range(1, 18):
-        c0, t_ = ((0, 18 - m) if m >= 15 else (288, 14 - m) if m >= 11 else (512, 10 - m) if m >= 7
-                  else (672, 6 - m) if m >= 3 else (800, 2 - m))
+        c0, t_ = ((0, 18 - m) if m >= 15 else (320, 14 - m) if m >= 11 else (544, 10 - m) if m >= 7
+                  else (704, 6 - m) if m >= 3 else (288, 2 - m))
         base[m] = 4 * c0 + t_
 
     def slot(m, c0=0, c1=None):
@@ -421,149 +454,164 @@ def _calls(g, core, T, topo, rank):
     def key(m):
         return col("SH", 16 * m + 15)
 
-    def wslot(t_, c0=0, c1=K):
-        return A("TW", 4 * c0 + t_, 4 * c1 + t_ - 3, 4)
-
     def unpack(t):
-        rec("x", None, [A("ql%d" % t, 0, 6), A("sl%d" % t, 0, 6)], [], ("none", 0), sem="arr%d" % t, full=16, chain="far%d" % t)
-        pick("qm%d" % t, "sm%d" % t, 96, "ql%d" % t, "sl%d" % t, 32, A("ol"))
+        c0 = LAND + GAP * t
+        rec("x", None, [A("ql", c0, c0 + 6), A("sl", c0, c0 + 6)], [], ("none", 0), sem="arr%d" % t, full=16, chain="far%d" % t)
         for h in range(8):
-            mm(7, 128, "qe", "se", 128 * (h // 2) + 16 * (h % 2), "qm%d" % t, "sm%d" % t,
-               (55 if h % 2 else 6) - h, h == 0, h == 7, grp="u%d" % t)
+            mm(7, 128, "qe", "se", 128 * (h // 2) + 16 * (h % 2), "ql", "sl", c0 - 6 * h, h == 0, h == 7, grp="u%d" % t)
         for b in range(4):
-            cp(A("X", 4 * C + b, 4 * E, 4, 0, 16), ps(7, 0, K, 32 * b, 32 * b + 16))
+            times(CFG["UC"], A("ST", 64 * b, 64 * b + K, 1, 0, 16), ps(7, 0, K, 32 * b, 32 * b + 16), 64.0)
+        times(CFG["XG"], A("X", 4 * C, 4 * E), A("ST"), 0.015625, A("ox"))
 
-    def keys(c0, c1):
-        out = []
-        if c0 < H:
-            out.append((c0, min(c1, H), ps(4, c0, min(c1, H))))
-        if c1 > H:
-            out.append((max(c0, H), c1, ps(2, max(c0, H) - H, c1 - H)))
-        return out
-
-    quant("qx", "sx", 0, A("X", 0, 4 * H))
-    quant("qx", "sx", H, A("X", 4 * H, 4 * C))
+    for c0, c1 in pieces:
+        quant("qx", "sx", c0, A("X", 4 * c0, 4 * c1))
     for t in range(R):
         first = t == 0
+        row = A("W", E * t, E * t + C)
+        whole = A("W", E * t, E * t + E)
         mm(4, H, "qk", "sk", 0, "qx", "sx", 0)
-        mm(2, H, "qk", "sk", 0, "qx", "sx", H)
-        mm(5, C, "qk", "sk", 0, "qx", "sx", 0)
-        for c0, c1, k_ in keys(0, C):
-            tt(A("KX", c0, c1), k_, A("AM", c0, c1), ALU.add)
+        mm(0, C, "qk", "sk", 0, "qx", "sx", 0)
+        mm(1, C, "qk", "sk", 0, "qx", "sx", 0)
+        for bank, (c0, c1) in zip((4, 0), pieces):
+            tt(A("KX", c0, c1), ps(bank, c0, c1), A("AM", c0, c1), ALU.add)
             scan(A("SH", c0, c1), A("RR", c0, c1), A("KX", c0, c1), BIG, ALU.max, ALU.min)
+        for bank, (c0, c1) in (zip((4, 0), pieces) if CFG["SPLIT"] else [(0, (0, C))]):
+            tt(A("TT", 4 * c0, 4 * c1, 4), ps(bank, c0, c1), A("SH", c0, c1), ALU.is_ge)
+            scan(A("DS", c0, c1), A("DA", c0, c1), A("TT", 4 * c0, 4 * c1, 4), 1000.0, ALU.min, ALU.add)
+        if SS:
+            mm(6, H, "qk", "sk", 0, "qx", "sx", 0)
+        else:
+            act(col("RS", RW - 1), col("DS", 15), ACT.Copy)
         for m in range(1, 18):
-            if m <= NV:
-                for c0, c1, k_ in keys(0, 16 * m):
-                    ts(slot(m, c0, c1), k_, key(m), ALU.is_gt)
-                scan(A("RS", RW * m + RW - 8 * m, RW * m + RW), slot(m, 0, 8 * m), slot(m, 8 * m, 16 * m), 0.0, ALU.add, ALU.add)
+            if SS < m <= NV:
+                ts(slot(m), ps(4 if 16 * m < H else 0, 0, 16 * m), key(m), ALU.is_gt)
+                scan(A("RS", RW * m + RW - 8 * m, RW * m + RW), slot(m, 0, 8 * m), slot(m, 8 * m, 16 * m),
+                     col("DS", 16 * m + 15), ALU.add, ALU.add)
             else:
                 sg = A("SG", 8 * m * (m - 1), 8 * m * (m + 1))
-                act(sg, ps(5, 0, 16 * m), ACT.Sign, key(m), -1.0)
-                act(slot(m), sg, ACT.Relu, None, -1.0, col("RS", RW * m + RW - 1))
-        for c0, c1, k_ in keys(0, C):
-            tt(A("TT", 4 * c0, 4 * c1, 4), k_, A("SH", c0, c1), ALU.is_ge)
-        scan(A("DS"), A("KEEP"), A("TT", 0, 4 * C, 4), 0.0, ALU.mult, ALU.add)
-        quant("qt", "st", 576, A("TT", 4 * 512, 4 * 832))
-        quant("qt", "st", 288, A("TT", 4 * 288, 4 * 512))
-        quant("qt", "st", 0, A("TT", 0, 4 * 288))
-        for i, (c0, n) in enumerate(((288, 288), (576, 160), (736, 128), (864, 128), (0, 288))):
+                act(sg, ps(6 if 16 * m < H else 1, 0, 16 * m), ACT.Sign, key(m), -1.0)
+                act(slot(m), sg, ACT.Relu, None, -1.0, col("CA", m))
+        for m0, m1 in ((0, SS + 1), (NV + 1, 18)):
+            if m1 > max(m0, 1):
+                tt(A("RS", RW * (m0 + 1) - 1, RW * m1, RW), A("DS", 16 * m0 + 15, 16 * m1, 16), A("CA", m0, m1), ALU.add)
+        ts(ends("AV", C), A("RS", RW - 1, 18 * RW, RW), -1.0, ALU.mult, -1024.0, ALU.add)
+        quant("qt", "st", 640, A("TT", 4 * 544, 4 * 800))
+        quant("qt", "st", 0, A("TT", 0, 4 * 320))
+        quant("qt", "st", 416, A("TT", 4 * 320, 4 * 544))
+        for i, (c0, n) in enumerate(((800, C), (640, 160), (0, C), (288, 128), (416, 224))):
             mm(6, n, "qo", "so", 0, "qt", "st", c0, i == 0, i == 4, grp="c%d" % t)
-        scan(A("CV"), A("AC"), ps(6, 0, C), 0.0, ALU.add, ALU.max)
-        tt(A("U0"), ends("DS", C), A("CM"), ALU.subtract)
-        tt(A("U1"), A("U0"), A("RS", RW - 1, 18 * RW, RW), ALU.add)
-        tt(A("RK"), ends("CV", C), A("U1"), ALU.subtract)
-        cp(A("ork"), A("RK"))
-        scatter(A("W", 0, C), A("ork"), A("IV", 0, C))
-        fill(A("W", C, C + K), 1024.0)
+        cuts = list(zip((0,) + CFG["SC"], CFG["SC"] + (18,)))
+        for c0, c1 in (cuts if CFG["CVP"] else [(0, 18)]):
+            scan(A("CV", 16 * c0, 16 * c1), ps(6, 16 * c0, 16 * c1), A("AV", 16 * c0, 16 * c1), -1024.0, ALU.max, ALU.add)
+            ts(A("ork", c0, c1), A("CV", 16 * c0 + 15, 16 * c1, 16), col("PC", 4), ALU.add)
+        for c0, c1 in cuts:
+            scatter(row, A("ork", c0, c1), A("IV", 16 * c0, 16 * c1))
         if not first:
             unpack(t - 1)
         quant("qa", "sa", 0, A("X", 4 * (E - 128), 4 * E))
-        mm(0, 128, "qk", "sk", 0, "qa", "sa", 0)
-        tt(A("KXW"), ps(0, 80, 128), A("AM", 0, K), ALU.add)
+        mm(5, 128, "qk", "sk", 0, "qa", "sa", 0)
+        tt(A("KXW"), ps(5, 80, 128), A("AM", 0, K), ALU.add)
         scan(A("SHW"), A("RR", 0, K), A("KXW"), BIG, ALU.max, ALU.min)
-        tt(wslot(3), ps(0, 80, 128), A("SHW"), ALU.is_equal)
+        tt(A("TE", 0, 3 * K, 3), ps(5, 80, 128), A("SHW"), ALU.is_equal)
         for m in range(3):
             e_ = 16 * m + 16
             kw_ = col("SHW", e_ - 1)
-            ts(wslot(m, 0, e_), ps(0, 80, 80 + e_), kw_, ALU.is_gt)
+            ts(A("TW", K * m, K * m + e_), ps(5, 80, 80 + e_), kw_, ALU.is_gt)
             if e_ < K:
-                ts(wslot(m, e_, K), ps(0, 80 + e_, 128), kw_, ALU.is_ge)
-            act(A("SGW", C * m, C * m + C), ps(5, 0, C), ACT.Sign, kw_, -1.0)
-            act(A("SGX", C * m, C * m + C), A("SGW", C * m, C * m + C), ACT.Relu, None, -1.0, col("CN", m))
-            act(A("BC", 32 * m, 32 * m + 32), A("ZT", 0, 32), ACT.Identity, col("CN", m))
-        turn(A("BD"), A("BC"))
-        act(A("KU"), A("BD"), ACT.Identity, float(C), -1.0, off=A("ok", 0, 3))
-        quant("qtw", "stw", 0, A("TW"))
-        mm(3, 128, "qo", "so", 0, "qtw", "stw", 0)
-        scan(A("CW"), A("AC", 0, K), ps(3, 0, K), 0.0, ALU.add, ALU.max)
+                ts(A("TW", K * m + e_, K * m + K), ps(5, 80 + e_, 128), kw_, ALU.is_ge)
+            scan(A("RW", K * m, K * m + K), A("TW", K * m, K * m + K), A("TE", K * m, K * m + K), 0.0, ALU.add, ALU.add)
+        for m in (2, 1, 0):
+            kw_, x0 = col("SHW", 16 * m + 15), (C + 64) * m
+            if CFG["KC"][m] == "v":
+                ts(A("SGX", x0, x0 + C), ps(0, 0, C), kw_, ALU.is_le)
+                scan(A("BC", 32 * m, 176 + 32 * m), A("SGX", x0, x0 + C + 64, 2), A("SGX", x0 + 1, x0 + C + 64, 2),
+                     -144.0, ALU.add, ALU.add)
+            else:
+                act(A("SGW", C * m, C * m + C), ps(1, 0, C), ACT.Sign, kw_, -1.0)
+                act(A("SGX", x0, x0 + C), A("SGW", C * m, C * m + C), ACT.Relu, None, -1.0, col("CN", m))
+                act(A("BC", 144 + 32 * m, 176 + 32 * m), A("NEG"), ACT.Identity, 144.0, col("CN", m))
+        turn(A("BD"), A("BC", 144, 240))
         for b in range(4):
             c0 = 0 if first else C
-            act(A("P64", E * b + c0, E * b + E), A("X", 4 * c0 + b, 4 * E, 4), ACT.Copy, None, 64.0)
-        ts(A("orb", 0, 3), ends("CW", K), col("PC", 2), ALU.add)
+            times("s" if first else CFG["PW"][b], A("P64", E * b + c0, E * b + E), A("X", 4 * c0 + b, 4 * E, 4), 64.0)
+        ts(A("orb", 0, 3), A("RW", K - 1, 3 * K, K), -1.0, ALU.mult, float(K), ALU.add)
         scatter(A("B0"), A("orb", 0, 3), A("IV", C, E))
-        scatter(A("KS"), A("orb", 0, 3), A("KU"))
-        scan(A("PP"), A("ONE", 0, K), A("KS"), -1.0, ALU.add, ALU.max)
-        scan(A("CP"), A("AC", 0, K), A("PP"), 0.0, ALU.add, ALU.max)
-        ts(A("op", 0, 3), ends("CP", K), col("PC", 3), ALU.add)
-        tt(A("WB"), A("W"), A("B0"), ALU.min, off=A("op", 0, 3))
-        scatter(A("W"), A("op", 0, 3), A("B0"))
-        scan(A("CB"), A("AC", 0, K), A("WB"), 0.0, ALU.add, ALU.max)
-        ts(A("ow", 0, 3), ends("CB", K), col("PC", 4), ALU.add)
-        scan(A("CE"), A("AC"), A("W", 0, C), 0.0, ALU.add, ALU.max)
-        ts(A("oe"), ends("CE", C), col("PC", 4), ALU.add)
+        if CFG["K96"]:
+            for h in range(2):
+                ts(A("o96", h, 6, 2), A("RW", K - 1, 3 * K, K), -1.0, ALU.mult, col("PC", 12 + h), ALU.add)
+            scatter(A("KS"), A("o96"), A("BD"))
+        else:
+            act(A("KU"), A("BD"), ACT.Copy, off=A("ok", 0, 3))
+            scatter(A("KS", 0, K), A("orb", 0, 3), A("KU"))
+        scan(A("PP"), A("ONE", 0, K), A("KS", 0, K), -145.0, ALU.add, ALU.max)
+        scan(A("CP"), A("AE", 0, K), A("PP"), 0.0, ALU.add, ALU.max)
+        ts(A("op", 0, 3), ends("CP", K), col("PC", 1), ALU.add, 144.0, ALU.add)
+        tt(A("WB"), whole, A("B0"), ALU.min, off=A("op", 0, 3))
+        scatter(whole, A("op", 0, 3), A("B0"))
+        scan(A("CB"), A("AE", 0, K), A("WB"), 0.0, ALU.add, ALU.max)
+        ts(A("ow", 0, 3), ends("CB", K), col("PC", 2), ALU.add)
+        scan(A("CE"), A("AE"), row, 0.0, ALU.add, ALU.max)
+        ts(A("oe"), ends("CE", C), col("PC", 2), ALU.add)
         for b in range(4):
-            times(WG[4 * t + b], A("ZW", b, 4 * K, 4), A("P64", E * b, E * b + E), 0.015625, A("ow", 0, 3))
+            times(CFG["WG"][b], A("ZW", b, 4 * K, 4), A("P64", E * b, E * b + E), 0.015625, A("ow", 0, 3))
         quant("qzw", "szw", 0, A("ZW"))
-        times("s", A("ZW64"), A("ZW", 0, 4 * K), 64.0)
+        times(CFG["ZE"], A("ZW64"), A("ZW", 0, 4 * K), 64.0)
         for b in range(4):
             mm(b, 128, "qw", "sw", 128 * b, "qzw", "szw", 0)
-            tt(A("MW64", b, 4 * K, 4), ps(b, 0, K), A("ZW64", b, 4 * K, 4), ALU.add)
-        for a in range(3):
-            times("v", A("MW", 256, 256 + 4 * K, 1, 32 * a, 32 * a + 32), A("MW64", 0, 4 * K, 1, 96, 128), 0.015625)
-        times("v", A("MW", 0, 4 * K), A("MW64"), 0.015625)
-        times(GE[t], A("G"), A("MW"), 1.0, A("ob"))
-        dma("y", "sh%d" % t, A("X", 4 * C, 4 * E, 1, 16, 128), A("MW", 0, 4 * K, 1, 0, 112))
-        turn(A("TB"), A("G"))
-        cp(A("TB", 32, 48), A("TB", 16, 32))
-        turn(A("BT", 0, 32), A("TB", 32, 64))
-        quant("qb%d" % t, "sb%d" % t, 0, A("BT"))
-        if t == R - 1:
-            ops[-1]["chain"] = "b last"
+            tt(A("MW64", 64 * b, 64 * b + K) if T8 else A("MW64", b, 4 * K, 4), ps(b, 0, K), A("ZW64", b, 4 * K, 4), ALU.add)
+        n = 256 if T8 else 4 * K
+        dma("y", "sh%d" % t, A("ST", 0, n, 1, 16, 128), A("MW64", 0, n, 1, 0, 112))
+        if T8:
+            for h in (1, 0):
+                for a in range(4):
+                    turn(A("TB", 16 * h, 16 * h + 32, 1, 32 * a, 32 * a + 32), A("MW64", 2 * a + h, 256, 8, 96, 128))
+            turn(A("BU"), A("TB", 16, 48))
+            times(CFG["GE"], A("BT", 0, 32), A("BU"), 0.015625, A("ob", 0, 2))
+        else:
+            for a in range(3):
+                times(CFG["QC"][a], A("MW64", 256, 256 + 4 * K, 1, 32 * a, 32 * a + 32), A("MW64", 0, 4 * K, 1, 96, 128), 1.0)
+            times(CFG["GE"], A("G"), A("MW64"), 0.015625, A("ob"))
+            turn(A("TB", 16, 48), A("G", 32, 64))
+            turn(A("TB", 0, 32), A("G", 0, 32))
+            turn(A("BT", 0, 32), A("TB", 16, 48))
+        quant("qb", "sb", 128 * t, A("BT"))
         dst = T.cores[(rank + t + 1) % N]
         rid, pid = topo.addr(dst, core)
         mask = topo.mask(core, dst)
         assert len(topo.engines(core, dst)) == 8
 
         def ship(t=t, rid=rid, pid=pid, mask=mask):
-            g.remote_dma(T["ql%d" % t][:, 0:6].bitcast(dt.uint8), T["qb%d" % t][:, 0:6].bitcast(dt.uint8),
+            c0, b0 = LAND + GAP * t, 128 * t
+            g.remote_dma(T.ql[:, c0:c0 + 6].bitcast(dt.uint8), T.qb[:, b0:b0 + 6].bitcast(dt.uint8),
                          T.sem["arr%d" % t], T.sem.sent, pid, rid, mask)
-            return g.remote_dma(T["sl%d" % t][:, 0:6], T["sb%d" % t][:, 0:6], T.sem["arr%d" % t], T.sem.sent, pid, rid, mask)
+            return g.remote_dma(T.sl[:, c0:c0 + 6], T.sb[:, b0:b0 + 6], T.sem["arr%d" % t], T.sem.sent, pid, rid, mask)
 
-        rec("g", ship, [], [A("qb%d" % t, 0, 6), A("sb%d" % t, 0, 6)], ("far", 0), chain="far%d" % t)
-        for b in range(4):
-            times(ZG[4 * t + b], A("Z", b, 4 * C, 4), A("P64", E * b, E * b + E), 0.015625, A("oe"))
-            if t == R - 1 and ZG[4 * t + b] == "v":
-                ops[-1]["chain"] = "b last"
-        for h in range(2):
-            zh = A("Z", 4 * H * h, 4 * H * (h + 1))
-            quant("qz", "sz", H * h, zh)
-            times("s", A("Z64", 4 * H * h, 4 * H * (h + 1)), zh, 64.0)
+        rec("g", ship, [], [A("qb", 128 * t, 128 * t + 6), A("sb", 128 * t, 128 * t + 6)], ("far", 0), chain="far%d" % t)
+        for h, (c0, c1) in enumerate(pieces if CFG["GP"] else [(0, C)]):
             for b in range(4):
-                mm(4 * (1 - h) + b, H, "qw", "sw", 128 * b, "qz", "sz", H * h)
+                times(CFG["ZG"][4 * h + b], A("Z", 4 * c0 + b, 4 * c1, 4), A("P64", E * b, E * b + E), 0.015625,
+                      A("oe", c0 // 16, c1 // 16))
+        for h, (c0, c1) in enumerate(pieces):
+            n = c1 - c0
+            zh = A("Z", 4 * c0, 4 * c1)
+            quant("qz", "sz", c0, zh)
+            times(CFG["Z6"][h], A("Z64", 4 * c0, 4 * c1), zh, 64.0)
             for b in range(4):
-                p_ = A("P64", E * b + H * h, E * b + H * h + H)
-                tt(p_, ps(4 * (1 - h) + b, 0, H), A("Z64", 4 * H * h + b, 4 * H * (h + 1), 4), ALU.add)
-                times(DN[4 * h + b], A("X", 4 * H * h + b, 4 * H * (h + 1), 4), p_, 0.015625)
-            quant("qx", "sx", H * h, A("X", 4 * H * h, 4 * H * (h + 1)))
+                mm(4 * (1 - h) + b, n, "qw", "sw", 128 * b, "qz", "sz", c0)
+            for b in range(4):
+                p_ = A("P64", E * b + c0, E * b + c1)
+                tt(p_, ps(4 * (1 - h) + b, 0, n), A("Z64", 4 * c0 + b, 4 * c1, 4), ALU.add)
+                times(CFG["DN"][4 * h + b], A("X", 4 * c0 + b, 4 * c1, 4), p_, 0.015625)
+            quant("qx", "sx", c0, A("X", 4 * c0, 4 * c1))
 
-    act(A("LE", 0, C), A("W", 0, C), ACT.Identity, 168.0)
+    act(A("LE", 0, C), A("W", E * (R - 1), E * (R - 1) + C), ACT.Identity, 168.0)
     act(A("LE", C, E), A("WB"), ACT.Identity, 168.0)
     dma("y", "oa", T.le[:], (T.LE[0:128:16, :],) + A("LE")[1:])
-    for h in range(2):
-        mm(4 - 2 * h, H, "qv", "sv", 0, "qx", "sx", H * h)
-        dma("y", "oa", T.oc[:, 4 * H * h:4 * H * (h + 1)], A("qx", H * h, H * (h + 1)), raw=True)
-        act(A("Y", H * h, H * (h + 1)), ps(4 - 2 * h, 0, H), ACT.Copy)
-        dma("y", "oa", T.y[:, H * h:H * (h + 1)], A("Y", H * h, H * (h + 1)))
+    for bank, (c0, c1) in zip((4, 0), pieces):
+        mm(bank, c1 - c0, "qv", "sv", 0, "qx", "sx", c0)
+        dma("y", "oa", T.oc[:, 4 * c0:4 * c1], A("qx", c0, c1), raw=True)
+        act(A("Y", c0, c1), ps(bank, 0, c1 - c0), ACT.Copy)
+        dma("y", "oa", T.y[:, c0:c1], A("Y", c0, c1))
     for k in range(4):
         dma("y", "oa", T.osc[4 * k:4 * k + 4, 0:C], A("sx", 0, C, 1, 32 * k, 32 * k + 4))
     unpack(R - 1)

@@ -6,26 +6,26 @@ BIG = 2.0e29
 CODE = "float8_e4m3fn_x4"
 LAND, GAP = 42, 128
 CFG = {
-    "NV": 17,
-    "SS": 10, "ZE": "s",
+    "NV": 13,
+    "SS": 4, "ZE": "s",
     "H": 128,
-    "UC": "s",
+    "UC": "v",
     "XG": "s",
     "PW": "ssss",
-    "SC": (8,),
-    "WG": "vsvv",
-    "QC": "vsv",
+    "SC": (10,),
+    "WG": "ssvv",
     "GE": "s",
     "ZG": "vvssvsss",
     "Z6": "ss",
     "DN": "sssvssvv",
-    "KC": "sss",
-    "K96": False, "T8": True, "GP": True, "CVP": False,
+    "KC": "vss",
+    "R": [{}, {}, {}],
+    "K96": False, "GP": False, "CVP": True,
     "SPLIT": True,
-    "HOP": 190, "ADD": 45, "TURNS": 2500,
+    "HOP": 215, "ADD": {"v": 10, "s": 60}, "TURNS": 4000,
 }
-FLIGHT = {"dma": 900, "far": 1500}
-RWMAX = 8 * 17
+FLIGHT = {"dma": 1000, "far": 1700}
+RW = 8 * 17
 
 
 def _sb(n, d):
@@ -47,20 +47,20 @@ SCRATCH = {
     "RI": _sb(C, "bfloat16"), "AM": _sb(C, "bfloat16"), "RR": _sb(C, "bfloat16"), "AG": _sb(C, "float32"),
     "AT": _sb(C, "float32"), "AE": _sb(C, "bfloat16"), "AV": _sb(C, "float32"), "DA": _sb(C, "bfloat16"),
     "IV": _sb(E, "bfloat16"), "LI": _sb(40, "float32"),
-    "ou": _sb(8, "uint16"), "ob": _sb(4, "uint16"), "ok": _sb(4, "uint16"), "ox": _sb(12, "uint16"),
+    "ou": _sb(8, "uint16"), "ob": _sb(2, "uint16"), "ok": _sb(4, "uint16"), "ox": _sb(12, "uint16"),
     "KX": _sb(C, "float32"), "SH": _sb(C, "float32"), "KXW": _sb(K, "float32"), "SHW": _sb(K, "float32"),
     "TT": _sb(4 * 800, "bfloat16"), "qt": _sb(1088, CODE), "st": _sb(1088, "uint8"),
     "TW": _sb(3 * K, "bfloat16"), "TE": _sb(3 * K, "bfloat16"), "RW": _sb(3 * K, "bfloat16"),
     "SG": _sb(2448, "bfloat16"), "SGW": _sb(3 * C, "bfloat16"), "SGX": _sb(3 * (C + 64), "bfloat16"),
-    "CN": _sb(4, "float32"), "BC": _sb(144 + 96, "bfloat16"), "BD": _sb(96, "bfloat16"),
-    "RS": _sb(18 * RWMAX, "bfloat16"), "CA": _sb(18, "float32"), "DS": _sb(C, "bfloat16"),
+    "CN": _sb(4, "float32"), "BC": _sb(3 * 176, "bfloat16"), "BD": _sb(96, "bfloat16"),
+    "RS": _sb(18 * RW, "bfloat16"), "CA": _sb(18, "float32"), "DS": _sb(C, "bfloat16"),
     "CV": _sb(C, "float32"), "ork": _sb(18, "uint16"),
     "orb": _sb(4, "uint16"), "KU": _sb(K, "float32"), "KS": _sb(2 * K, "float32"), "o96": _sb(6, "uint16"),
     "PP": _sb(K, "float32"), "CP": _sb(K, "float32"), "op": _sb(4, "uint16"),
     "B0": _sb(K, "bfloat16"), "W": _sb(R * E, "bfloat16"), "WB": _sb(K, "bfloat16"),
     "CE": _sb(C, "float16"), "oe": _sb(18, "uint16"), "CB": _sb(K, "float32"), "ow": _sb(4, "uint16"),
-    "MW64": _sb(512, "bfloat16"), "ST": _sb(256, "bfloat16"), "BU": _sb(32, "bfloat16"), "NEG": _sb(32, "bfloat16"),
-    "G": _sb(64, "bfloat16"), "TB": _sb(64, "bfloat16"), "BT": _sb(512, "bfloat16"),
+    "MW64": _sb(256, "bfloat16"), "ST": _sb(256, "bfloat16"), "BU": _sb(32, "bfloat16"), "NEG": _sb(32, "bfloat16"),
+    "TB": _sb(64, "bfloat16"), "BT": _sb(512, "bfloat16"),
     "qb": _sb(128 * R, CODE), "sb": _sb(128 * R, "uint8"),
     "ql": _sb(LAND + GAP * R, CODE), "sl": _sb(LAND + GAP * R, "uint8"),
     "LE": _sb(E, "float32"), "Y": _sb(E, "float32"),
@@ -68,7 +68,7 @@ SCRATCH = {
 for _b in range(8):
     SCRATCH["ps%d" % _b] = ("psum", [128, 512], "float32")
 
-DMA_SEMS = ["ldu", "ldx", "ldz", "ldw", "lds", "ldv", "sh0", "sh1", "sh2", "oa", "oz"] + ["z%d" % _i for _i in range(14)]
+DMA_SEMS = ["ldu", "ldx", "ldz", "ldw", "lds", "ldv", "sh0", "sh1", "sh2", "oa", "oz"] + ["q%d" % _i for _i in range(14)] + ["z%d" % _i for _i in range(13)]
 SEMAPHORES = ["cv", "cs", "ct", "cg", "sent", "arr0", "arr1", "arr2"] + DMA_SEMS
 COUNTER = {"v": "cv", "s": "cs", "t": "ct", "g": "cg"}
 WIDTH = {"float32": 4, "int32": 4, "bfloat16": 2, "float16": 2, "uint16": 2, "uint8": 1, CODE: 4}
@@ -104,7 +104,7 @@ def _links(ops):
 def _time(o):
     kind, n = o["size"]
     if kind in ("v", "s"):
-        return max(64, n + CFG["ADD"]) * 0.83
+        return max(64, n + CFG["ADD"][kind]) * 0.83
     fixed, each = {"gat": (55, 1.3), "sca": (50, 3.1), "q": (12, 0.88), "pe": (10, 0.6), "g": (150, 1.66),
                    "dma": (60, 0), "far": (300, 0), "none": (0, 0)}[kind]
     return fixed + each * n
@@ -228,8 +228,7 @@ def rank_program(g, core, T, topo):
 
 def _calls(g, core, T, topo, rank):
     N = len(T.cores)
-    NV, SS, H = CFG["NV"], CFG["SS"], CFG["H"]
-    RW = 8 * NV
+    H = CFG["H"]
     pieces = ((0, H), (H, C))
     ops = []
 
@@ -311,8 +310,11 @@ def _calls(g, core, T, topo, rank):
         else:
             ts(out, a, c, ALU.mult, off=off)
 
+    fills = [0]
+
     def zero(out):
-        act(out, A("ZT", 0, len(out[4])), ACT.Copy)
+        dma("y", "z%d" % fills[0], out, A("ZT", 0, len(out[4])))
+        fills[0] += 1
 
     def mm(bank, n, ql, sl, l0, qr, sr, r0, start=True, stop=True, grp=None):
         o = A("ps%d" % bank, 0, n)
@@ -345,7 +347,6 @@ def _calls(g, core, T, topo, rank):
     def ps(bank, c0, c1, p0=0, p1=128):
         return A("ps%d" % bank, c0, c1, 1, p0, p1)
 
-    T8 = CFG["T8"]
     dma("y", "ldu", A("U"), T.u[:], chain="loads")
     dma("y", "ldx", A("X", 0, 4 * H), T.x[:, 0:4 * H], chain="loads")
     dma("y", "ldz", A("X", 4 * H, 4 * E), T.x[:, 4 * H:4 * E], chain="loads")
@@ -377,28 +378,19 @@ def _calls(g, core, T, topo, rank):
     act(col("PC", 2), col("PC", 1), ACT.Identity, 168.0)
     act(col("PC", 3), col("PC", 1), ACT.Identity, 1024.0 + 159.0)
     act(col("PC", 4), q, ACT.Identity, col("PC", 3), -1.0)
-    if T8:
-        act(col("PC", 14), q3, ACT.Identity, 0.0, 63.75)
-        act(col("PC", 15), q, ACT.Identity, col("PC", 14), 0.25)
-        act(col("PC", 5), q3, ACT.Identity, 0.0, 7.75)
-        act(col("PC", 8), q, ACT.Identity, col("PC", 5), 0.25)
-        for b in range(4):
-            zero(A("MW64", 64 * b + K, 64 * b + 64))
-    else:
-        act(col("PC", 5), q3, ACT.Identity, 0.0, -7.0)
-        act(col("PC", 6), q, ACT.Identity, col("PC", 5), 8.0)
-        act(col("PC", 7), p, ACT.Identity, col("PC", 6), 0.25)
-        act(col("PC", 8), q31, ACT.Identity, col("PC", 7), -0.25)
-        zero(A("MW64", 192, 256))
-        zero(A("MW64", 448, 512))
+    act(col("PC", 14), q3, ACT.Identity, 0.0, 63.75)
+    act(col("PC", 15), q, ACT.Identity, col("PC", 14), 0.25)
+    act(col("PC", 5), q3, ACT.Identity, 0.0, 7.75)
+    act(col("PC", 8), q, ACT.Identity, col("PC", 5), 0.25)
     act(col("PC", 9), q3, ACT.Identity, 0.0, 62.5)
     act(col("PC", 10), q, ACT.Identity, col("PC", 9), 1.5)
-    if CFG["K96"]:
+    rounds = [dict(CFG, **CFG["R"][t]) for t in range(R)]
+    if any(cf["K96"] for cf in rounds):
         act(col("PC", 11), q31, ACT.Identity, q, -1.0)
         act(col("PC", 12), col("PC", 11), ACT.Identity, float(K), -3.0)
         act(col("PC", 13), col("PC", 11), ACT.Identity, float(2 * K), 3.0)
     for m in range(3):
-        if CFG["KC"][m] == "v":
+        if any(cf["KC"][m] == "v" for cf in rounds):
             zero(A("SGX", (C + 64) * m + C, (C + 64) * (m + 1)))
     for c0, c1 in ((240, 320), (496, 544), (656, 704), (752, 800)):
         zero(A("TT", 4 * c0, 4 * c1))
@@ -408,10 +400,11 @@ def _calls(g, core, T, topo, rank):
     gaps = [("t", 896, 1024), ("t", 1024, 1088), ("t", 320, 416), ("l", 0, LAND)]
     gaps += [("l", LAND + GAP * t + 6, LAND + GAP * (t + 1)) for t in range(R)]
     for j, (n_, c0, c1) in enumerate(gaps):
-        dma("y", "z%d" % (2 * j), A("q" + n_, c0, c1), A("q0", 0, c1 - c0), raw=True, chain="loads")
-        dma("y", "z%d" % (2 * j + 1), A("s" + n_, c0, c1), A("s0", 0, c1 - c0), chain="loads")
+        dma("y", "q%d" % (2 * j), A("q" + n_, c0, c1), A("q0", 0, c1 - c0), raw=True)
+        dma("y", "q%d" % (2 * j + 1), A("s" + n_, c0, c1), A("s0", 0, c1 - c0))
     zero(A("TE"))
-    zero(col("CA", 0))
+    act(col("CA", 0), col("ZT", 0), ACT.Copy)
+    zero(A("MW64"))
     zero(A("ZW", 4 * K, 512))
     zero(A("EM", 2048, 2112))
     zero(A("BT", 32, 512))
@@ -421,19 +414,14 @@ def _calls(g, core, T, topo, rank):
     quant("qo", "so", 0, A("OD"))
     iota(A("IV"), [[1, E]], -168, 0)
     iota(A("LI", 8, 11), [[32, 3]], 0, 0)
-    iota(A("LI", 12, 16), [[0, 2], [4, 2]] if T8 else [[4, 2], [128, 2]], 0, 0)
-    iota(A("LI", 16, 28), [[4 if T8 else 16, 12]], 0, 0)
+    iota(A("LI", 16, 28), [[4, 12]], 0, 0)
     iota(A("LI", 28, 40), [[1, 6], [24, 2]], 0, 0)
     for t in range(R):
         iota(A("W", E * t + C, E * t + E), [[0, K]], 1024, 0)
-    if not CFG["K96"]:
+    if not all(cf["K96"] for cf in rounds):
         ts(A("ok", 0, 3), A("LI", 8, 11), q31, ALU.add)
-    if T8:
-        ts(A("ob", 0, 2), A("LI", 12, 14), col("PC", 8), ALU.add)
-    else:
-        ts(A("ob"), A("LI", 12, 16), col("PC", 8), ALU.add, 256.0, ALU.add)
-        ts(A("ob", 0, 4, 1, 96, 128), A("LI", 12, 16, 1, 96, 128), A("PC", 8, 9, 1, 96, 128), ALU.add)
-    ts(A("ox"), A("LI", 16, 28), col("PC", 15) if T8 else q, ALU.add)
+    ts(A("ob"), A("LI", 16, 18), col("PC", 8), ALU.add)
+    ts(A("ox"), A("LI", 16, 28), col("PC", 15), ALU.add)
     ts(A("ox", 0, 12, 1, 0, 16), A("LI", 28, 40, 1, 0, 16), A("PC", 10, 11, 1, 0, 16), ALU.add)
     for a in range(4):
         sel(A("EM", 512 * a, 512 * a + 512), A("ONE"), [[-128, 4], [-1, 32], [128, 4]], ALU.is_equal, -32 * a, 1)
@@ -460,13 +448,14 @@ def _calls(g, core, T, topo, rank):
         for h in range(8):
             mm(7, 128, "qe", "se", 128 * (h // 2) + 16 * (h % 2), "ql", "sl", c0 - 6 * h, h == 0, h == 7, grp="u%d" % t)
         for b in range(4):
-            times(CFG["UC"], A("ST", 64 * b, 64 * b + K, 1, 0, 16), ps(7, 0, K, 32 * b, 32 * b + 16), 64.0)
-        times(CFG["XG"], A("X", 4 * C, 4 * E), A("ST"), 0.015625, A("ox"))
+            times(rounds[t]["UC"], A("ST", 64 * b, 64 * b + K, 1, 0, 16), ps(7, 0, K, 32 * b, 32 * b + 16), 64.0)
+        times(rounds[t]["XG"], A("X", 4 * C, 4 * E), A("ST"), 0.015625, A("ox"))
 
     for c0, c1 in pieces:
         quant("qx", "sx", c0, A("X", 4 * c0, 4 * c1))
     for t in range(R):
-        first = t == 0
+        first, cf = t == 0, rounds[t]
+        NV, SS = cf["NV"], cf["SS"]
         row = A("W", E * t, E * t + C)
         whole = A("W", E * t, E * t + E)
         mm(4, H, "qk", "sk", 0, "qx", "sx", 0)
@@ -475,7 +464,7 @@ def _calls(g, core, T, topo, rank):
         for bank, (c0, c1) in zip((4, 0), pieces):
             tt(A("KX", c0, c1), ps(bank, c0, c1), A("AM", c0, c1), ALU.add)
             scan(A("SH", c0, c1), A("RR", c0, c1), A("KX", c0, c1), BIG, ALU.max, ALU.min)
-        for bank, (c0, c1) in (zip((4, 0), pieces) if CFG["SPLIT"] else [(0, (0, C))]):
+        for bank, (c0, c1) in (zip((4, 0), pieces) if cf["SPLIT"] else [(0, (0, C))]):
             tt(A("TT", 4 * c0, 4 * c1, 4), ps(bank, c0, c1), A("SH", c0, c1), ALU.is_ge)
             scan(A("DS", c0, c1), A("DA", c0, c1), A("TT", 4 * c0, 4 * c1, 4), 1000.0, ALU.min, ALU.add)
         if SS:
@@ -500,8 +489,8 @@ def _calls(g, core, T, topo, rank):
         quant("qt", "st", 416, A("TT", 4 * 320, 4 * 544))
         for i, (c0, n) in enumerate(((800, C), (640, 160), (0, C), (288, 128), (416, 224))):
             mm(6, n, "qo", "so", 0, "qt", "st", c0, i == 0, i == 4, grp="c%d" % t)
-        cuts = list(zip((0,) + CFG["SC"], CFG["SC"] + (18,)))
-        for c0, c1 in (cuts if CFG["CVP"] else [(0, 18)]):
+        cuts = list(zip((0,) + cf["SC"], cf["SC"] + (18,)))
+        for c0, c1 in (cuts if cf["CVP"] else [(0, 18)]):
             scan(A("CV", 16 * c0, 16 * c1), ps(6, 16 * c0, 16 * c1), A("AV", 16 * c0, 16 * c1), -1024.0, ALU.max, ALU.add)
             ts(A("ork", c0, c1), A("CV", 16 * c0 + 15, 16 * c1, 16), col("PC", 4), ALU.add)
         for c0, c1 in cuts:
@@ -520,23 +509,27 @@ def _calls(g, core, T, topo, rank):
             if e_ < K:
                 ts(A("TW", K * m + e_, K * m + K), ps(5, 80 + e_, 128), kw_, ALU.is_ge)
             scan(A("RW", K * m, K * m + K), A("TW", K * m, K * m + K), A("TE", K * m, K * m + K), 0.0, ALU.add, ALU.add)
-        for m in (2, 1, 0):
-            kw_, x0 = col("SHW", 16 * m + 15), (C + 64) * m
-            if CFG["KC"][m] == "v":
+        apart = "v" in cf["KC"][1:]
+        for m in range(3):
+            kw_, x0, b0 = col("SHW", 16 * m + 15), (C + 64) * m, (176 if apart else 32) * m
+            if cf["KC"][m] == "v":
                 ts(A("SGX", x0, x0 + C), ps(0, 0, C), kw_, ALU.is_le)
-                scan(A("BC", 32 * m, 176 + 32 * m), A("SGX", x0, x0 + C + 64, 2), A("SGX", x0 + 1, x0 + C + 64, 2),
+                scan(A("BC", b0, b0 + 176), A("SGX", x0, x0 + C + 64, 2), A("SGX", x0 + 1, x0 + C + 64, 2),
                      -144.0, ALU.add, ALU.add)
             else:
                 act(A("SGW", C * m, C * m + C), ps(1, 0, C), ACT.Sign, kw_, -1.0)
                 act(A("SGX", x0, x0 + C), A("SGW", C * m, C * m + C), ACT.Relu, None, -1.0, col("CN", m))
-                act(A("BC", 144 + 32 * m, 176 + 32 * m), A("NEG"), ACT.Identity, 144.0, col("CN", m))
-        turn(A("BD"), A("BC", 144, 240))
+                act(A("BC", b0 + 144, b0 + 176), A("NEG"), ACT.Identity, 144.0, col("CN", m))
+            if apart:
+                turn(A("BD", 32 * m, 32 * m + 32), A("BC", b0 + 144, b0 + 176))
+        if not apart:
+            turn(A("BD"), A("BC", 144, 240))
         for b in range(4):
             c0 = 0 if first else C
-            times("s" if first else CFG["PW"][b], A("P64", E * b + c0, E * b + E), A("X", 4 * c0 + b, 4 * E, 4), 64.0)
+            times(cf["PW"][b], A("P64", E * b + c0, E * b + E), A("X", 4 * c0 + b, 4 * E, 4), 64.0)
         ts(A("orb", 0, 3), A("RW", K - 1, 3 * K, K), -1.0, ALU.mult, float(K), ALU.add)
         scatter(A("B0"), A("orb", 0, 3), A("IV", C, E))
-        if CFG["K96"]:
+        if cf["K96"]:
             for h in range(2):
                 ts(A("o96", h, 6, 2), A("RW", K - 1, 3 * K, K), -1.0, ALU.mult, col("PC", 12 + h), ALU.add)
             scatter(A("KS"), A("o96"), A("BD"))
@@ -553,27 +546,18 @@ def _calls(g, core, T, topo, rank):
         scan(A("CE"), A("AE"), row, 0.0, ALU.add, ALU.max)
         ts(A("oe"), ends("CE", C), col("PC", 2), ALU.add)
         for b in range(4):
-            times(CFG["WG"][b], A("ZW", b, 4 * K, 4), A("P64", E * b, E * b + E), 0.015625, A("ow", 0, 3))
+            times(cf["WG"][b], A("ZW", b, 4 * K, 4), A("P64", E * b, E * b + E), 0.015625, A("ow", 0, 3))
         quant("qzw", "szw", 0, A("ZW"))
-        times(CFG["ZE"], A("ZW64"), A("ZW", 0, 4 * K), 64.0)
+        times(cf["ZE"], A("ZW64"), A("ZW", 0, 4 * K), 64.0)
         for b in range(4):
             mm(b, 128, "qw", "sw", 128 * b, "qzw", "szw", 0)
-            tt(A("MW64", 64 * b, 64 * b + K) if T8 else A("MW64", b, 4 * K, 4), ps(b, 0, K), A("ZW64", b, 4 * K, 4), ALU.add)
-        n = 256 if T8 else 4 * K
-        dma("y", "sh%d" % t, A("ST", 0, n, 1, 16, 128), A("MW64", 0, n, 1, 0, 112))
-        if T8:
-            for h in (1, 0):
-                for a in range(4):
-                    turn(A("TB", 16 * h, 16 * h + 32, 1, 32 * a, 32 * a + 32), A("MW64", 2 * a + h, 256, 8, 96, 128))
-            turn(A("BU"), A("TB", 16, 48))
-            times(CFG["GE"], A("BT", 0, 32), A("BU"), 0.015625, A("ob", 0, 2))
-        else:
-            for a in range(3):
-                times(CFG["QC"][a], A("MW64", 256, 256 + 4 * K, 1, 32 * a, 32 * a + 32), A("MW64", 0, 4 * K, 1, 96, 128), 1.0)
-            times(CFG["GE"], A("G"), A("MW64"), 0.015625, A("ob"))
-            turn(A("TB", 16, 48), A("G", 32, 64))
-            turn(A("TB", 0, 32), A("G", 0, 32))
-            turn(A("BT", 0, 32), A("TB", 16, 48))
+            tt(A("MW64", 64 * b, 64 * b + K), ps(b, 0, K), A("ZW64", b, 4 * K, 4), ALU.add)
+        dma("y", "sh%d" % t, A("ST", 0, 256, 1, 16, 128), A("MW64", 0, 256, 1, 0, 112))
+        for h in (1, 0):
+            for a in range(4):
+                turn(A("TB", 16 * h, 16 * h + 32, 1, 32 * a, 32 * a + 32), A("MW64", 2 * a + h, 256, 8, 96, 128))
+        turn(A("BU"), A("TB", 16, 48))
+        times(cf["GE"], A("BT", 0, 32), A("BU"), 0.015625, A("ob"))
         quant("qb", "sb", 128 * t, A("BT"))
         dst = T.cores[(rank + t + 1) % N]
         rid, pid = topo.addr(dst, core)
@@ -587,21 +571,21 @@ def _calls(g, core, T, topo, rank):
             return g.remote_dma(T.sl[:, c0:c0 + 6], T.sb[:, b0:b0 + 6], T.sem["arr%d" % t], T.sem.sent, pid, rid, mask)
 
         rec("g", ship, [], [A("qb", 128 * t, 128 * t + 6), A("sb", 128 * t, 128 * t + 6)], ("far", 0), chain="far%d" % t)
-        for h, (c0, c1) in enumerate(pieces if CFG["GP"] else [(0, C)]):
+        for h, (c0, c1) in enumerate(pieces if cf["GP"] else [(0, C)]):
             for b in range(4):
-                times(CFG["ZG"][4 * h + b], A("Z", 4 * c0 + b, 4 * c1, 4), A("P64", E * b, E * b + E), 0.015625,
+                times(cf["ZG"][4 * h + b], A("Z", 4 * c0 + b, 4 * c1, 4), A("P64", E * b, E * b + E), 0.015625,
                       A("oe", c0 // 16, c1 // 16))
         for h, (c0, c1) in enumerate(pieces):
             n = c1 - c0
             zh = A("Z", 4 * c0, 4 * c1)
             quant("qz", "sz", c0, zh)
-            times(CFG["Z6"][h], A("Z64", 4 * c0, 4 * c1), zh, 64.0)
+            times(cf["Z6"][h], A("Z64", 4 * c0, 4 * c1), zh, 64.0)
             for b in range(4):
                 mm(4 * (1 - h) + b, n, "qw", "sw", 128 * b, "qz", "sz", c0)
             for b in range(4):
                 p_ = A("P64", E * b + c0, E * b + c1)
                 tt(p_, ps(4 * (1 - h) + b, 0, n), A("Z64", 4 * c0 + b, 4 * c1, 4), ALU.add)
-                times(CFG["DN"][4 * h + b], A("X", 4 * c0 + b, 4 * c1, 4), p_, 0.015625)
+                times(cf["DN"][4 * h + b], A("X", 4 * c0 + b, 4 * c1, 4), p_, 0.015625)
             quant("qx", "sx", c0, A("X", 4 * c0, 4 * c1))
 
     act(A("LE", 0, C), A("W", E * (R - 1), E * (R - 1) + C), ACT.Identity, 168.0)

@@ -7,24 +7,22 @@ CODE = "float8_e4m3fn_x4"
 LAND, GAP = 42, 128
 CFG = {
     "NV": 13,
-    "SS": 4, "ZE": "s",
-    "H": 128,
+    "SS": 3, "ZE": "s",
+    "H": 160,
     "UC": "v",
     "XG": "s",
-    "PW": "ssss",
     "SC": (10,),
-    "WG": "ssvv",
     "GE": "s",
-    "ZG": "vvssvsss",
-    "Z6": "ss",
+    "ZG": (("s", 80), ("v", 80), ("s", 128)),
+    "Z6": "sv",
     "DN": "sssvssvv",
     "KC": "vss",
-    "R": [{}, {}, {}],
-    "K96": False, "GP": False, "CVP": True,
+    "R": [{"SS": 5}, {}, {"XG": "vs"}],
+    "K96": False, "EP": False, "CVP": True, "W4": "vs", "ZF": True, "US": "vvv", "QC": "ssvv",
     "SPLIT": True,
-    "HOP": 215, "ADD": {"v": 10, "s": 60}, "TURNS": 4000,
+    "HOP": 217, "ADD": {"v": 10, "s": 60}, "TURNS": 7000, "SLOW": 0.75, "LATE": 0.25, "SEED": 1,
 }
-FLIGHT = {"dma": 1000, "far": 1700}
+FLIGHT = {"dma": 1000, "far": 1800}
 RW = 8 * 17
 
 
@@ -33,22 +31,22 @@ def _sb(n, d):
 
 
 SCRATCH = {
-    "X": _sb(4 * E, "bfloat16"), "P64": _sb(4 * E, "bfloat16"), "Z": _sb(4 * C, "bfloat16"), "Z64": _sb(4 * C, "bfloat16"),
+    "X": _sb(4 * E, "bfloat16"), "M64": _sb(4 * C, "bfloat16"), "Z": _sb(4 * C, "bfloat16"), "Z64": _sb(4 * C, "bfloat16"),
     "ZW": _sb(512, "bfloat16"), "ZW64": _sb(4 * K, "bfloat16"), "qzw": _sb(128, CODE), "szw": _sb(128, "uint8"),
     "U": _sb(512, "bfloat16"), "V": _sb(512, "bfloat16"),
     "qu": _sb(128, CODE), "su": _sb(128, "uint8"), "qk": _sb(128, CODE), "sk": _sb(128, "uint8"),
     "qv": _sb(128, CODE), "sv": _sb(128, "uint8"), "qw": _sb(512, CODE), "sw": _sb(512, "uint8"),
-    "qx": _sb(C, CODE), "sx": _sb(C, "uint8"), "qa": _sb(128, CODE), "sa": _sb(128, "uint8"),
+    "qx": _sb(E, CODE), "sx": _sb(E, "uint8"), "qa": _sb(128, CODE), "sa": _sb(128, "uint8"),
     "qz": _sb(C, CODE), "sz": _sb(C, "uint8"),
     "ONE": _sb(512, "bfloat16"), "ZT": _sb(512, "bfloat16"), "OD1": _sb(512, "bfloat16"), "OD": _sb(512, "bfloat16"),
     "qo": _sb(128, CODE), "so": _sb(128, "uint8"), "q0": _sb(128, CODE), "s0": _sb(128, "uint8"),
     "EM": _sb(4 * 528, "bfloat16"), "qe": _sb(528, CODE), "se": _sb(528, "uint8"),
     "PI": _sb(2, "int32"), "PB": _sb(4, "int32"), "PF": _sb(4, "float32"), "PC": _sb(16, "float32"),
-    "RI": _sb(C, "bfloat16"), "AM": _sb(C, "bfloat16"), "RR": _sb(C, "bfloat16"), "AG": _sb(C, "float32"),
-    "AT": _sb(C, "float32"), "AE": _sb(C, "bfloat16"), "AV": _sb(C, "float32"), "DA": _sb(C, "bfloat16"),
+    "RI": _sb(E, "bfloat16"), "AM": _sb(E, "bfloat16"), "RR": _sb(E, "bfloat16"), "AG": _sb(64, "float32"),
+    "AT": _sb(64, "float32"), "AE": _sb(K, "bfloat16"), "AV": _sb(C, "float32"), "DA": _sb(C, "bfloat16"),
     "IV": _sb(E, "bfloat16"), "LI": _sb(40, "float32"),
     "ou": _sb(8, "uint16"), "ob": _sb(2, "uint16"), "ok": _sb(4, "uint16"), "ox": _sb(12, "uint16"),
-    "KX": _sb(C, "float32"), "SH": _sb(C, "float32"), "KXW": _sb(K, "float32"), "SHW": _sb(K, "float32"),
+    "KX": _sb(E, "float32"), "SH": _sb(E, "float32"),
     "TT": _sb(4 * 800, "bfloat16"), "qt": _sb(1088, CODE), "st": _sb(1088, "uint8"),
     "TW": _sb(3 * K, "bfloat16"), "TE": _sb(3 * K, "bfloat16"), "RW": _sb(3 * K, "bfloat16"),
     "SG": _sb(2448, "bfloat16"), "SGW": _sb(3 * C, "bfloat16"), "SGX": _sb(3 * (C + 64), "bfloat16"),
@@ -56,10 +54,12 @@ SCRATCH = {
     "RS": _sb(18 * RW, "bfloat16"), "CA": _sb(18, "float32"), "DS": _sb(C, "bfloat16"),
     "CV": _sb(C, "float32"), "ork": _sb(18, "uint16"),
     "orb": _sb(4, "uint16"), "KU": _sb(K, "float32"), "KS": _sb(2 * K, "float32"), "o96": _sb(6, "uint16"),
-    "PP": _sb(K, "float32"), "CP": _sb(K, "float32"), "op": _sb(4, "uint16"),
+    "AP": _sb(K, "bfloat16"), "CP": _sb(3 * K, "float32"), "op": _sb(4, "uint16"),
     "B0": _sb(K, "bfloat16"), "W": _sb(R * E, "bfloat16"), "WB": _sb(K, "bfloat16"),
-    "CE": _sb(C, "float16"), "oe": _sb(18, "uint16"), "CB": _sb(K, "float32"), "ow": _sb(4, "uint16"),
-    "MW64": _sb(256, "bfloat16"), "ST": _sb(256, "bfloat16"), "BU": _sb(32, "bfloat16"), "NEG": _sb(32, "bfloat16"),
+    "CE": _sb(C, "float16"), "oe": _sb(72, "uint16"), "CB": _sb(K, "float32"), "ow": _sb(12, "uint16"),
+    "MW64": _sb(256, "bfloat16"), "ST": _sb(256, "bfloat16"), "BU": _sb(64, "bfloat16"), "NEG": _sb(32, "bfloat16"),
+    "R4": _sb(K, "bfloat16"), "AG4": _sb(K, "float32"), "AT4": _sb(K, "float32"), "A4": _sb(C, "bfloat16"),
+    "PD": _sb(6, "float32"),
     "TB": _sb(64, "bfloat16"), "BT": _sb(512, "bfloat16"),
     "qb": _sb(128 * R, CODE), "sb": _sb(128 * R, "uint8"),
     "ql": _sb(LAND + GAP * R, CODE), "sl": _sb(LAND + GAP * R, "uint8"),
@@ -68,7 +68,7 @@ SCRATCH = {
 for _b in range(8):
     SCRATCH["ps%d" % _b] = ("psum", [128, 512], "float32")
 
-DMA_SEMS = ["ldu", "ldx", "ldz", "ldw", "lds", "ldv", "sh0", "sh1", "sh2", "oa", "oz"] + ["q%d" % _i for _i in range(14)] + ["z%d" % _i for _i in range(13)]
+DMA_SEMS = ["ldu", "ldx", "ldz", "ldw", "lds", "ldv", "sh0", "sh1", "sh2", "oa", "oz"] + ["q%d" % _i for _i in range(14)] + ["z%d" % _i for _i in range(24)]
 SEMAPHORES = ["cv", "cs", "ct", "cg", "sent", "arr0", "arr1", "arr2"] + DMA_SEMS
 COUNTER = {"v": "cv", "s": "cs", "t": "ct", "g": "cg"}
 WIDTH = {"float32": 4, "int32": 4, "bfloat16": 2, "float16": 2, "uint16": 2, "uint8": 1, CODE: 4}
@@ -101,27 +101,33 @@ def _links(ops):
     return needs, soft
 
 
-def _time(o):
+def _time(o, slow=False):
     kind, n = o["size"]
+    if kind == "dma" and o["q"] == "y" and slow:
+        return 150
     if kind in ("v", "s"):
-        return max(64, n + CFG["ADD"][kind]) * 0.83
-    fixed, each = {"gat": (55, 1.3), "sca": (50, 3.1), "q": (12, 0.88), "pe": (10, 0.6), "g": (150, 1.66),
-                   "dma": (60, 0), "far": (300, 0), "none": (0, 0)}[kind]
-    return fixed + each * n
+        return max(64, n + CFG["ADD"][kind]) * (1.12 if slow else 0.83)
+    fixed, each, most = {"gat": (55, 1.3, 2.1), "sca": (50, 3.1, 5.6), "q": (12, 0.88, 1.19), "pe": (10, 0.6, 0.6),
+                         "g": (150, 1.66, 2.2), "dma": (60, 0, 0), "far": (300, 0, 0), "none": (0, 0, 0)}[kind]
+    return fixed + (most if slow else each) * n
 
 
 def _place(seq, behind, hold, queue, first):
-    start, busy = [0] * len(hold), {}
+    start, busy = [0] * len(hold), {q: ([], []) for q in set(queue)}
     for i in seq:
-        at = max([first[i]] + [start[j] + d for j, d in behind[i]])
-        line = busy.setdefault(queue[i], [])
-        n = len(line)
-        while n and line[n - 1][1] > at:
+        at = first[i]
+        for j, d in behind[i]:
+            if start[j] + d > at:
+                at = start[j] + d
+        froms, tos = busy[queue[i]]
+        n = last = len(tos)
+        while n and tos[n - 1] > at:
             n -= 1
-        while n < len(line) and line[n][0] < at + hold[i]:
-            at = max(at, line[n][1])
+        while n < last and froms[n] < at + hold[i]:
+            at = tos[n]
             n += 1
-        line.insert(n, (at, at + hold[i]))
+        froms.insert(n, at)
+        tos.insert(n, at + hold[i])
         start[i] = at
     return start
 
@@ -137,37 +143,58 @@ def _order(ops):
     hold, queue = [_time(o) for o in ops], [o["q"] for o in ops]
     fly = [FLIGHT.get(o["size"][0], 0) for o in ops]
     land = [f if o["size"][0] == "dma" else 0 for o, f in zip(ops, fly)]
-    before, after = [[] for _ in ops], [[] for _ in ops]
+    before, after, above = [[] for _ in ops], [[] for _ in ops], [0] * n
     for k in range(n):
-        for j in sorted(needs[k] | soft[k]):
+        for j in sorted(needs[k] | soft[k], reverse=True):
+            if above[k] >> j & 1 and not fly[j]:
+                continue
             if j in soft[k]:
                 gap = 0 if ops[k]["fn"] else fly[j]
             else:
                 gap = land[j] + CFG["HOP"] if ops[k]["fn"] else 0
+                above[k] |= above[j] | 1 << j
             before[k].append((j, hold[j] + gap))
             after[j].append((k, hold[k] + gap))
 
     def plan(key):
-        key = list(key)
         for i in range(n):
-            key[i] = max([key[i]] + [key[j] + 0.001 for j, d in before[i]])
+            for j, d in before[i]:
+                if key[j] >= key[i]:
+                    key[i] = key[j] + 0.001
         plans = [_place(sorted(range(n), key=lambda i: key[i]), before, hold, queue, [0] * n)]
         late = _place(sorted(range(n), key=lambda i: (-plans[0][i] - hold[i], -i)), after, hold, queue, land)
         plans.append(_place(sorted(range(n), key=lambda i: (-late[i] - hold[i], i)), before, hold, queue, [0] * n))
-        return min((max(s[i] + hold[i] + land[i] for i in range(n)), s) for s in plans)
+        end, best_ = min((max(s[i] + hold[i] + land[i] for i in range(n)), s) for s in plans)
+        seq = sorted(range(n), key=lambda i: (best_[i], i))
+        return end + CFG["SLOW"] * replay(seq, slow, slow) + CFG["LATE"] * replay(seq, [0] * n, late_), best_
+
+    slow = [_time(o, True) - h for o, h in zip(ops, hold)]
+    late_ = [0.6 * f for f in fly]
+    waits = [[(j, d) for j, d in before[i] if queue[i] + queue[j] != "yy"] for i in range(n)]
+
+    def replay(seq, longer, later):
+        start, free = [0] * n, {q: 0 for q in set(queue)}
+        for i in seq:
+            at = free[queue[i]]
+            for j, d in waits[i]:
+                if start[j] + d + later[j] > at:
+                    at = start[j] + d + later[j]
+            start[i] = at
+            free[queue[i]] = at + hold[i] + longer[i]
+        return max(start[i] + hold[i] + later[i] + land[i] for i in range(n))
 
     tail = [0] * n
     for i in range(n - 1, -1, -1):
         tail[i] = max([fly[i]] + [d + tail[k] for k, d in after[i]])
-    best, seed = plan([-tail[i] - hold[i] for i in range(n)]), [1]
+    best, seed = plan([-tail[i] - hold[i] for i in range(n)]), [CFG["SEED"]]
 
     def draw():
         seed[0] = seed[0] * 16807 % 2147483647
         return seed[0] / 2147483647
 
     for turn in range(CFG["TURNS"]):
-        mid, wide, far = draw() * best[0], (500, 1500, 4000)[turn % 3], (100, 300, 800)[turn // 3 % 3]
-        best = min(best, plan([s + (far * (2 * draw() - 1) if abs(s - mid) < wide else 0) for s in best[1]]), key=lambda b: b[0])
+        mid, wide, far = draw() * max(best[1]), (500, 1500, 4000)[turn % 3], (100, 300, 800)[turn // 3 % 3]
+        best = min(plan([s + (far * (2 * draw() - 1) if abs(s - mid) < wide else 0) for s in best[1]]), best, key=lambda b: b[0])
     _ORDERS[n] = sorted(range(n), key=lambda i: (best[1][i], i))
     return _ORDERS[n]
 
@@ -316,6 +343,11 @@ def _calls(g, core, T, topo, rank):
         dma("y", "z%d" % fills[0], out, A("ZT", 0, len(out[4])))
         fills[0] += 1
 
+    def repeat(name):
+        for c0 in range(K, C, K):
+            dma("y", "z%d" % fills[0], A(name, c0, c0 + K), A(name, 0, K))
+            fills[0] += 1
+
     def mm(bank, n, ql, sl, l0, qr, sr, r0, start=True, stop=True, grp=None):
         o = A("ps%d" % bank, 0, n)
         a, b, c, d = A(ql, l0, l0 + 128), A(sl, l0, l0 + 128), A(qr, r0, r0 + n), A(sr, r0, r0 + n)
@@ -349,13 +381,13 @@ def _calls(g, core, T, topo, rank):
 
     dma("y", "ldu", A("U"), T.u[:], chain="loads")
     dma("y", "ldx", A("X", 0, 4 * H), T.x[:, 0:4 * H], chain="loads")
-    dma("y", "ldz", A("X", 4 * H, 4 * E), T.x[:, 4 * H:4 * E], chain="loads")
+    dma("s", "ldz", A("X", 4 * H, 4 * E), T.x[:, 4 * H:4 * E])
     dma("y", "ldw", A("qw"), T.wc[:], raw=True, chain="loads")
     dma("y", "lds", A("sw"), T.ws[:], chain="loads")
     dma("y", "ldv", A("V"), T.v[:], chain="loads")
     iota(col("PI", 0), [[0, 1]], 0, 1, False)
     iota(A("LI", 0, 8), [[16, 8]], 0, 0)
-    iota(A("RI"), [[0, 18], [1, 16]], 0, 0)
+    iota(A("RI"), [[0, 21], [1, 16]], 0, 0)
     iota(col("PF", 3), [[0, 1]], 0, 1)
     fill(A("ONE"), 1.0)
     for j, c in enumerate((15, 3, 31)):
@@ -364,27 +396,43 @@ def _calls(g, core, T, topo, rank):
     cp(A("PF", 0, 3), A("PB", 0, 3))
     q, q3, q31, p = (col("PF", j) for j in range(4))
     fill(A("RR"), -BIG)
-    fill(A("RR", 0, C, 16), BIG)
+    fill(A("RR", 0, E, 16), BIG)
     fill(A("ZT"), 0.0)
     act(A("NEG"), A("ONE", 0, 32), ACT.Copy, None, -1.0)
     zero(A("ST"))
     ts(A("AM"), A("RI"), q, ALU.not_equal, BIG, ALU.mult)
     act(col("PC", 0), q, ACT.Identity, 2.0)
-    act(A("AG"), A("RI"), ACT.Relu, col("PC", 0), -1.0)
+    act(A("AG"), A("RI", 0, 64), ACT.Relu, col("PC", 0), -1.0)
     act(A("AT"), A("AG"), ACT.Square, -24.0, 32.0)
-    act(A("AE"), A("AT"), ACT.Identity, 576.0, -1.0)
-    act(A("AV", 0, C - 1), A("AT", 1, C), ACT.Identity, 576.0, -1.0)
+    act(A("AV", 0, K), A("AT", 1, K + 1), ACT.Identity, 576.0, -1.0)
+    repeat("AV")
+    act(A("AE", 0, 16), A("AT", 0, 16), ACT.Relu, 576.0, -1.0)
+    act(A("AE", 16, 32), A("AG", 0, 16), ACT.Relu, -1.0)
+    act(A("AE", 32, 48), A("AE", 16, 32), ACT.Sign)
+    act(A("AP", 0, 32), A("ONE", 0, 32), ACT.Copy)
+    tt(A("AP", 32, K), A("AE", 0, 16), A("AE", 32, 48), ALU.add)
     ts(col("PC", 1), q, 15.0, ALU.is_lt, -512.0, ALU.mult)
-    act(col("PC", 2), col("PC", 1), ACT.Identity, 168.0)
     act(col("PC", 3), col("PC", 1), ACT.Identity, 1024.0 + 159.0)
     act(col("PC", 4), q, ACT.Identity, col("PC", 3), -1.0)
     act(col("PC", 14), q3, ACT.Identity, 0.0, 63.75)
     act(col("PC", 15), q, ACT.Identity, col("PC", 14), 0.25)
     act(col("PC", 5), q3, ACT.Identity, 0.0, 7.75)
-    act(col("PC", 8), q, ACT.Identity, col("PC", 5), 0.25)
+    act(col("PC", 6), q, ACT.Identity, col("PC", 5), -1.75)
+    act(col("PC", 8), q31, ACT.Identity, col("PC", 6), 2.0)
+    zero(A("TB", 32, 64))
     act(col("PC", 9), q3, ACT.Identity, 0.0, 62.5)
     act(col("PC", 10), q, ACT.Identity, col("PC", 9), 1.5)
     rounds = [dict(CFG, **CFG["R"][t]) for t in range(R)]
+    iota(A("R4"), [[0, 12], [1, 4]], 0, 0)
+    act(col("PD", 0), q3, ACT.Identity, 2.0, -0.25)
+    act(col("PD", 1), q, ACT.Identity, col("PD", 0), 0.25)
+    act(A("AG4"), A("R4"), ACT.Relu, col("PD", 1), -1.0)
+    act(A("AT4"), A("AG4"), ACT.Square, -24.0, 32.0)
+    act(A("A4", 0, K), A("AT4"), ACT.Identity, 576.0, -1.0)
+    repeat("A4")
+    ts(col("PD", 2), q, 12.0, ALU.is_lt, -2048.0, ALU.mult)
+    act(col("PD", 3), q3, ACT.Identity, col("PD", 2))
+    act(col("PD", 4), col("PD", 3), ACT.Identity, 4.0 * 168)
     if any(cf["K96"] for cf in rounds):
         act(col("PC", 11), q31, ACT.Identity, q, -1.0)
         act(col("PC", 12), col("PC", 11), ACT.Identity, float(K), -3.0)
@@ -425,8 +473,8 @@ def _calls(g, core, T, topo, rank):
     ts(A("ox", 0, 12, 1, 0, 16), A("LI", 28, 40, 1, 0, 16), A("PC", 10, 11, 1, 0, 16), ALU.add)
     for a in range(4):
         sel(A("EM", 512 * a, 512 * a + 512), A("ONE"), [[-128, 4], [-1, 32], [128, 4]], ALU.is_equal, -32 * a, 1)
-    quant("qe", "se", 0, A("EM", 0, 1056))
-    quant("qe", "se", 264, A("EM", 1056, 2112))
+    for a in range(4):
+        quant("qe", "se", 132 * a, A("EM", 528 * a, 528 * a + 528))
     quant("qv", "sv", 0, A("V"))
 
     base = {}
@@ -449,19 +497,23 @@ def _calls(g, core, T, topo, rank):
             mm(7, 128, "qe", "se", 128 * (h // 2) + 16 * (h % 2), "ql", "sl", c0 - 6 * h, h == 0, h == 7, grp="u%d" % t)
         for b in range(4):
             times(rounds[t]["UC"], A("ST", 64 * b, 64 * b + K, 1, 0, 16), ps(7, 0, K, 32 * b, 32 * b + 16), 64.0)
-        times(rounds[t]["XG"], A("X", 4 * C, 4 * E), A("ST"), 0.015625, A("ox"))
+        n = len(rounds[t]["XG"])
+        for h in range(n):
+            times(rounds[t]["XG"][h], A("X", 4 * C + 192 // n * h, 4 * C + 192 // n * (h + 1)), A("ST"), 0.015625,
+                  A("ox", 12 // n * h, 12 // n * (h + 1)))
 
-    for c0, c1 in pieces:
+    for c0, c1 in ((0, H), (H, E)):
         quant("qx", "sx", c0, A("X", 4 * c0, 4 * c1))
     for t in range(R):
         first, cf = t == 0, rounds[t]
         NV, SS = cf["NV"], cf["SS"]
         row = A("W", E * t, E * t + C)
         whole = A("W", E * t, E * t + E)
+        known = E if first else C
         mm(4, H, "qk", "sk", 0, "qx", "sx", 0)
-        mm(0, C, "qk", "sk", 0, "qx", "sx", 0)
+        mm(0, known, "qk", "sk", 0, "qx", "sx", 0)
         mm(1, C, "qk", "sk", 0, "qx", "sx", 0)
-        for bank, (c0, c1) in zip((4, 0), pieces):
+        for bank, (c0, c1) in zip((4, 0), ((0, H), (H, known))):
             tt(A("KX", c0, c1), ps(bank, c0, c1), A("AM", c0, c1), ALU.add)
             scan(A("SH", c0, c1), A("RR", c0, c1), A("KX", c0, c1), BIG, ALU.max, ALU.min)
         for bank, (c0, c1) in (zip((4, 0), pieces) if cf["SPLIT"] else [(0, (0, C))]):
@@ -481,9 +533,15 @@ def _calls(g, core, T, topo, rank):
                 act(sg, ps(6 if 16 * m < H else 1, 0, 16 * m), ACT.Sign, key(m), -1.0)
                 act(slot(m), sg, ACT.Relu, None, -1.0, col("CA", m))
         for m0, m1 in ((0, SS + 1), (NV + 1, 18)):
-            if m1 > max(m0, 1):
+            if cf["US"][m0 > 0] == "s":
+                for m in range(m0, m1):
+                    act(col("RS", RW * m + RW - 1), col("CA", m), ACT.Identity, col("DS", 16 * m + 15))
+            elif m1 > max(m0, 1):
                 tt(A("RS", RW * (m0 + 1) - 1, RW * m1, RW), A("DS", 16 * m0 + 15, 16 * m1, 16), A("CA", m0, m1), ALU.add)
-        ts(ends("AV", C), A("RS", RW - 1, 18 * RW, RW), -1.0, ALU.mult, -1024.0, ALU.add)
+        if cf["US"][2] == "s":
+            act(ends("AV", C), A("RS", RW - 1, 18 * RW, RW), ACT.Identity, -1024.0, -1.0)
+        else:
+            ts(ends("AV", C), A("RS", RW - 1, 18 * RW, RW), -1.0, ALU.mult, -1024.0, ALU.add)
         quant("qt", "st", 640, A("TT", 4 * 544, 4 * 800))
         quant("qt", "st", 0, A("TT", 0, 4 * 320))
         quant("qt", "st", 416, A("TT", 4 * 320, 4 * 544))
@@ -495,23 +553,24 @@ def _calls(g, core, T, topo, rank):
             ts(A("ork", c0, c1), A("CV", 16 * c0 + 15, 16 * c1, 16), col("PC", 4), ALU.add)
         for c0, c1 in cuts:
             scatter(row, A("ork", c0, c1), A("IV", 16 * c0, 16 * c1))
+        bank, w0 = (0, C) if first else (5, 80)
         if not first:
             unpack(t - 1)
-        quant("qa", "sa", 0, A("X", 4 * (E - 128), 4 * E))
-        mm(5, 128, "qk", "sk", 0, "qa", "sa", 0)
-        tt(A("KXW"), ps(5, 80, 128), A("AM", 0, K), ALU.add)
-        scan(A("SHW"), A("RR", 0, K), A("KXW"), BIG, ALU.max, ALU.min)
-        tt(A("TE", 0, 3 * K, 3), ps(5, 80, 128), A("SHW"), ALU.is_equal)
+            quant("qa", "sa", 0, A("X", 4 * (E - 128), 4 * E))
+            mm(5, 128, "qk", "sk", 0, "qa", "sa", 0)
+            tt(A("KX", C, E), ps(5, 80, 128), A("AM", 0, K), ALU.add)
+            scan(A("SH", C, E), A("RR", 0, K), A("KX", C, E), BIG, ALU.max, ALU.min)
+        tt(A("TE", 0, 3 * K, 3), ps(bank, w0, w0 + K), A("SH", C, E), ALU.is_equal)
         for m in range(3):
             e_ = 16 * m + 16
-            kw_ = col("SHW", e_ - 1)
-            ts(A("TW", K * m, K * m + e_), ps(5, 80, 80 + e_), kw_, ALU.is_gt)
+            kw_ = key(18 + m)
+            ts(A("TW", K * m, K * m + e_), ps(bank, w0, w0 + e_), kw_, ALU.is_gt)
             if e_ < K:
-                ts(A("TW", K * m + e_, K * m + K), ps(5, 80 + e_, 128), kw_, ALU.is_ge)
+                ts(A("TW", K * m + e_, K * m + K), ps(bank, w0 + e_, w0 + K), kw_, ALU.is_ge)
             scan(A("RW", K * m, K * m + K), A("TW", K * m, K * m + K), A("TE", K * m, K * m + K), 0.0, ALU.add, ALU.add)
         apart = "v" in cf["KC"][1:]
         for m in range(3):
-            kw_, x0, b0 = col("SHW", 16 * m + 15), (C + 64) * m, (176 if apart else 32) * m
+            kw_, x0, b0 = key(18 + m), (C + 64) * m, (176 if apart else 32) * m
             if cf["KC"][m] == "v":
                 ts(A("SGX", x0, x0 + C), ps(0, 0, C), kw_, ALU.is_le)
                 scan(A("BC", b0, b0 + 176), A("SGX", x0, x0 + C + 64, 2), A("SGX", x0 + 1, x0 + C + 64, 2),
@@ -524,9 +583,6 @@ def _calls(g, core, T, topo, rank):
                 turn(A("BD", 32 * m, 32 * m + 32), A("BC", b0 + 144, b0 + 176))
         if not apart:
             turn(A("BD"), A("BC", 144, 240))
-        for b in range(4):
-            c0 = 0 if first else C
-            times(cf["PW"][b], A("P64", E * b + c0, E * b + E), A("X", 4 * c0 + b, 4 * E, 4), 64.0)
         ts(A("orb", 0, 3), A("RW", K - 1, 3 * K, K), -1.0, ALU.mult, float(K), ALU.add)
         scatter(A("B0"), A("orb", 0, 3), A("IV", C, E))
         if cf["K96"]:
@@ -536,27 +592,30 @@ def _calls(g, core, T, topo, rank):
         else:
             act(A("KU"), A("BD"), ACT.Copy, off=A("ok", 0, 3))
             scatter(A("KS", 0, K), A("orb", 0, 3), A("KU"))
-        scan(A("PP"), A("ONE", 0, K), A("KS", 0, K), -145.0, ALU.add, ALU.max)
-        scan(A("CP"), A("AE", 0, K), A("PP"), 0.0, ALU.add, ALU.max)
-        ts(A("op", 0, 3), ends("CP", K), col("PC", 1), ALU.add, 144.0, ALU.add)
+        for m in range(3):
+            n = 16 * m + 16
+            scan(A("CP", K * m + K - n, K * m + K), A("AP", K - n, K), A("KS", 0, n), -145.0, ALU.add, ALU.max)
+        ts(A("op", 0, 3), A("CP", K - 1, 3 * K, K), col("PC", 1), ALU.add, 144.0, ALU.add)
         tt(A("WB"), whole, A("B0"), ALU.min, off=A("op", 0, 3))
         scatter(whole, A("op", 0, 3), A("B0"))
-        scan(A("CB"), A("AE", 0, K), A("WB"), 0.0, ALU.add, ALU.max)
-        ts(A("ow", 0, 3), ends("CB", K), col("PC", 2), ALU.add)
-        scan(A("CE"), A("AE"), row, 0.0, ALU.add, ALU.max)
-        ts(A("oe"), ends("CE", C), col("PC", 2), ALU.add)
-        for b in range(4):
-            times(cf["WG"][b], A("ZW", b, 4 * K, 4), A("P64", E * b, E * b + E), 0.015625, A("ow", 0, 3))
+        for c0, c1 in (pieces if cf["EP"] else [(0, C)]):
+            scan(A("CE", c0, c1), A("A4", c0, c1), A("W", E * t + c0, E * t + c1), 0.0, ALU.add, ALU.max)
+            ts(A("oe", c0 // 4, c1 // 4), A("CE", c0 + 3, c1, 4), 4.0, ALU.mult, col("PD", 4), ALU.add)
+        scan(A("CB"), A("A4", 0, K), A("WB"), 0.0, ALU.add, ALU.max)
+        ts(A("ow"), A("CB", 3, K, 4), 4.0, ALU.mult, col("PD", 4), ALU.add)
+        n = len(cf["W4"])
+        for h in range(n):
+            times(cf["W4"][h], A("ZW", 192 // n * h, 192 // n * (h + 1)), A("X"), 1.0, A("ow", 12 // n * h, 12 // n * (h + 1)))
         quant("qzw", "szw", 0, A("ZW"))
         times(cf["ZE"], A("ZW64"), A("ZW", 0, 4 * K), 64.0)
         for b in range(4):
             mm(b, 128, "qw", "sw", 128 * b, "qzw", "szw", 0)
             tt(A("MW64", 64 * b, 64 * b + K), ps(b, 0, K), A("ZW64", b, 4 * K, 4), ALU.add)
         dma("y", "sh%d" % t, A("ST", 0, 256, 1, 16, 128), A("MW64", 0, 256, 1, 0, 112))
-        for h in (1, 0):
-            for a in range(4):
-                turn(A("TB", 16 * h, 16 * h + 32, 1, 32 * a, 32 * a + 32), A("MW64", 2 * a + h, 256, 8, 96, 128))
-        turn(A("BU"), A("TB", 16, 48))
+        for a in range(4):
+            turn(A("TB", 0, 32, 1, 32 * a, 32 * a + 32), A("MW64", 2 * a, 256, 8, 96, 128))
+            times(cf["QC"][a], A("BU", 32, 64, 1, 32 * a, 32 * a + 32), A("MW64", 2 * a + 1, 256, 8, 96, 128), 1.0)
+        turn(A("BU", 0, 32), A("TB", 16, 48))
         times(cf["GE"], A("BT", 0, 32), A("BU"), 0.015625, A("ob"))
         quant("qb", "sb", 128 * t, A("BT"))
         dst = T.cores[(rank + t + 1) % N]
@@ -571,19 +630,23 @@ def _calls(g, core, T, topo, rank):
             return g.remote_dma(T.sl[:, c0:c0 + 6], T.sb[:, b0:b0 + 6], T.sem["arr%d" % t], T.sem.sent, pid, rid, mask)
 
         rec("g", ship, [], [A("qb", 128 * t, 128 * t + 6), A("sb", 128 * t, 128 * t + 6)], ("far", 0), chain="far%d" % t)
-        for h, (c0, c1) in enumerate(pieces if cf["GP"] else [(0, C)]):
-            for b in range(4):
-                times(cf["ZG"][4 * h + b], A("Z", 4 * c0 + b, 4 * c1, 4), A("P64", E * b, E * b + E), 0.015625,
-                      A("oe", c0 // 16, c1 // 16))
+        c0 = 0
+        for on, n in cf["ZG"]:
+            times(on, A("Z", 4 * c0, 4 * (c0 + n)), A("X"), 1.0, A("oe", c0 // 4, (c0 + n) // 4))
+            c0 += n
         for h, (c0, c1) in enumerate(pieces):
             n = c1 - c0
             zh = A("Z", 4 * c0, 4 * c1)
             quant("qz", "sz", c0, zh)
-            times(cf["Z6"][h], A("Z64", 4 * c0, 4 * c1), zh, 64.0)
+            if cf["Z6"][h] == "s":
+                for b in range(4):
+                    times(cf["Z6"][h], A("Z64", 4 * c0 + b, 4 * c1, 4), A("Z", 4 * c0 + b, 4 * c1, 4), 64.0)
+            else:
+                times(cf["Z6"][h], A("Z64", 4 * c0, 4 * c1), zh, 64.0)
             for b in range(4):
                 mm(4 * (1 - h) + b, n, "qw", "sw", 128 * b, "qz", "sz", c0)
             for b in range(4):
-                p_ = A("P64", E * b + c0, E * b + c1)
+                p_ = A("M64", C * b + c0, C * b + c1)
                 tt(p_, ps(4 * (1 - h) + b, 0, n), A("Z64", 4 * c0 + b, 4 * c1, 4), ALU.add)
                 times(cf["DN"][4 * h + b], A("X", 4 * c0 + b, 4 * c1, 4), p_, 0.015625)
             quant("qx", "sx", c0, A("X", 4 * c0, 4 * c1))

from concourse.mybir import dt, AluOpType, ActivationFunctionType

ALU, ACT = AluOpType, ActivationFunctionType
C, K, E, R = 288, 48, 336, 3
BIG = 2.0e29
CODE = "float8_e4m3fn_x4"
LAND, GAP = 42, 128
CFG = {
    "NV": 13,
    "SS": 3, "ZE": "s",
    "H": 160,
    "UC": "v",
    "XG": "s",
    "SC": (10,),
    "GE": "s",
    "ZG": (("s", 80), ("v", 80), ("s", 128)),
    "Z6": "sv",
    "DN": "sssvssvv",
    "KC": "vss",
    "R": [{"SS": 5}, {}, {"XG": "vs"}],
    "K96": False, "EP": False, "CVP": True, "W4": "vs", "ZF": True, "US": "vvv", "QC": "ssvv",
    "SPLIT": True,
    "HOP": 217, "ADD": {"v": 10, "s": 60}, "TURNS": 7000, "SLOW": 0.75, "LATE": 0.25, "SEED": 1,
}
FLIGHT = {"dma": 1000, "far": 1800}
RW = 8 * 17


def _sb(n, d):
    return ("sbuf", [128, n], d)


SCRATCH = {
    "X": _sb(4 * E, "bfloat16"), "M64": _sb(4 * C, "bfloat16"), "Z": _sb(4 * C, "bfloat16"), "Z64": _sb(4 * C, "bfloat16"),
    "ZW": _sb(512, "bfloat16"), "ZW64": _sb(4 * K, "bfloat16"), "qzw": _sb(128, CODE), "szw": _sb(128, "uint8"),
    "U": _sb(512, "bfloat16"), "V": _sb(512, "bfloat16"),
    "qu": _sb(128, CODE), "su": _sb(128, "uint8"), "qk": _sb(128, CODE), "sk": _sb(128, "uint8"),
    "qv": _sb(128, CODE), "sv": _sb(128, "uint8"), "qw": _sb(512, CODE), "sw": _sb(512, "uint8"),
    "qx": _sb(E, CODE), "sx": _sb(E, "uint8"), "qa": _sb(128, CODE), "sa": _sb(128, "uint8"),
    "qz": _sb(C, CODE), "sz": _sb(C, "uint8"),
    "ONE": _sb(512, "bfloat16"), "ZT": _sb(512, "bfloat16"), "OD1": _sb(512, "bfloat16"), "OD": _sb(512, "bfloat16"),
    "qo": _sb(128, CODE), "so": _sb(128, "uint8"), "q0": _sb(128, CODE), "s0": _sb(128, "uint8"),
    "EM": _sb(4 * 528, "bfloat16"), "qe": _sb(528, CODE), "se": _sb(528, "uint8"),
    "PI": _sb(2, "int32"), "PB": _sb(4, "int32"), "PF": _sb(4, "float32"), "PC": _sb(16, "float32"),
    "RI": _sb(E, "bfloat16"), "AM": _sb(E, "bfloat16"), "RR": _sb(E, "bfloat16"), "AG": _sb(64, "float32"),
    "AT": _sb(64, "float32"), "AE": _sb(K, "bfloat16"), "AV": _sb(C, "float32"), "DA": _sb(C, "bfloat16"),
    "IV": _sb(E, "bfloat16"), "LI": _sb(40, "float32"),
    "ou": _sb(8, "uint16"), "ob": _sb(2, "uint16"), "ok": _sb(4, "uint16"), "ox": _sb(12, "uint16"),
    "KX": _sb(E, "float32"), "SH": _sb(E, "float32"),
    "TT": _sb(4 * 800, "bfloat16"), "qt": _sb(1088, CODE), "st": _sb(1088, "uint8"),
    "TW": _sb(3 * K, "bfloat16"), "TE": _sb(3 * K, "bfloat16"), "RW": _sb(3 * K, "bfloat16"),
    "SG": _sb(2448, "bfloat16"), "SGW": _sb(3 * C, "bfloat16"), "SGX": _sb(3 * (C + 64), "bfloat16"),
    "CN": _sb(4, "float32"), "BC": _sb(3 * 176, "bfloat16"), "BD": _sb(96, "bfloat16"),
    "RS": _sb(18 * RW, "bfloat16"), "CA": _sb(18, "float32"), "DS": _sb(C, "bfloat16"),
    "CV": _sb(C, "float32"), "ork": _sb(18, "uint16"),
    "orb": _sb(4, "uint16"), "KU": _sb(K, "float32"), "KS": _sb(2 * K, "float32"), "o96": _sb(6, "uint16"),
    "AP": _sb(K, "bfloat16"), "CP": _sb(3 * K, "float32"), "op": _sb(4, "uint16"),
    "B0": _sb(K, "bfloat16"), "W": _sb(R * E, "bfloat16"), "WB": _sb(K, "bfloat16"),
    "CE": _sb(C, "float16"), "oe": _sb(72, "uint16"), "CB": _sb(K, "float32"), "ow": _sb(12, "uint16"),
    "MW64": _sb(256, "bfloat16"), "ST": _sb(256, "bfloat16"), "BU": _sb(64, "bfloat16"), "NEG": _sb(32, "bfloat16"),
    "R4": _sb(K, "bfloat16"), "AG4": _sb(K, "float32"), "AT4": _sb(K, "float32"), "A4": _sb(C, "bfloat16"),
    "PD": _sb(6, "float32"),
    "TB": _sb(64, "bfloat16"), "BT": _sb(512, "bfloat16"),
    "qb": _sb(128 * R, CODE), "sb": _sb(128 * R, "uint8"),
    "ql": _sb(LAND + GAP * R, CODE), "sl": _sb(LAND + GAP * R, "uint8"),
    "LE": _sb(E, "float32"), "Y": _sb(E, "float32"),
}
for _b in range(8):
    SCRATCH["ps%d" % _b] = ("psum", [128, 512], "float32")

DMA_SEMS = ["ldu", "ldx", "ldz", "ldw", "lds", "ldv", "sh0", "sh1", "sh2", "oa", "oz"] + ["q%d" % _i for _i in range(14)] + ["z%d" % _i for _i in range(24)]
SEMAPHORES = ["cv", "cs", "ct", "cg", "sent", "arr0", "arr1", "arr2"] + DMA_SEMS
COUNTER = {"v": "cv", "s": "cs", "t": "ct", "g": "cg"}
WIDTH = {"float32": 4, "int32": 4, "bfloat16": 2, "float16": 2, "uint16": 2, "uint8": 1, CODE: 4}


def _clash(a, b):
    if a[0].startswith("ps"):
        if a[6] is not None and a[6] == b[6]:
            return False
        return a[5] != b[5] or a[4] or b[4]
    if not (a[4] or b[4]) or a[2] <= b[1] or b[2] <= a[1]:
        return False
    return not a[3].isdisjoint(b[3])


def _links(ops):
    seen, needs, soft, prev = {}, [], [], {}
    for i, o in enumerate(ops):
        hard, order = set(), set()
        for a in o["acc"]:
            hard.update(j for j, b in seen.get(a[0], []) if _clash(a, b))
        for a in o["acc"]:
            seen.setdefault(a[0], []).append((i, a))
        if o["chain"] is not None:
            if o["chain"] in prev:
                order.add(prev[o["chain"]])
            prev[o["chain"]] = i
        needs.append(hard)
        soft.append(order - hard)
    return needs, soft


def _time(o, slow=False):
    kind, n = o["size"]
    if kind == "dma" and o["q"] == "y" and slow:
        return 150
    if kind in ("v", "s"):
        return max(64, n + CFG["ADD"][kind]) * (1.12 if slow else 0.83)
    fixed, each, most = {"gat": (55, 1.3, 2.1), "sca": (50, 3.1, 5.6), "q": (12, 0.88, 1.19), "pe": (10, 0.6, 0.6),
                         "g": (150, 1.66, 2.2), "dma": (60, 0, 0), "far": (300, 0, 0), "none": (0, 0, 0)}[kind]
    return fixed + (most if slow else each) * n


def _place(seq, behind, hold, queue, first):
    start, busy = [0] * len(hold), {q: ([], []) for q in set(queue)}
    for i in seq:
        at = first[i]
        for j, d in behind[i]:
            if start[j] + d > at:
                at = start[j] + d
        froms, tos = busy[queue[i]]
        n = last = len(tos)
        while n and tos[n - 1] > at:
            n -= 1
        while n < last and froms[n] < at + hold[i]:
            at = tos[n]
            n += 1
        froms.insert(n, at)
        tos.insert(n, at + hold[i])
        start[i] = at
    return start


_ORDERS = {}


def _order(ops):
    n = len(ops)
    if n in _ORDERS:
        return _ORDERS[n]
    needs, soft = _links(ops)
    hold, queue = [_time(o) for o in ops], [o["q"] for o in ops]
    fly = [FLIGHT.get(o["size"][0], 0) for o in ops]
    land = [f if o["size"][0] == "dma" else 0 for o, f in zip(ops, fly)]
    before, after, above = [[] for _ in ops], [[] for _ in ops], [0] * n
    for k in range(n):
        for j in sorted(needs[k] | soft[k], reverse=True):
            if above[k] >> j & 1 and not fly[j]:
                continue
            if j in soft[k]:
                gap = 0 if ops[k]["fn"] else fly[j]
            else:
                gap = land[j] + CFG["HOP"] if ops[k]["fn"] else 0
                above[k] |= above[j] | 1 << j
            before[k].append((j, hold[j] + gap))
            after[j].append((k, hold[k] + gap))

    def plan(key):
        for i in range(n):
            for j, d in before[i]:
                if key[j] >= key[i]:
                    key[i] = key[j] + 0.001
        plans = [_place(sorted(range(n), key=lambda i: key[i]), before, hold, queue, [0] * n)]
        late = _place(sorted(range(n), key=lambda i: (-plans[0][i] - hold[i], -i)), after, hold, queue, land)
        plans.append(_place(sorted(range(n), key=lambda i: (-late[i] - hold[i], i)), before, hold, queue, [0] * n))
        end, best_ = min((max(s[i] + hold[i] + land[i] for i in range(n)), s) for s in plans)
        seq = sorted(range(n), key=lambda i: (best_[i], i))
        return end + CFG["SLOW"] * replay(seq, slow, slow) + CFG["LATE"] * replay(seq, [0] * n, late_), best_

    slow = [_time(o, True) - h for o, h in zip(ops, hold)]
    late_ = [0.6 * f for f in fly]
    waits = [[(j, d) for j, d in before[i] if queue[i] + queue[j] != "yy"] for i in range(n)]

    def replay(seq, longer, later):
        start, free = [0] * n, {q: 0 for q in set(queue)}
        for i in seq:
            at = free[queue[i]]
            for j, d in waits[i]:
                if start[j] + d + later[j] > at:
                    at = start[j] + d + later[j]
            start[i] = at
            free[queue[i]] = at + hold[i] + longer[i]
        return max(start[i] + hold[i] + later[i] + land[i] for i in range(n))

    tail = [0] * n
    for i in range(n - 1, -1, -1):
        tail[i] = max([fly[i]] + [d + tail[k] for k, d in after[i]])
    best, seed = plan([-tail[i] - hold[i] for i in range(n)]), [CFG["SEED"]]

    def draw():
        seed[0] = seed[0] * 16807 % 2147483647
        return seed[0] / 2147483647

    for turn in range(CFG["TURNS"]):
        mid, wide, far = draw() * max(best[1]), (500, 1500, 4000)[turn % 3], (100, 300, 800)[turn // 3 % 3]
        best = min(plan([s + (far * (2 * draw() - 1) if abs(s - mid) < wide else 0) for s in best[1]]), best, key=lambda b: b[0])
    _ORDERS[n] = sorted(range(n), key=lambda i: (best[1][i], i))
    return _ORDERS[n]


def _emit(g, T, ops):
    eng = {"v": g.vector, "s": g.scalar, "t": g.tensor, "g": g, "y": g.sync}
    known, clock, waits, batch = {q: {} for q in list(eng) + ["x"]}, [], [], {}
    for i, o in enumerate(ops):
        if o["sem"]:
            batch.setdefault(o["sem"], []).append(i)
    for i, (o, nd) in enumerate(zip(ops, _links(ops)[0])):
        need = {}
        for j in nd:
            key = ops[j]["sem"] or ops[j]["q"]
            assert not ops[j]["sem"] or len(batch[key]) == 1
            need[key] = max(need.get(key, -1), j)
        kn, w = known[o["q"]], []
        for key, j in sorted(need.items(), key=lambda kv: -kv[1]):
            if kn.get(key, -1) >= j:
                continue
            w.append(j)
            kn[key] = j
            for k2, j2 in clock[j].items():
                kn[k2] = max(kn.get(k2, -1), j2)
        waits.append(w)
        clock.append(dict(kn))
    marked = set(j for w in waits for j in w)
    count, value = {}, {}
    for i, o in enumerate(ops):
        if o["sem"]:
            value[i] = o["full"] or 16 * len(batch[o["sem"]])
        elif i in marked:
            count[o["q"]] = count.get(o["q"], 0) + 1
            value[i] = count[o["q"]]
    for i, o in enumerate(ops):
        for j in waits[i]:
            eng[o["q"]].wait_ge(T.sem[ops[j]["sem"] or COUNTER[ops[j]["q"]]], value[j])
        if o["fn"] is None:
            continue
        ins = o["fn"]()
        if o["sem"]:
            ins.then_inc(T.sem[o["sem"]], 16)
        elif i in marked:
            ins.then_inc(T.sem[COUNTER[o["q"]]], 1)
    for key, members in batch.items():
        if members[-1] not in marked:
            eng[ops[members[-1]]["q"]].wait_ge(T.sem[key], value[members[-1]])


def rank_program(g, core, T, topo):
    rank = T.rank_of(core)
    if rank is None:
        return
    ops = _calls(g, core, T, topo, rank)
    _emit(g, T, [ops[i] for i in _order(ops)])
    g.wait_ge(T.sem.sent, 16 * R)


def _calls(g, core, T, topo, rank):
    N = len(T.cores)
    H = CFG["H"]
    pieces = ((0, H), (H, C))
    ops = []

    def A(name, c0=0, c1=None, step=1, p0=0, p1=128):
        if c1 is None:
            c1 = SCRATCH[name][1][1]
        ap = T[name][p0:p1, c0:c1] if step == 1 else T[name][p0:p1, c0:c1:step]
        return (ap, name, p0, p1, frozenset(range(c0, c1, step)))

    def rec(q, fn, outs, ins, size, sem=None, full=0, grp=None, chain=None):
        acc = [(a[1], a[2], a[3], a[4], True, q, grp) for a in outs]
        acc += [(a[1], a[2], a[3], a[4], False, q, None) for a in ins if isinstance(a, tuple)]
        ops.append({"q": q, "fn": fn, "acc": acc, "sem": sem, "full": full, "size": size, "chain": chain or grp})

    def val(a):
        return a[0] if isinstance(a, tuple) else a

    def span(out, ins, rate=None, off=None, q="v"):
        if off is not None:
            return ("gat", 16 * len(off[4]))
        if rate is None:
            rate = 0.5 if all(WIDTH[SCRATCH[z[1]][2]] == 2 for z in [out] + ins) else 1.0
        return (q, len(ins[0][4]) * rate)

    def ts(out, a, s1, op0, s2=None, op1=None, off=None):
        src = a[0] if off is None else a[0].indirect(off[0])
        if op1 is None:
            rec("v", lambda: g.vector.tensor_scalar(out[0], src, val(s1), None, op0), [out], [a, s1, off], span(out, [a], None, off))
        else:
            rec("v", lambda: g.vector.tensor_scalar(out[0], src, val(s1), val(s2), op0, op1), [out], [a, s1, s2, off], span(out, [a], None, off))

    def tt(out, a, b, op, off=None):
        src = a[0] if off is None else a[0].indirect(off[0])
        rec("v", lambda: g.vector.tensor_tensor(out[0], src, b[0], op), [out], [a, b, off],
            span(out, [a], 1.0 if a[1].startswith("ps") else 2.0, off))

    def cp(out, a):
        rec("v", lambda: g.vector.tensor_copy(out[0], a[0]), [out], [a], span(out, [a]))

    def scatter(win, off, a):
        rec("v", lambda: g.vector.tensor_copy(win[0].indirect(off[0]), a[0]), [win], [a, off], ("sca", len(a[4])))

    def scan(out, d0, d1, init, op0, op1):
        rec("v", lambda: g.vector.tensor_tensor_scan(out[0], d0[0], d1[0], val(init), op0, op1), [out], [d0, d1, init],
            span(out, [d0, d1]))

    def turn(out, a):
        rec("v", lambda: g.vector.transpose(out[0], a[0]), [out], [a], span(out, [a]))

    def fill(out, c):
        rec("v", lambda: g.vector.memset(out[0], c), [out], [], span(out, [out]))

    def quant(qn, sn, c0, a):
        n = len(a[4]) // 4
        q, s = A(qn, c0, c0 + n), A(sn, c0, c0 + n)
        rec("v", lambda: g.vector.quantize_mx(q[0], s[0], a[0]), [q, s], [a], ("q", n))

    def pick(qo, so, n, qi, si, nw, off):
        a, b, c, d = A(qo, 0, n), A(so, 0, n), A(qi, 0, nw), A(si, 0, nw)
        rec("v", lambda: g.vector.tensor_copy(a[0].bitcast(dt.uint32), c[0].bitcast(dt.uint32).indirect(off[0])), [a], [c, off],
            span(a, [c], None, off))
        rec("s", lambda: g.scalar.activation(b[0], d[0].indirect(off[0]), ACT.Copy), [b], [d, off], span(b, [d], None, off))

    def act(out, a, func, bias=None, scale=None, acc=None, off=None):
        src = a[0] if off is None else a[0].indirect(off[0])
        kw = {}
        if bias is not None:
            kw["bias"] = val(bias)
        if scale is not None:
            kw["scale"] = val(scale)
        if acc is not None:
            kw["accum_out"] = acc[0]
        rec("s", lambda: g.scalar.activation(out[0], src, func, **kw), [out] + ([acc] if acc else []), [a, bias, scale, off],
            span(out, [a], 1.0, off, "s"))

    def times(on, out, a, c, off=None):
        if on == "s":
            act(out, a, ACT.Copy, None, c, off=off)
        else:
            ts(out, a, c, ALU.mult, off=off)

    fills = [0]

    def zero(out):
        dma("y", "z%d" % fills[0], out, A("ZT", 0, len(out[4])))
        fills[0] += 1

    def repeat(name):
        for c0 in range(K, C, K):
            dma("y", "z%d" % fills[0], A(name, c0, c0 + K), A(name, 0, K))
            fills[0] += 1

    def mm(bank, n, ql, sl, l0, qr, sr, r0, start=True, stop=True, grp=None):
        o = A("ps%d" % bank, 0, n)
        a, b, c, d = A(ql, l0, l0 + 128), A(sl, l0, l0 + 128), A(qr, r0, r0 + n), A(sr, r0, r0 + n)
        rec("t", lambda: g.tensor.matmul_mx(o[0], a[0], b[0], c[0], d[0], start, stop), [o], [a, b, c, d], ("pe", n), grp=grp)

    def dma(q, sem, out, a, raw=False, chain=None):
        e = {"y": g.sync, "s": g.scalar}[q]
        o, i = val(out), val(a)
        if raw:
            o = o.bitcast(dt.uint8) if isinstance(out, tuple) else o
            i = i.bitcast(dt.uint8) if isinstance(a, tuple) else i
        rec(q, lambda: e.dma_start(o, i), [out] if isinstance(out, tuple) else [], [a], ("dma", 0), sem=sem, chain=chain)

    def iota(out, pat, base, cm, small=True):
        if small:
            rec("g", lambda: g.iota(out[0], pat, base, cm, allow_small_or_imprecise_dtypes=True), [out], [], ("g", len(out[4])))
        else:
            rec("g", lambda: g.iota(out[0], pat, base, cm), [out], [], ("g", len(out[4])))

    def sel(out, a, pat, op, base, cm):
        rec("g", lambda: g.affine_select(out[0], a[0], pat, op, 0.0, base, cm), [out], [a], ("g", len(out[4])))

    def col(name, j):
        return A(name, j, j + 1)

    def ends(name, n):
        return A(name, 15, n, 16)

    def ps(bank, c0, c1, p0=0, p1=128):
        return A("ps%d" % bank, c0, c1, 1, p0, p1)

    dma("y", "ldu", A("U"), T.u[:], chain="loads")
    dma("y", "ldx", A("X", 0, 4 * H), T.x[:, 0:4 * H], chain="loads")
    dma("s", "ldz", A("X", 4 * H, 4 * E), T.x[:, 4 * H:4 * E])
    dma("y", "ldw", A("qw"), T.wc[:], raw=True, chain="loads")
    dma("y", "lds", A("sw"), T.ws[:], chain="loads")
    dma("y", "ldv", A("V"), T.v[:], chain="loads")
    iota(col("PI", 0), [[0, 1]], 0, 1, False)
    iota(A("LI", 0, 8), [[16, 8]], 0, 0)
    iota(A("RI"), [[0, 21], [1, 16]], 0, 0)
    iota(col("PF", 3), [[0, 1]], 0, 1)
    fill(A("ONE"), 1.0)
    for j, c in enumerate((15, 3, 31)):
        ts(col("PB", j), col("PI", 0), c, ALU.bitwise_and)
    cp(A("ou"), A("LI", 0, 8))
    cp(A("PF", 0, 3), A("PB", 0, 3))
    q, q3, q31, p = (col("PF", j) for j in range(4))
    fill(A("RR"), -BIG)
    fill(A("RR", 0, E, 16), BIG)
    fill(A("ZT"), 0.0)
    act(A("NEG"), A("ONE", 0, 32), ACT.Copy, None, -1.0)
    zero(A("ST"))
    ts(A("AM"), A("RI"), q, ALU.not_equal, BIG, ALU.mult)
    act(col("PC", 0), q, ACT.Identity, 2.0)
    act(A("AG"), A("RI", 0, 64), ACT.Relu, col("PC", 0), -1.0)
    act(A("AT"), A("AG"), ACT.Square, -24.0, 32.0)
    act(A("AV", 0, K), A("AT", 1, K + 1), ACT.Identity, 576.0, -1.0)
    repeat("AV")
    act(A("AE", 0, 16), A("AT", 0, 16), ACT.Relu, 576.0, -1.0)
    act(A("AE", 16, 32), A("AG", 0, 16), ACT.Relu, -1.0)
    act(A("AE", 32, 48), A("AE", 16, 32), ACT.Sign)
    act(A("AP", 0, 32), A("ONE", 0, 32), ACT.Copy)
    tt(A("AP", 32, K), A("AE", 0, 16), A("AE", 32, 48), ALU.add)
    ts(col("PC", 1), q, 15.0, ALU.is_lt, -512.0, ALU.mult)
    act(col("PC", 3), col("PC", 1), ACT.Identity, 1024.0 + 159.0)
    act(col("PC", 4), q, ACT.Identity, col("PC", 3), -1.0)
    act(col("PC", 14), q3, ACT.Identity, 0.0, 63.75)
    act(col("PC", 15), q, ACT.Identity, col("PC", 14), 0.25)
    act(col("PC", 5), q3, ACT.Identity, 0.0, 7.75)
    act(col("PC", 6), q, ACT.Identity, col("PC", 5), -1.75)
    act(col("PC", 8), q31, ACT.Identity, col("PC", 6), 2.0)
    zero(A("TB", 32, 64))
    act(col("PC", 9), q3, ACT.Identity, 0.0, 62.5)
    act(col("PC", 10), q, ACT.Identity, col("PC", 9), 1.5)
    rounds = [dict(CFG, **CFG["R"][t]) for t in range(R)]
    iota(A("R4"), [[0, 12], [1, 4]], 0, 0)
    act(col("PD", 0), q3, ACT.Identity, 2.0, -0.25)
    act(col("PD", 1), q, ACT.Identity, col("PD", 0), 0.25)
    act(A("AG4"), A("R4"), ACT.Relu, col("PD", 1), -1.0)
    act(A("AT4"), A("AG4"), ACT.Square, -24.0, 32.0)
    act(A("A4", 0, K), A("AT4"), ACT.Identity, 576.0, -1.0)
    repeat("A4")
    ts(col("PD", 2), q, 12.0, ALU.is_lt, -2048.0, ALU.mult)
    act(col("PD", 3), q3, ACT.Identity, col("PD", 2))
    act(col("PD", 4), col("PD", 3), ACT.Identity, 4.0 * 168)
    if any(cf["K96"] for cf in rounds):
        act(col("PC", 11), q31, ACT.Identity, q, -1.0)
        act(col("PC", 12), col("PC", 11), ACT.Identity, float(K), -3.0)
        act(col("PC", 13), col("PC", 11), ACT.Identity, float(2 * K), 3.0)
    for m in range(3):
        if any(cf["KC"][m] == "v" for cf in rounds):
            zero(A("SGX", (C + 64) * m + C, (C + 64) * (m + 1)))
    for c0, c1 in ((240, 320), (496, 544), (656, 704), (752, 800)):
        zero(A("TT", 4 * c0, 4 * c1))
    quant("qu", "su", 0, A("U"))
    pick("qk", "sk", 128, "qu", "su", 128, A("ou"))
    quant("q0", "s0", 0, A("ZT"))
    gaps = [("t", 896, 1024), ("t", 1024, 1088), ("t", 320, 416), ("l", 0, LAND)]
    gaps += [("l", LAND + GAP * t + 6, LAND + GAP * (t + 1)) for t in range(R)]
    for j, (n_, c0, c1) in enumerate(gaps):
        dma("y", "q%d" % (2 * j), A("q" + n_, c0, c1), A("q0", 0, c1 - c0), raw=True)
        dma("y", "q%d" % (2 * j + 1), A("s" + n_, c0, c1), A("s0", 0, c1 - c0))
    zero(A("TE"))
    act(col("CA", 0), col("ZT", 0), ACT.Copy)
    zero(A("MW64"))
    zero(A("ZW", 4 * K, 512))
    zero(A("EM", 2048, 2112))
    zero(A("BT", 32, 512))
    iota(A("DA"), [[-16, 18], [512, 16]], 144, 0)
    sel(A("OD1"), A("ONE"), [[-16, 8], [0, 64]], ALU.is_ge, 0, 1)
    sel(A("OD"), A("OD1"), [[16, 8], [0, 64]], ALU.is_ge, 15, -1)
    quant("qo", "so", 0, A("OD"))
    iota(A("IV"), [[1, E]], -168, 0)
    iota(A("LI", 8, 11), [[32, 3]], 0, 0)
    iota(A("LI", 16, 28), [[4, 12]], 0, 0)
    iota(A("LI", 28, 40), [[1, 6], [24, 2]], 0, 0)
    for t in range(R):
        iota(A("W", E * t + C, E * t + E), [[0, K]], 1024, 0)
    if not all(cf["K96"] for cf in rounds):
        ts(A("ok", 0, 3), A("LI", 8, 11), q31, ALU.add)
    ts(A("ob"), A("LI", 16, 18), col("PC", 8), ALU.add)
    ts(A("ox"), A("LI", 16, 28), col("PC", 15), ALU.add)
    ts(A("ox", 0, 12, 1, 0, 16), A("LI", 28, 40, 1, 0, 16), A("PC", 10, 11, 1, 0, 16), ALU.add)
    for a in range(4):
        sel(A("EM", 512 * a, 512 * a + 512), A("ONE"), [[-128, 4], [-1, 32], [128, 4]], ALU.is_equal, -32 * a, 1)
    for a in range(4):
        quant("qe", "se", 132 * a, A("EM", 528 * a, 528 * a + 528))
    quant("qv", "sv", 0, A("V"))

    base = {}
    for m in range(1, 18):
        c0, t_ = ((0, 18 - m) if m >= 15 else (320, 14 - m) if m >= 11 else (544, 10 - m) if m >= 7
                  else (704, 6 - m) if m >= 3 else (288, 2 - m))
        base[m] = 4 * c0 + t_

    def slot(m, c0=0, c1=None):
        c1 = 16 * m if c1 is None else c1
        return A("TT", base[m] + 4 * c0, base[m] + 4 * c1 - 3, 4)

    def key(m):
        return col("SH", 16 * m + 15)

    def unpack(t):
        c0 = LAND + GAP * t
        rec("x", None, [A("ql", c0, c0 + 6), A("sl", c0, c0 + 6)], [], ("none", 0), sem="arr%d" % t, full=16, chain="far%d" % t)
        for h in range(8):
            mm(7, 128, "qe", "se", 128 * (h // 2) + 16 * (h % 2), "ql", "sl", c0 - 6 * h, h == 0, h == 7, grp="u%d" % t)
        for b in range(4):
            times(rounds[t]["UC"], A("ST", 64 * b, 64 * b + K, 1, 0, 16), ps(7, 0, K, 32 * b, 32 * b + 16), 64.0)
        n = len(rounds[t]["XG"])
        for h in range(n):
            times(rounds[t]["XG"][h], A("X", 4 * C + 192 // n * h, 4 * C + 192 // n * (h + 1)), A("ST"), 0.015625,
                  A("ox", 12 // n * h, 12 // n * (h + 1)))

    for c0, c1 in ((0, H), (H, E)):
        quant("qx", "sx", c0, A("X", 4 * c0, 4 * c1))
    for t in range(R):
        first, cf = t == 0, rounds[t]
        NV, SS = cf["NV"], cf["SS"]
        row = A("W", E * t, E * t + C)
        whole = A("W", E * t, E * t + E)
        known = E if first else C
        mm(4, H, "qk", "sk", 0, "qx", "sx", 0)
        mm(0, known, "qk", "sk", 0, "qx", "sx", 0)
        mm(1, C, "qk", "sk", 0, "qx", "sx", 0)
        for bank, (c0, c1) in zip((4, 0), ((0, H), (H, known))):
            tt(A("KX", c0, c1), ps(bank, c0, c1), A("AM", c0, c1), ALU.add)
            scan(A("SH", c0, c1), A("RR", c0, c1), A("KX", c0, c1), BIG, ALU.max, ALU.min)
        for bank, (c0, c1) in (zip((4, 0), pieces) if cf["SPLIT"] else [(0, (0, C))]):
            tt(A("TT", 4 * c0, 4 * c1, 4), ps(bank, c0, c1), A("SH", c0, c1), ALU.is_ge)
            scan(A("DS", c0, c1), A("DA", c0, c1), A("TT", 4 * c0, 4 * c1, 4), 1000.0, ALU.min, ALU.add)
        if SS:
            mm(6, H, "qk", "sk", 0, "qx", "sx", 0)
        else:
            act(col("RS", RW - 1), col("DS", 15), ACT.Copy)
        for m in range(1, 18):
            if SS < m <= NV:
                ts(slot(m), ps(4 if 16 * m < H else 0, 0, 16 * m), key(m), ALU.is_gt)
                scan(A("RS", RW * m + RW - 8 * m, RW * m + RW), slot(m, 0, 8 * m), slot(m, 8 * m, 16 * m),
                     col("DS", 16 * m + 15), ALU.add, ALU.add)
            else:
                sg = A("SG", 8 * m * (m - 1), 8 * m * (m + 1))
                act(sg, ps(6 if 16 * m < H else 1, 0, 16 * m), ACT.Sign, key(m), -1.0)
                act(slot(m), sg, ACT.Relu, None, -1.0, col("CA", m))
        for m0, m1 in ((0, SS + 1), (NV + 1, 18)):
            if cf["US"][m0 > 0] == "s":
                for m in range(m0, m1):
                    act(col("RS", RW * m + RW - 1), col("CA", m), ACT.Identity, col("DS", 16 * m + 15))
            elif m1 > max(m0, 1):
                tt(A("RS", RW * (m0 + 1) - 1, RW * m1, RW), A("DS", 16 * m0 + 15, 16 * m1, 16), A("CA", m0, m1), ALU.add)
        if cf["US"][2] == "s":
            act(ends("AV", C), A("RS", RW - 1, 18 * RW, RW), ACT.Identity, -1024.0, -1.0)
        else:
            ts(ends("AV", C), A("RS", RW - 1, 18 * RW, RW), -1.0, ALU.mult, -1024.0, ALU.add)
        quant("qt", "st", 640, A("TT", 4 * 544, 4 * 800))
        quant("qt", "st", 0, A("TT", 0, 4 * 320))
        quant("qt", "st", 416, A("TT", 4 * 320, 4 * 544))
        for i, (c0, n) in enumerate(((800, C), (640, 160), (0, C), (288, 128), (416, 224))):
            mm(6, n, "qo", "so", 0, "qt", "st", c0, i == 0, i == 4, grp="c%d" % t)
        cuts = list(zip((0,) + cf["SC"], cf["SC"] + (18,)))
        for c0, c1 in (cuts if cf["CVP"] else [(0, 18)]):
            scan(A("CV", 16 * c0, 16 * c1), ps(6, 16 * c0, 16 * c1), A("AV", 16 * c0, 16 * c1), -1024.0, ALU.max, ALU.add)
            ts(A("ork", c0, c1), A("CV", 16 * c0 + 15, 16 * c1, 16), col("PC", 4), ALU.add)
        for c0, c1 in cuts:
            scatter(row, A("ork", c0, c1), A("IV", 16 * c0, 16 * c1))
        bank, w0 = (0, C) if first else (5, 80)
        if not first:
            unpack(t - 1)
            quant("qa", "sa", 0, A("X", 4 * (E - 128), 4 * E))
            mm(5, 128, "qk", "sk", 0, "qa", "sa", 0)
            tt(A("KX", C, E), ps(5, 80, 128), A("AM", 0, K), ALU.add)
            scan(A("SH", C, E), A("RR", 0, K), A("KX", C, E), BIG, ALU.max, ALU.min)
        tt(A("TE", 0, 3 * K, 3), ps(bank, w0, w0 + K), A("SH", C, E), ALU.is_equal)
        for m in range(3):
            e_ = 16 * m + 16
            kw_ = key(18 + m)
            ts(A("TW", K * m, K * m + e_), ps(bank, w0, w0 + e_), kw_, ALU.is_gt)
            if e_ < K:
                ts(A("TW", K * m + e_, K * m + K), ps(bank, w0 + e_, w0 + K), kw_, ALU.is_ge)
            scan(A("RW", K * m, K * m + K), A("TW", K * m, K * m + K), A("TE", K * m, K * m + K), 0.0, ALU.add, ALU.add)
        apart = "v" in cf["KC"][1:]
        for m in range(3):
            kw_, x0, b0 = key(18 + m), (C + 64) * m, (176 if apart else 32) * m
            if cf["KC"][m] == "v":
                ts(A("SGX", x0, x0 + C), ps(0, 0, C), kw_, ALU.is_le)
                scan(A("BC", b0, b0 + 176), A("SGX", x0, x0 + C + 64, 2), A("SGX", x0 + 1, x0 + C + 64, 2),
                     -144.0, ALU.add, ALU.add)
            else:
                act(A("SGW", C * m, C * m + C), ps(1, 0, C), ACT.Sign, kw_, -1.0)
                act(A("SGX", x0, x0 + C), A("SGW", C * m, C * m + C), ACT.Relu, None, -1.0, col("CN", m))
                act(A("BC", b0 + 144, b0 + 176), A("NEG"), ACT.Identity, 144.0, col("CN", m))
            if apart:
                turn(A("BD", 32 * m, 32 * m + 32), A("BC", b0 + 144, b0 + 176))
        if not apart:
            turn(A("BD"), A("BC", 144, 240))
        ts(A("orb", 0, 3), A("RW", K - 1, 3 * K, K), -1.0, ALU.mult, float(K), ALU.add)
        scatter(A("B0"), A("orb", 0, 3), A("IV", C, E))
        if cf["K96"]:
            for h in range(2):
                ts(A("o96", h, 6, 2), A("RW", K - 1, 3 * K, K), -1.0, ALU.mult, col("PC", 12 + h), ALU.add)
            scatter(A("KS"), A("o96"), A("BD"))
        else:
            act(A("KU"), A("BD"), ACT.Copy, off=A("ok", 0, 3))
            scatter(A("KS", 0, K), A("orb", 0, 3), A("KU"))
        for m in range(3):
            n = 16 * m + 16
            scan(A("CP", K * m + K - n, K * m + K), A("AP", K - n, K), A("KS", 0, n), -145.0, ALU.add, ALU.max)
        ts(A("op", 0, 3), A("CP", K - 1, 3 * K, K), col("PC", 1), ALU.add, 144.0, ALU.add)
        tt(A("WB"), whole, A("B0"), ALU.min, off=A("op", 0, 3))
        scatter(whole, A("op", 0, 3), A("B0"))
        for c0, c1 in (pieces if cf["EP"] else [(0, C)]):
            scan(A("CE", c0, c1), A("A4", c0, c1), A("W", E * t + c0, E * t + c1), 0.0, ALU.add, ALU.max)
            ts(A("oe", c0 // 4, c1 // 4), A("CE", c0 + 3, c1, 4), 4.0, ALU.mult, col("PD", 4), ALU.add)
        scan(A("CB"), A("A4", 0, K), A("WB"), 0.0, ALU.add, ALU.max)
        ts(A("ow"), A("CB", 3, K, 4), 4.0, ALU.mult, col("PD", 4), ALU.add)
        n = len(cf["W4"])
        for h in range(n):
            times(cf["W4"][h], A("ZW", 192 // n * h, 192 // n * (h + 1)), A("X"), 1.0, A("ow", 12 // n * h, 12 // n * (h + 1)))
        quant("qzw", "szw", 0, A("ZW"))
        times(cf["ZE"], A("ZW64"), A("ZW", 0, 4 * K), 64.0)
        for b in range(4):
            mm(b, 128, "qw", "sw", 128 * b, "qzw", "szw", 0)
            tt(A("MW64", 64 * b, 64 * b + K), ps(b, 0, K), A("ZW64", b, 4 * K, 4), ALU.add)
        dma("y", "sh%d" % t, A("ST", 0, 256, 1, 16, 128), A("MW64", 0, 256, 1, 0, 112))
        for a in range(4):
            turn(A("TB", 0, 32, 1, 32 * a, 32 * a + 32), A("MW64", 2 * a, 256, 8, 96, 128))
            times(cf["QC"][a], A("BU", 32, 64, 1, 32 * a, 32 * a + 32), A("MW64", 2 * a + 1, 256, 8, 96, 128), 1.0)
        turn(A("BU", 0, 32), A("TB", 16, 48))
        times(cf["GE"], A("BT", 0, 32), A("BU"), 0.015625, A("ob"))
        quant("qb", "sb", 128 * t, A("BT"))
        dst = T.cores[(rank + t + 1) % N]
        rid, pid = topo.addr(dst, core)
        mask = topo.mask(core, dst)
        assert len(topo.engines(core, dst)) == 8

        def ship(t=t, rid=rid, pid=pid, mask=mask):
            c0, b0 = LAND + GAP * t, 128 * t
            g.remote_dma(T.ql[:, c0:c0 + 6].bitcast(dt.uint8), T.qb[:, b0:b0 + 6].bitcast(dt.uint8),
                         T.sem["arr%d" % t], T.sem.sent, pid, rid, mask)
            return g.remote_dma(T.sl[:, c0:c0 + 6], T.sb[:, b0:b0 + 6], T.sem["arr%d" % t], T.sem.sent, pid, rid, mask)

        rec("g", ship, [], [A("qb", 128 * t, 128 * t + 6), A("sb", 128 * t, 128 * t + 6)], ("far", 0), chain="far%d" % t)
        c0 = 0
        for on, n in cf["ZG"]:
            times(on, A("Z", 4 * c0, 4 * (c0 + n)), A("X"), 1.0, A("oe", c0 // 4, (c0 + n) // 4))
            c0 += n
        for h, (c0, c1) in enumerate(pieces):
            n = c1 - c0
            zh = A("Z", 4 * c0, 4 * c1)
            quant("qz", "sz", c0, zh)
            if cf["Z6"][h] == "s":
                for b in range(4):
                    times(cf["Z6"][h], A("Z64", 4 * c0 + b, 4 * c1, 4), A("Z", 4 * c0 + b, 4 * c1, 4), 64.0)
            else:
                times(cf["Z6"][h], A("Z64", 4 * c0, 4 * c1), zh, 64.0)
            for b in range(4):
                mm(4 * (1 - h) + b, n, "qw", "sw", 128 * b, "qz", "sz", c0)
            for b in range(4):
                p_ = A("M64", C * b + c0, C * b + c1)
                tt(p_, ps(4 * (1 - h) + b, 0, n), A("Z64", 4 * c0 + b, 4 * c1, 4), ALU.add)
                times(cf["DN"][4 * h + b], A("X", 4 * c0 + b, 4 * c1, 4), p_, 0.015625)
            quant("qx", "sx", c0, A("X", 4 * c0, 4 * c1))

    act(A("LE", 0, C), A("W", E * (R - 1), E * (R - 1) + C), ACT.Identity, 168.0)
    act(A("LE", C, E), A("WB"), ACT.Identity, 168.0)
    dma("y", "oa", T.le[:], (T.LE[0:128:16, :],) + A("LE")[1:])
    for bank, (c0, c1) in zip((4, 0), pieces):
        mm(bank, c1 - c0, "qv", "sv", 0, "qx", "sx", c0)
        dma("y", "oa", T.oc[:, 4 * c0:4 * c1], A("qx", c0, c1), raw=True)
        act(A("Y", c0, c1), ps(bank, 0, c1 - c0), ACT.Copy)
        dma("y", "oa", T.y[:, c0:c1], A("Y", c0, c1))
    for k in range(4):
        dma("y", "oa", T.osc[4 * k:4 * k + 4, 0:C], A("sx", 0, C, 1, 32 * k, 32 * k + 4))
    unpack(R - 1)
    quant("qa", "sa", 0, A("X", 4 * (E - 128), 4 * E))
    mm(5, 128, "qv", "sv", 0, "qa", "sa", 0)
    dma("y", "oa", T.oc[:, 4 * C:4 * E], A("qa", 80, 128), raw=True)
    for k in range(4):
        dma("y" if k < 1 else "s", "oa" if k < 1 else "oz", T.osc[4 * k:4 * k + 4, C:E], A("sa", 80, 128, 1, 32 * k, 32 * k + 4))
    cp(A("Y", C, E), ps(5, 80, 128))
    dma("y", "oa", T.y[:, C:E], A("Y", C, E))
    return ops
